import numpy as np
import ml_dtypes


def mxq(x, axis, fmt="e4m3"):
    dtype, down = {"e4m3": (ml_dtypes.float8_e4m3fn, 7), "e5m2": (ml_dtypes.float8_e5m2, 14)}[fmt]
    v = np.moveaxis(np.asarray(x, np.float32).astype(ml_dtypes.bfloat16).astype(np.float64), axis, -1)
    blocks = v.reshape(v.shape[:-1] + (-1, 32))
    amax = np.abs(blocks).max(-1, keepdims=True)
    byte = np.maximum(np.where(amax > 0, np.frexp(amax)[1] - 1 + 127, 0) - down, 1)
    scale = np.exp2(byte - 127.0)
    codes = (blocks / scale).astype(np.float32).astype(dtype).astype(np.float64)
    return np.moveaxis((codes * scale).reshape(v.shape), -1, axis)


WIDE = False


def mx_kscale(k):
    if not WIDE:
        return np.ones(k)
    levels = np.array([10, -10, 5, -5, 0])
    if k % 512:
        return np.exp2(np.random.permutation(np.resize(levels, k // 32))).repeat(32)
    a = np.empty((k // 512, 16))
    for p in range(k // 512):
        a[p, :8] = np.random.permutation(np.resize(levels, 8))
        for g in range(8):
            far = levels[np.abs(levels - a[p, g]) >= 10]
            a[p, g + 8] = far[np.random.randint(len(far))]
    return np.exp2(a.ravel()).repeat(32)


def f64(x):
    return np.asarray(x).astype(np.float64)


def striped(idx):
    return np.tile(idx.reshape(-1, 16).T, (8, 1)).astype(np.uint16)


def unstriped(offs):
    return offs[:16].T.reshape(-1).astype(np.int64)


E2M1 = np.array([0.0, 0.5, 1.0, 1.5, 2.0, 3.0, 4.0, 6.0, -0.0, -0.5, -1.0, -1.5, -2.0, -3.0, -4.0, -6.0])


def pack_weight(w, fmt):
    k, n = w.shape
    w = f64(np.asarray(w, np.float32).astype(ml_dtypes.bfloat16)).reshape(k // 32, 32, n)
    amax = np.abs(w).max(1)
    if fmt == "e4m3":
        byte = np.frexp(amax)[1] - 1 + 127 - 7
    else:
        mant, ex = np.frexp(amax / 6.0)
        byte = np.where(mant > 0.5, ex, ex - 1) + 127
    byte = np.clip(np.where(amax > 0, byte, 1), 1, 254)
    scaled = (w * np.exp2(127.0 - byte)[:, None, :]).reshape(k, n).astype(np.float32)
    by_word = np.ascontiguousarray(scaled.reshape(k // 512, 128, 4, n).transpose(0, 1, 3, 2))
    if fmt == "e4m3":
        words = by_word.astype(ml_dtypes.float8_e4m3fn).view(np.uint8)
    else:
        c = by_word.astype(ml_dtypes.float4_e2m1fn).view(np.uint8) & 0xF
        words = (c[..., 0::2] | (c[..., 1::2] << 4)).reshape(k // 512, 128, 2 * n)
    return np.ascontiguousarray(words), np.ascontiguousarray(byte.astype(np.uint8).reshape(k // 512, 16, n))


def unpack_weight(words, scales, fmt):
    g, _, n = scales.shape
    words = np.ascontiguousarray(words).reshape(g, 128, n, -1)
    if fmt == "e4m3":
        vals = words.view(ml_dtypes.float8_e4m3fn).astype(np.float64)
    else:
        nib = np.empty((g, 128, n, 4), np.uint8)
        nib[..., 0::2] = words & 0xF
        nib[..., 1::2] = words >> 4
        vals = E2M1[nib]
    vals = vals * np.repeat(np.exp2(scales.astype(np.float64) - 127.0), 8, axis=1)[..., None]
    return vals.transpose(0, 1, 3, 2).reshape(g * 512, n)


def gelu(v):
    return 0.5 * v * (1.0 + np.tanh(np.sqrt(2.0 / np.pi) * (v + 0.044715 * v**3)))


def bf(x):
    return np.asarray(x, np.float32).astype(ml_dtypes.bfloat16)


def planes(Y):
    n, m = Y.shape
    b = f64(bf(Y)).reshape(n // 32, 32, m)
    amax = np.abs(b).max(1)
    byte = np.clip(np.where(amax > 0, np.frexp(amax)[1] - 1 + 127 - 7, 1), 1, 254)
    codes = (b * np.exp2(127.0 - byte)[:, None, :]).reshape(n, m).astype(np.float32).astype(ml_dtypes.float8_e4m3fn).view(np.uint8)
    words = codes.reshape(n // 512, 128, 4, m).transpose(0, 1, 3, 2)
    return np.ascontiguousarray(words), np.ascontiguousarray(byte.astype(np.uint8).reshape(n // 512, 16, m))


KH, K, T, S, T2, P, H, N = 1024, 2048, 2048, 1024, 2048, 1024, 1024, 512

def setup_inputs():
    n = np.random.standard_normal
    s = np.tile(mx_kscale(KH), K // KH)[:, None]
    u = mx_kscale(H)[:, None]
    x = n((KH, T))
    tab_words, tab_scales = pack_weight(np.concatenate([np.abs(x), x], axis=0) * s, "e4m3")
    wo = n((H, N)) * np.exp(0.8 * n((1, N))) / np.sqrt(H) / u
    wo_words, wo_scales = pack_weight(wo, "e2m1")
    return {
        "tab_words": tab_words, "tab_scales": tab_scales,
        "offs": striped(np.random.permutation(T)[:S]),
        "offs2": striped(np.random.permutation(T2)[:S]),
        "offs3": striped(np.random.permutation(T2)[:P]),
        "w1": (n((KH, H)) * u.T / np.sqrt(KH) / s[:KH]).astype(np.float32),
        "wgs": np.exp(0.3 * n((128, S))).astype(np.float32),
        "thr": (n((H, P)) * u).astype(np.float32),
        "wo_words": wo_words, "wo_scales": wo_scales,
    }

def reference(tab_words, tab_scales, offs, offs2, offs3, w1, wgs, thr, wo_words, wo_scales):
    v = unpack_weight(tab_words, tab_scales, "e4m3")[:, unstriped(offs)]
    wq = mxq(f64(w1), 0, "e4m3")
    mag = wq.T @ v[:KH]
    raw = wq.T @ v[KH:]
    h = mag - np.abs(raw)
    page = np.zeros((H, T2))
    page[:, unstriped(offs2)] = np.tile(f64(wgs), (H // 128, 1)) * h
    x = page[:, unstriped(offs3)]
    z = np.maximum(x, f64(thr))
    zq = mxq(z, 0, "e4m3")
    wo = unpack_weight(wo_words, wo_scales, "e2m1")
    y = wo.T @ zq
    words, scales = planes(y)
    return y, words, scales

@@ -1,0 +1,313 @@
+from contextlib import ExitStack
+
+import concourse.mybir as mybir
+from concourse.masks import make_identity
+
+KH, T, S, T2, M, H, N = 1024, 2048, 1024, 2048, 1024, 1024, 512
+FLOPS = 2 * (2 * KH * H * S + H * N * M)
+
+F32 = mybir.dt.float32
+BF16 = mybir.dt.bfloat16
+I32 = mybir.dt.int32
+U32 = mybir.dt.uint32
+U16 = mybir.dt.uint16
+U8 = mybir.dt.uint8
+FP8X4 = mybir.dt.float8_e4m3fn_x4
+FP4X4 = mybir.dt.float4_e2m1fn_x4
+COPY = mybir.ActivationFunctionType.Copy
+ABS = mybir.ActivationFunctionType.Abs
+MULT = mybir.AluOpType.mult
+MAX = mybir.AluOpType.max
+
+P = 128
+PACK = 4
+K_PASS = P * PACK
+CHUNK = 256
+
+
+def tile_list_leakage_gap_audit_kernel(
+    tc, tab_words, tab_scales, offs, offs2, offs3, w1, wgs, thr, wo_words, wo_scales, out_0, out_1, out_2
+):
+    nc = tc.nc
+    with ExitStack() as ctx:
+        sb = ctx.enter_context(tc.tile_pool(name="sb", bufs=1))
+        ps = ctx.enter_context(tc.psum_pool(name="ps", bufs=1))
+
+        def tile(shape, dtype, name, tag=None):
+            return sb.tile(shape, dtype, name=name, tag=tag or name, align_bytes=64)
+
+        def bank(index, shape, name):
+            return ps.tile(shape, F32, name=name, tag="bank%d" % index)
+
+        def entries(lst, j0, j1):
+            return lst[:, j0 // 16 : j1 // 16]
+
+        list1 = tile([P, S // 16], U16, "list1")
+        list2 = tile([P, S // 16], U16, "list2")
+        list3 = tile([P, M // 16], U16, "list3")
+        ident = tile([P, P], F32, "ident")
+        tab_sc = tile([P, T], U8, "tab_sc")
+        wo_sc_raw = tile([P, 2, N], U8, "wo_sc_raw")
+        pages = [tile([P, T2], F32, "page%d" % t) for t in range(PACK)]
+        nc.vector.memset(tab_sc[:].bitcast(I32), 0)
+        nc.vector.memset(wo_sc_raw[:].bitcast(I32), 0)
+        make_identity(nc, ident[:])
+        for t in range(PACK):
+            nc.vector.memset(pages[t][:], 0.0)
+
+        tab = [tile([P, T], I32, "tab%d" % a) for a in range(4)]
+
+        def load_tab(a):
+            nc.sync.dma_start(tab[a][:], tab_words[a].rearrange("p t i -> p (t i)").bitcast(I32))
+
+        w_raw = {}
+
+        def load_w1(a, b):
+            w_raw[a, b] = tile([P, PACK, K_PASS], F32, "w_raw%d%d" % (a, b), "w_raw%d" % b)
+            rows = w1[b * K_PASS : (b + 1) * K_PASS, a * K_PASS : (a + 1) * K_PASS]
+            nc.sync.dma_start(w_raw[a, b][:], rows.rearrange("(p i) c -> p i c", i=PACK))
+
+        wg = tile([P, PACK, S], F32, "wg")
+        wgs_rows = wgs.rearrange("(q t) j -> q t j", t=PACK)
+
+        def load_wg(t0, t1, j0, j1):
+            for quad in range(4):
+                nc.sync.dma_start(wg[32 * quad : 32 * quad + 32, t0:t1, j0:j1], wgs_rows[:, t0:t1, j0:j1])
+
+        nc.sync.dma_start(list1[:], offs)
+        load_tab(0)
+        for quad in range(4):
+            nc.scalar.dma_start(
+                tab_sc[32 * quad : 32 * quad + 16, :].bitcast(I32),
+                tab_scales[:, 4 * quad : 4 * quad + 4, :].bitcast(I32),
+            )
+        load_w1(0, 0)
+        load_w1(0, 1)
+        load_tab(1)
+        load_tab(2)
+        load_tab(3)
+        wo_raw = tile([P, 2, 2 * N], U8, "wo_raw")
+        nc.sync.dma_start(wo_raw[:].bitcast(I32), wo_words.rearrange("a p c -> p a c").bitcast(I32))
+        for quad in range(4):
+            nc.scalar.dma_start(
+                wo_sc_raw[32 * quad : 32 * quad + 4, :, :].bitcast(I32),
+                wo_scales[:, 4 * quad : 4 * quad + 4, :].rearrange("a q c -> q a c").bitcast(I32),
+            )
+        nc.sync.dma_start(list2[:], offs2)
+        load_wg(0, 2, 0, S // 2)
+        load_wg(2, 4, 0, S // 2)
+
+        w_codes = {}
+        w_scales = {}
+
+        def quantise_w1(a, b, on_vector):
+            grouped = tile([P, K_PASS, PACK], BF16, "w_bf%d%d" % (a, b), "w_bf%d" % b)
+            dst = grouped[:].rearrange("p (c u) i -> p c i u", u=4)
+            src = w_raw[a, b][:].rearrange("p i (c u) -> p c i u", u=4)
+            if on_vector:
+                nc.vector.tensor_copy(dst, src)
+            else:
+                nc.scalar.copy(dst, src)
+            w_codes[a, b] = tile([P, K_PASS], U32, "w_codes%d%d" % (a, b))
+            w_scales[a, b] = tile([P, K_PASS], U8, "w_scales%d%d" % (a, b))
+            nc.vector.quantize_mx(
+                out=w_codes[a, b][:].bitcast(FP8X4),
+                scales=w_scales[a, b][:],
+                in_=grouped[:].rearrange("p c i -> p (c i)"),
+            )
+
+        picked_sc = tile([P, S], U8, "picked_sc")
+        picked = [tile([P, S], U32, "picked%d" % a) for a in range(4)]
+
+        def gather_tab(a, cuts):
+            for j0, j1 in zip(cuts[:-1], cuts[1:]):
+                nc.vector.tensor_copy(picked[a][:, j0:j1], tab[a][:].bitcast(U32).indirect(entries(list1, j0, j1)))
+
+        gather_tab(0, [0, S])
+        nc.vector.tensor_copy(picked_sc[:], tab_sc[:].indirect(list1[:]))
+        quantise_w1(0, 0, False)
+        quantise_w1(0, 1, True)
+        gather_tab(1, [0, S // 2, S])
+        gather_tab(2, [0, S])
+        gather_tab(3, [0, S // 4, S // 2, S])
+
+        wo_codes = tile([P, 2, 2 * N], U8, "wo_codes")
+        wo_sc = tile([P, 2, N], U8, "wo_sc")
+        for a in range(2):
+            nc.vector.tensor_copy(
+                wo_codes[:, a, :].rearrange("p (t c b) -> p c t b", t=PACK, b=2),
+                wo_raw[:, a, :].rearrange("p (c t b) -> p c t b", t=PACK, b=2),
+            )
+        nc.vector.tensor_copy(
+            wo_sc[:].rearrange("p a (t c) -> p a c t", t=PACK),
+            wo_sc_raw[:].rearrange("p a (c t) -> p a c t", t=PACK),
+        )
+
+        def product(a, jt, half, index):
+            acc = bank(index, [P, K_PASS], "acc%d_%d_%d" % (a, jt, half))
+            cols = slice(jt * P, (jt + 1) * P)
+            for b in range(2):
+                k = 2 * half + b
+                nc.tensor.matmul_mx(
+                    out=acc[:],
+                    lhsT=picked[k][:, cols].bitcast(FP8X4),
+                    lhsT_scale=picked_sc[4 * k :, cols],
+                    rhs=w_codes[a, b][:].bitcast(FP8X4),
+                    rhs_scale=w_scales[a, b][:],
+                    start=(b == 0),
+                    stop=(b == 1),
+                )
+            return acc[:].rearrange("p (m t) -> p t m", t=PACK)
+
+        def negated_mag(a, jt, dst):
+            nc.scalar.activation(dst, product(a, jt, 0, jt % 3), COPY, scale=-1.0)
+
+        def gap(a, jt, neg_mag, h):
+            abs_raw = tile([P, PACK, P], F32, "abs_raw%d_%d" % (a, jt), "abs_raw%d" % (jt % 3))
+            nc.scalar.activation(abs_raw[:], product(a, jt, 1, 3 + jt % 3), ABS)
+            turned = bank(6 + jt % 2, [P, PACK, P], "turned%d_%d" % (a, jt))
+            for t in range(PACK):
+                nc.tensor.matmul(turned[:, t, :], neg_mag[:, t, :], ident[:], start=True, stop=False, is_transpose=True)
+                nc.tensor.matmul(turned[:, t, :], abs_raw[:, t, :], ident[:], start=False, stop=True, is_transpose=True)
+            nc.scalar.activation(h[:, :, jt * P : (jt + 1) * P], turned[:], COPY, scale=-1.0)
+
+        def scatter(h, t, j0, j1):
+            nc.vector.tensor_tensor(pages[t][:].indirect(entries(list2, j0, j1)), h[:, t, j0:j1], wg[:, t, j0:j1], MULT)
+
+        h0 = tile([P, PACK, S], F32, "h0")
+        h1 = tile([P, PACK, S], F32, "h1")
+        neg0 = [tile([P, 2, PACK, P], F32, "neg0_%d" % i) for i in range(4)]
+        for jt in range(8):
+            negated_mag(0, jt, neg0[jt // 2][:, jt % 2, :, :])
+        for jt in range(8):
+            gap(0, jt, neg0[jt // 2][:, jt % 2, :, :], h0)
+
+        load_w1(1, 0)
+        load_w1(1, 1)
+        load_wg(0, 4, S // 2, S)
+        nc.sync.dma_start(list3[:], offs3)
+        thr_rows = thr.rearrange("(a p t) m -> a p t m", p=P, t=PACK)
+        thr1 = [tile([P, PACK, M // 2], F32, "thr1_%d" % i, "tab%d" % i) for i in range(2)]
+        for i in range(2):
+            nc.sync.dma_start(thr1[i][:], thr_rows[1][:, :, i * M // 2 : (i + 1) * M // 2])
+
+        for j0 in (0, S // 4):
+            for t in (0, 1):
+                scatter(h0, t, j0, j0 + S // 4)
+        quantise_w1(1, 0, False)
+        quantise_w1(1, 1, False)
+        for t in (2, 3):
+            scatter(h0, t, 0, S // 2)
+        for t in range(PACK):
+            scatter(h0, t, S // 2, S)
+
+        thr0 = [tile([P, 2, M], F32, "thr0_%d" % i, "w_raw%d" % i) for i in range(2)]
+        for i in range(2):
+            nc.sync.dma_start(thr0[i][:], thr_rows[0][:, 2 * i : 2 * i + 2, :])
+
+        for jt in range(8):
+            neg1 = tile([P, PACK, P], F32, "neg1_%d" % jt, "neg1_%d" % (jt % 3))
+            negated_mag(1, jt, neg1[:])
+            gap(1, jt, neg1, h1)
+
+        z_codes = [tile([P, M], U32, "z_codes%d" % a) for a in range(2)]
+        z_scales = [tile([P, M], U8, "z_scales%d" % a) for a in range(2)]
+        z0 = tile([P, PACK, M], BF16, "z0")
+        x0 = [tile([P, M], F32, "x0_%d" % t, "neg0_%d" % t) for t in range(PACK)]
+        for t in range(PACK):
+            nc.vector.tensor_copy(x0[t][:], pages[t][:].indirect(list3[:]))
+        for t in range(PACK):
+            nc.vector.tensor_tensor(z0[:, t, :], x0[t][:], thr0[t // 2][:, t % 2, :], MAX)
+
+        def interleave(dst, src):
+            nc.scalar.copy(dst.rearrange("p (c u) t -> p c t u", u=4), src.rearrange("p t (c u) -> p c t u", u=4))
+
+        def quantise_z(a, grouped, m0, m1):
+            nc.vector.quantize_mx(
+                out=z_codes[a][:, m0:m1].bitcast(FP8X4),
+                scales=z_scales[a][:, m0:m1],
+                in_=grouped.rearrange("p m t -> p (m t)"),
+            )
+
+        z0_grouped = [tile([P, M // 2, PACK], BF16, "z0_grouped%d" % i, "picked%d" % i) for i in range(2)]
+        for i in range(2):
+            interleave(z0_grouped[i][:], z0[:, :, i * M // 2 : (i + 1) * M // 2])
+
+        for j0 in (0, S // 2):
+            for t in range(PACK):
+                scatter(h1, t, j0, j0 + S // 2)
+
+        for i in range(2):
+            quantise_z(0, z0_grouped[i][:], i * M // 2, (i + 1) * M // 2)
+
+        y_banks = [bank(i, [P, PACK, P], "y%d" % i) for i in range(M // P)]
+
+        def output_pass(a, i):
+            cols = slice(i * P, (i + 1) * P)
+            for t in range(PACK):
+                nc.tensor.matmul_mx(
+                    out=y_banks[i][:, t, :],
+                    lhsT=wo_codes[:, a, 2 * P * t : 2 * P * (t + 1)].bitcast(FP4X4),
+                    lhsT_scale=wo_sc[:, a, P * t : P * (t + 1)],
+                    rhs=z_codes[a][:, cols].bitcast(FP8X4),
+                    rhs_scale=z_scales[a][:, cols],
+                    start=(a == 0 and t == 0),
+                    stop=(a == 1 and t == PACK - 1),
+                )
+
+        for i in range(M // P):
+            output_pass(0, i)
+
+        y = tile([P, PACK, M], F32, "y", "h0")
+        y_codes = tile([P, M], U32, "y_codes")
+        y_scales = tile([P, M], U8, "y_scales")
+        out_rows = out_0.rearrange("(p t) m -> p t m", t=PACK)
+        out_words = out_1[0].rearrange("p m t -> p (m t)").bitcast(I32)
+
+        def quantise_y(grouped, m0, m1):
+            nc.vector.quantize_mx(
+                out=y_codes[:, m0:m1].bitcast(FP8X4),
+                scales=y_scales[:, m0:m1],
+                in_=grouped.rearrange("p m t -> p (m t)"),
+            )
+
+        chunks = M // CHUNK
+        for c in range(chunks):
+            m0 = c * CHUNK
+            last = c == chunks - 1
+            x1 = tile([P, PACK, CHUNK], F32, "x1_%d" % c, "tab%d" % (2 + c % 2))
+            z1 = tile([P, PACK, CHUNK], BF16, "z1_%d" % c, "w_bf%d" % (c % 2))
+            z1_grouped = tile([P, CHUNK, PACK], BF16, "z1_grouped%d" % c, "picked%d" % (2 + c % 2))
+            y_grouped = tile([P, CHUNK, PACK], BF16, "y_grouped%d" % c, "y_grouped%d" % (c % 2))
+            for t in range(PACK):
+                nc.vector.tensor_copy(x1[:, t, :], pages[t][:].indirect(entries(list3, m0, m0 + CHUNK)))
+            step = P if last else CHUNK
+            for s0 in range(0, CHUNK, step):
+                part = slice(s0, s0 + step)
+                t0 = (m0 + s0) % (M // 2)
+                nc.vector.tensor_tensor(z1[:, :, part], x1[:, :, part], thr1[m0 // (M // 2)][:, :, t0 : t0 + step], MAX)
+                interleave(z1_grouped[:, part, :], z1[:, :, part])
+            for s0 in range(0, CHUNK, step):
+                quantise_z(1, z1_grouped[:, s0 : s0 + step, :], m0 + s0, m0 + s0 + step)
+            for s0 in range(0, CHUNK, P):
+                i = (m0 + s0) // P
+                output_pass(1, i)
+                rounded = y_grouped[:, s0 : s0 + P, :]
+                sums = y_banks[i][:].rearrange("p t m -> p m t")
+                if last:
+                    nc.vector.tensor_copy(rounded, sums)
+                    nc.scalar.copy(y[:, :, i * P : (i + 1) * P], y_banks[i][:])
+                    quantise_y(rounded, i * P, (i + 1) * P)
+                else:
+                    nc.scalar.copy(y[:, :, i * P : (i + 1) * P], y_banks[i][:])
+                    nc.scalar.copy(rounded, sums)
+            if not last:
+                quantise_y(y_grouped[:], m0, m0 + CHUNK)
+            nc.sync.dma_start(out_rows[:, :, m0 : m0 + CHUNK], y[:, :, m0 : m0 + CHUNK])
+            nc.sync.dma_start(out_words[:, m0 : m0 + CHUNK], y_codes[:, m0 : m0 + CHUNK].bitcast(I32))
+        for quad in range(4):
+            queue = nc.sync if quad % 2 == 0 else nc.scalar
+            queue.dma_start(
+                out_2[0][4 * quad : 4 * quad + 4, :].bitcast(I32),
+                y_scales[32 * quad : 32 * quad + 4, :].bitcast(I32),
+            )

@@ -36,8 +36,14 @@ def tile_list_leakage_gap_audit_kernel(
         def tile(shape, dtype, name, tag=None):
             return sb.tile(shape, dtype, name=name, tag=tag or name, align_bytes=64)
 
+        opened = []
+
         def bank(index, shape, name):
             return ps.tile(shape, F32, name=name, tag="bank%d" % index)
+
+        def ring_bank(shape, name):
+            opened.append(name)
+            return bank(len(opened) % 6, shape, name)
 
         def entries(lst, j0, j1):
             return lst[:, j0 // 16 : j1 // 16]
@@ -49,23 +55,27 @@ def tile_list_leakage_gap_audit_kernel(
         tab_sc = tile([P, T], U8, "tab_sc")
         wo_sc_raw = tile([P, 2, N], U8, "wo_sc_raw")
         pages = [tile([P, T2], F32, "page%d" % t) for t in range(PACK)]
-        nc.vector.memset(tab_sc[:].bitcast(I32), 0)
-        nc.vector.memset(wo_sc_raw[:].bitcast(I32), 0)
+        nc.gpsimd.memset(tab_sc[:].bitcast(I32), 0)
+        nc.gpsimd.memset(wo_sc_raw[:].bitcast(I32), 0)
         make_identity(nc, ident[:])
         for t in range(PACK):
-            nc.vector.memset(pages[t][:], 0.0)
+            nc.vector.memset(pages[t][:].bitcast(I32), 0)
 
         tab = [tile([P, T], I32, "tab%d" % a) for a in range(4)]
 
-        def load_tab(a):
-            nc.sync.dma_start(tab[a][:], tab_words[a].rearrange("p t i -> p (t i)").bitcast(I32))
+        def load_tab(a, pieces=1):
+            words = tab_words[a].rearrange("p t i -> p (t i)").bitcast(I32)
+            for c0 in range(0, T, T // pieces):
+                nc.sync.dma_start(tab[a][:, c0 : c0 + T // pieces], words[:, c0 : c0 + T // pieces])
 
         w_raw = {}
 
-        def load_w1(a, b):
+        def load_w1(a, b, pieces=1):
             w_raw[a, b] = tile([P, PACK, K_PASS], F32, "w_raw%d%d" % (a, b), "w_raw%d" % b)
             rows = w1[b * K_PASS : (b + 1) * K_PASS, a * K_PASS : (a + 1) * K_PASS]
-            nc.sync.dma_start(w_raw[a, b][:], rows.rearrange("(p i) c -> p i c", i=PACK))
+            rows = rows.rearrange("(p i) c -> p i c", i=PACK)
+            for i0 in range(0, PACK, PACK // pieces):
+                nc.sync.dma_start(w_raw[a, b][:, i0 : i0 + PACK // pieces, :], rows[:, i0 : i0 + PACK // pieces, :])
 
         wg = tile([P, PACK, S], F32, "wg")
         wgs_rows = wgs.rearrange("(q t) j -> q t j", t=PACK)
@@ -75,41 +85,43 @@ def tile_list_leakage_gap_audit_kernel(
                 nc.sync.dma_start(wg[32 * quad : 32 * quad + 32, t0:t1, j0:j1], wgs_rows[:, t0:t1, j0:j1])
 
         nc.sync.dma_start(list1[:], offs)
-        load_tab(0)
+        nc.sync.dma_start(list2[:], offs2)
+        nc.sync.dma_start(list3[:], offs3)
+        load_tab(0, 2)
+        load_w1(0, 0, 2)
         for quad in range(4):
-            nc.scalar.dma_start(
+            nc.sync.dma_start(
                 tab_sc[32 * quad : 32 * quad + 16, :].bitcast(I32),
                 tab_scales[:, 4 * quad : 4 * quad + 4, :].bitcast(I32),
             )
-        load_w1(0, 0)
-        load_w1(0, 1)
         load_tab(1)
+        load_w1(0, 1)
         load_tab(2)
         load_tab(3)
         wo_raw = tile([P, 2, 2 * N], U8, "wo_raw")
         nc.sync.dma_start(wo_raw[:].bitcast(I32), wo_words.rearrange("a p c -> p a c").bitcast(I32))
+        load_wg(0, 4, 0, S // 4)
         for quad in range(4):
-            nc.scalar.dma_start(
+            nc.sync.dma_start(
                 wo_sc_raw[32 * quad : 32 * quad + 4, :, :].bitcast(I32),
                 wo_scales[:, 4 * quad : 4 * quad + 4, :].rearrange("a q c -> q a c").bitcast(I32),
             )
-        nc.sync.dma_start(list2[:], offs2)
-        load_wg(0, 2, 0, S // 2)
-        load_wg(2, 4, 0, S // 2)
+        load_wg(0, 4, S // 4, S // 2)
 
         w_codes = {}
         w_scales = {}
 
-        def quantise_w1(a, b, on_vector):
+        def quantise_w1(a, b, shared):
             grouped = tile([P, K_PASS, PACK], BF16, "w_bf%d%d" % (a, b), "w_bf%d" % b)
             dst = grouped[:].rearrange("p (c u) i -> p c i u", u=4)
             src = w_raw[a, b][:].rearrange("p i (c u) -> p c i u", u=4)
-            if on_vector:
-                nc.vector.tensor_copy(dst, src)
+            if shared:
+                nc.scalar.copy(dst[:, :48], src[:, :48])
+                nc.vector.tensor_copy(dst[:, 48:], src[:, 48:])
             else:
                 nc.scalar.copy(dst, src)
-            w_codes[a, b] = tile([P, K_PASS], U32, "w_codes%d%d" % (a, b))
-            w_scales[a, b] = tile([P, K_PASS], U8, "w_scales%d%d" % (a, b))
+            w_codes[a, b] = tile([P, K_PASS], U32, "w_codes%d%d" % (a, b), "w_codes%d" % b)
+            w_scales[a, b] = tile([P, K_PASS], U8, "w_scales%d%d" % (a, b), "w_scales%d" % b)
             nc.vector.quantize_mx(
                 out=w_codes[a, b][:].bitcast(FP8X4),
                 scales=w_scales[a, b][:],
@@ -126,9 +138,9 @@ def tile_list_leakage_gap_audit_kernel(
         gather_tab(0, [0, S])
         nc.vector.tensor_copy(picked_sc[:], tab_sc[:].indirect(list1[:]))
         quantise_w1(0, 0, False)
+        gather_tab(1, [0, S])
         quantise_w1(0, 1, True)
-        gather_tab(1, [0, S // 2, S])
-        gather_tab(2, [0, S])
+        gather_tab(2, [0, S // 2, S])
         gather_tab(3, [0, S // 4, S // 2, S])
 
         wo_codes = tile([P, 2, 2 * N], U8, "wo_codes")
@@ -143,8 +155,9 @@ def tile_list_leakage_gap_audit_kernel(
             wo_sc_raw[:].rearrange("p a (c t) -> p a c t", t=PACK),
         )
 
-        def product(a, jt, half, index):
-            acc = bank(index, [P, K_PASS], "acc%d_%d_%d" % (a, jt, half))
+        def product(a, jt, half):
+            name = "acc%d_%d_%d" % (a, jt, half)
+            acc = bank(6 + jt % 2, [P, K_PASS], name) if half else ring_bank([P, K_PASS], name)
             cols = slice(jt * P, (jt + 1) * P)
             for b in range(2):
                 k = 2 * half + b
@@ -159,68 +172,66 @@ def tile_list_leakage_gap_audit_kernel(
                 )
             return acc[:].rearrange("p (m t) -> p t m", t=PACK)
 
-        def negated_mag(a, jt, dst):
-            nc.scalar.activation(dst, product(a, jt, 0, jt % 3), COPY, scale=-1.0)
-
-        def gap(a, jt, neg_mag, h):
-            abs_raw = tile([P, PACK, P], F32, "abs_raw%d_%d" % (a, jt), "abs_raw%d" % (jt % 3))
-            nc.scalar.activation(abs_raw[:], product(a, jt, 1, 3 + jt % 3), ABS)
-            turned = bank(6 + jt % 2, [P, PACK, P], "turned%d_%d" % (a, jt))
-            for t in range(PACK):
-                nc.tensor.matmul(turned[:, t, :], neg_mag[:, t, :], ident[:], start=True, stop=False, is_transpose=True)
-                nc.tensor.matmul(turned[:, t, :], abs_raw[:, t, :], ident[:], start=False, stop=True, is_transpose=True)
-            nc.scalar.activation(h[:, :, jt * P : (jt + 1) * P], turned[:], COPY, scale=-1.0)
+        def gaps(a, q, h):
+            pair = (2 * q, 2 * q + 1)
+            neg_mag = {}
+            abs_raw = {}
+            for jt in pair:
+                neg_mag[jt] = tile([P, PACK, P], F32, "neg_mag%d_%d" % (a, jt), "neg_mag%d" % (jt % 4))
+                nc.scalar.activation(neg_mag[jt][:], product(a, jt, 0), COPY, scale=-1.0)
+            for jt in pair:
+                abs_raw[jt] = tile([P, PACK, P], F32, "abs_raw%d_%d" % (a, jt), "abs_raw%d" % (jt % 4))
+                nc.scalar.activation(abs_raw[jt][:], product(a, jt, 1), ABS)
+            for jt in pair:
+                turned = ring_bank([P, PACK, P], "turned%d_%d" % (a, jt))
+                for t in range(PACK):
+                    nc.tensor.matmul(turned[:, t, :], neg_mag[jt][:, t, :], ident[:], start=True, stop=False, is_transpose=True)
+                    nc.tensor.matmul(turned[:, t, :], abs_raw[jt][:, t, :], ident[:], start=False, stop=True, is_transpose=True)
+                nc.scalar.activation(h[:, :, jt * P : (jt + 1) * P], turned[:], COPY, scale=-1.0)
 
         def scatter(h, t, j0, j1):
             nc.vector.tensor_tensor(pages[t][:].indirect(entries(list2, j0, j1)), h[:, t, j0:j1], wg[:, t, j0:j1], MULT)
 
         h0 = tile([P, PACK, S], F32, "h0")
         h1 = tile([P, PACK, S], F32, "h1")
-        neg0 = [tile([P, 2, PACK, P], F32, "neg0_%d" % i) for i in range(4)]
-        for jt in range(8):
-            negated_mag(0, jt, neg0[jt // 2][:, jt % 2, :, :])
-        for jt in range(8):
-            gap(0, jt, neg0[jt // 2][:, jt % 2, :, :], h0)
+        Q = S // 4
+
+        for q in range(4):
+            gaps(0, q, h0)
 
         load_w1(1, 0)
+        load_wg(0, 4, 2 * Q, 3 * Q)
         load_w1(1, 1)
-        load_wg(0, 4, S // 2, S)
-        nc.sync.dma_start(list3[:], offs3)
+        load_wg(0, 4, 3 * Q, S)
         thr_rows = thr.rearrange("(a p t) m -> a p t m", p=P, t=PACK)
         thr1 = [tile([P, PACK, M // 2], F32, "thr1_%d" % i, "tab%d" % i) for i in range(2)]
         for i in range(2):
             nc.sync.dma_start(thr1[i][:], thr_rows[1][:, :, i * M // 2 : (i + 1) * M // 2])
 
-        for j0 in (0, S // 4):
-            for t in (0, 1):
-                scatter(h0, t, j0, j0 + S // 4)
         quantise_w1(1, 0, False)
         quantise_w1(1, 1, False)
-        for t in (2, 3):
-            scatter(h0, t, 0, S // 2)
-        for t in range(PACK):
-            scatter(h0, t, S // 2, S)
+        for j0 in range(0, S, Q):
+            for t in range(PACK):
+                scatter(h0, t, j0, j0 + Q)
 
         thr0 = [tile([P, 2, M], F32, "thr0_%d" % i, "w_raw%d" % i) for i in range(2)]
         for i in range(2):
             nc.sync.dma_start(thr0[i][:], thr_rows[0][:, 2 * i : 2 * i + 2, :])
 
-        for jt in range(8):
-            neg1 = tile([P, PACK, P], F32, "neg1_%d" % jt, "neg1_%d" % (jt % 3))
-            negated_mag(1, jt, neg1[:])
-            gap(1, jt, neg1, h1)
+        for q in range(4):
+            gaps(1, q, h1)
 
         z_codes = [tile([P, M], U32, "z_codes%d" % a) for a in range(2)]
         z_scales = [tile([P, M], U8, "z_scales%d" % a) for a in range(2)]
         z0 = tile([P, PACK, M], BF16, "z0")
-        x0 = [tile([P, M], F32, "x0_%d" % t, "neg0_%d" % t) for t in range(PACK)]
+        x0 = tile([P, PACK, M], F32, "x0")
         for t in range(PACK):
-            nc.vector.tensor_copy(x0[t][:], pages[t][:].indirect(list3[:]))
-        for t in range(PACK):
-            nc.vector.tensor_tensor(z0[:, t, :], x0[t][:], thr0[t // 2][:, t % 2, :], MAX)
+            nc.vector.tensor_copy(x0[:, t, :], pages[t][:].indirect(list3[:]))
+        for i in range(2):
+            nc.vector.tensor_tensor(z0[:, 2 * i : 2 * i + 2, :], x0[:, 2 * i : 2 * i + 2, :], thr0[i][:], MAX)
 
-        def interleave(dst, src):
-            nc.scalar.copy(dst.rearrange("p (c u) t -> p c t u", u=4), src.rearrange("p t (c u) -> p c t u", u=4))
+        def interleave(copy, dst, src):
+            copy(dst.rearrange("p (c u) t -> p c t u", u=4), src.rearrange("p t (c u) -> p c t u", u=4))
 
         def quantise_z(a, grouped, m0, m1):
             nc.vector.quantize_mx(
@@ -231,7 +242,7 @@ def tile_list_leakage_gap_audit_kernel(
 
         z0_grouped = [tile([P, M // 2, PACK], BF16, "z0_grouped%d" % i, "picked%d" % i) for i in range(2)]
         for i in range(2):
-            interleave(z0_grouped[i][:], z0[:, :, i * M // 2 : (i + 1) * M // 2])
+            interleave(nc.scalar.copy, z0_grouped[i][:], z0[:, :, i * M // 2 : (i + 1) * M // 2])
 
         for j0 in (0, S // 2):
             for t in range(PACK):
@@ -271,40 +282,69 @@ def tile_list_leakage_gap_audit_kernel(
                 in_=grouped.rearrange("p m t -> p (m t)"),
             )
 
+        def store_words(m0, m1):
+            nc.sync.dma_start(out_words[:, m0:m1], y_codes[:, m0:m1].bitcast(I32))
+
+        def store_y(m0, m1):
+            nc.sync.dma_start(out_rows[:, :, m0:m1], y[:, :, m0:m1])
+
         chunks = M // CHUNK
-        for c in range(chunks):
-            m0 = c * CHUNK
-            last = c == chunks - 1
-            x1 = tile([P, PACK, CHUNK], F32, "x1_%d" % c, "tab%d" % (2 + c % 2))
-            z1 = tile([P, PACK, CHUNK], BF16, "z1_%d" % c, "w_bf%d" % (c % 2))
-            z1_grouped = tile([P, CHUNK, PACK], BF16, "z1_grouped%d" % c, "picked%d" % (2 + c % 2))
-            y_grouped = tile([P, CHUNK, PACK], BF16, "y_grouped%d" % c, "y_grouped%d" % (c % 2))
+        last = chunks - 1
+        x1 = {}
+        z1_grouped = {}
+
+        def fetch(c):
+            x1[c] = tile([P, PACK, CHUNK], F32, "x1_%d" % c, "tab%d" % (2 + c % 2))
             for t in range(PACK):
-                nc.vector.tensor_copy(x1[:, t, :], pages[t][:].indirect(entries(list3, m0, m0 + CHUNK)))
-            step = P if last else CHUNK
-            for s0 in range(0, CHUNK, step):
-                part = slice(s0, s0 + step)
-                t0 = (m0 + s0) % (M // 2)
-                nc.vector.tensor_tensor(z1[:, :, part], x1[:, :, part], thr1[m0 // (M // 2)][:, :, t0 : t0 + step], MAX)
-                interleave(z1_grouped[:, part, :], z1[:, :, part])
-            for s0 in range(0, CHUNK, step):
-                quantise_z(1, z1_grouped[:, s0 : s0 + step, :], m0 + s0, m0 + s0 + step)
+                nc.vector.tensor_copy(x1[c][:, t, :], pages[t][:].indirect(entries(list3, c * CHUNK, (c + 1) * CHUNK)))
+
+        def parts(c):
+            step = P if c == last else CHUNK
+            return [(s0, s0 + step) for s0 in range(0, CHUNK, step)]
+
+        def threshold(c):
+            z1 = tile([P, PACK, CHUNK], BF16, "z1_%d" % c, "w_bf0")
+            z1_grouped[c] = tile([P, CHUNK, PACK], BF16, "z1_grouped%d" % c, "picked%d" % (2 + c % 2))
+            half, t0 = divmod(c * CHUNK, M // 2)
+            for s0, s1 in parts(c):
+                nc.vector.tensor_tensor(z1[:, :, s0:s1], x1[c][:, :, s0:s1], thr1[half][:, :, t0 + s0 : t0 + s1], MAX)
+            for s0, s1 in parts(c):
+                interleave(nc.vector.tensor_copy if c == last else nc.scalar.copy, z1_grouped[c][:, s0:s1, :], z1[:, :, s0:s1])
+
+        def quantise_z1(c):
+            for s0, s1 in parts(c):
+                quantise_z(1, z1_grouped[c][:, s0:s1, :], c * CHUNK + s0, c * CHUNK + s1)
+
+        def finish(c):
+            m0 = c * CHUNK
+            y_grouped = tile([P, CHUNK, PACK], BF16, "y_grouped%d" % c, "y_grouped%d" % (c % 2))
             for s0 in range(0, CHUNK, P):
                 i = (m0 + s0) // P
                 output_pass(1, i)
                 rounded = y_grouped[:, s0 : s0 + P, :]
                 sums = y_banks[i][:].rearrange("p t m -> p m t")
-                if last:
+                if c == last:
                     nc.vector.tensor_copy(rounded, sums)
                     nc.scalar.copy(y[:, :, i * P : (i + 1) * P], y_banks[i][:])
                     quantise_y(rounded, i * P, (i + 1) * P)
+                    store_y(i * P, (i + 1) * P)
                 else:
                     nc.scalar.copy(y[:, :, i * P : (i + 1) * P], y_banks[i][:])
                     nc.scalar.copy(rounded, sums)
-            if not last:
+            if c != last:
                 quantise_y(y_grouped[:], m0, m0 + CHUNK)
-            nc.sync.dma_start(out_rows[:, :, m0 : m0 + CHUNK], y[:, :, m0 : m0 + CHUNK])
-            nc.sync.dma_start(out_words[:, m0 : m0 + CHUNK], y_codes[:, m0 : m0 + CHUNK].bitcast(I32))
+                store_y(m0, m0 + CHUNK)
+            store_words(m0, m0 + CHUNK)
+
+        for c in range(chunks + 1):
+            if c < chunks:
+                fetch(c)
+            if c > 0:
+                quantise_z1(c - 1)
+            if c < chunks:
+                threshold(c)
+            if c > 0:
+                finish(c - 1)
         for quad in range(4):
             queue = nc.sync if quad % 2 == 0 else nc.scalar
             queue.dma_start(

@@ -36,14 +36,8 @@ def tile_list_leakage_gap_audit_kernel(
         def tile(shape, dtype, name, tag=None):
             return sb.tile(shape, dtype, name=name, tag=tag or name, align_bytes=64)
 
-        opened = []
-
         def bank(index, shape, name):
             return ps.tile(shape, F32, name=name, tag="bank%d" % index)
-
-        def ring_bank(shape, name):
-            opened.append(name)
-            return bank(len(opened) % 6, shape, name)
 
         def entries(lst, j0, j1):
             return lst[:, j0 // 16 : j1 // 16]
@@ -54,202 +48,213 @@ def tile_list_leakage_gap_audit_kernel(
         ident = tile([P, P], F32, "ident")
         tab_sc = tile([P, T], U8, "tab_sc")
         wo_sc_raw = tile([P, 2, N], U8, "wo_sc_raw")
-        pages = [tile([P, T2], F32, "page%d" % t) for t in range(PACK)]
         nc.gpsimd.memset(tab_sc[:].bitcast(I32), 0)
         nc.gpsimd.memset(wo_sc_raw[:].bitcast(I32), 0)
         make_identity(nc, ident[:])
-        for t in range(PACK):
-            nc.vector.memset(pages[t][:].bitcast(I32), 0)
+        warm = tile([P, 16], F32, "warm")
+        nc.vector.memset(warm[:, 0:1], 0.0)
+        nc.scalar.activation(warm[:, 8:9], warm[:, 0:1], ABS)
 
         tab = [tile([P, T], I32, "tab%d" % a) for a in range(4)]
-
-        def load_tab(a, pieces=1):
-            words = tab_words[a].rearrange("p t i -> p (t i)").bitcast(I32)
-            for c0 in range(0, T, T // pieces):
-                nc.sync.dma_start(tab[a][:, c0 : c0 + T // pieces], words[:, c0 : c0 + T // pieces])
-
         w_raw = {}
 
-        def load_w1(a, b, pieces=1):
-            w_raw[a, b] = tile([P, PACK, K_PASS], F32, "w_raw%d%d" % (a, b), "w_raw%d" % b)
-            rows = w1[b * K_PASS : (b + 1) * K_PASS, a * K_PASS : (a + 1) * K_PASS]
+        def load_w1(g, b, i0, i1):
+            if (g, b) not in w_raw:
+                w_raw[g, b] = tile([P, PACK, K_PASS], F32, "w_raw%d%d" % (g, b), "w_raw%d" % b)
+            rows = w1[b * K_PASS : (b + 1) * K_PASS, g * K_PASS : (g + 1) * K_PASS]
             rows = rows.rearrange("(p i) c -> p i c", i=PACK)
-            for i0 in range(0, PACK, PACK // pieces):
-                nc.sync.dma_start(w_raw[a, b][:, i0 : i0 + PACK // pieces, :], rows[:, i0 : i0 + PACK // pieces, :])
+            nc.sync.dma_start(w_raw[g, b][:, i0:i1, :], rows[:, i0:i1, :])
 
-        wg = tile([P, PACK, S], F32, "wg")
+        wg = [tile([P, 2, S], F32, "wg%d" % tp) for tp in range(2)]
         wgs_rows = wgs.rearrange("(q t) j -> q t j", t=PACK)
 
-        def load_wg(t0, t1, j0, j1):
-            for quad in range(4):
-                nc.sync.dma_start(wg[32 * quad : 32 * quad + 32, t0:t1, j0:j1], wgs_rows[:, t0:t1, j0:j1])
+        def load_wg(tp, j0, j1):
+            for quad in (0, 2, 1, 3):
+                nc.sync.dma_start(wg[tp][32 * quad : 32 * quad + 32, :, j0:j1], wgs_rows[:, 2 * tp : 2 * tp + 2, j0:j1])
 
+        wo_raw = tile([P, 2, 2 * N], U8, "wo_raw")
         nc.sync.dma_start(list1[:], offs)
         nc.sync.dma_start(list2[:], offs2)
         nc.sync.dma_start(list3[:], offs3)
-        load_tab(0, 2)
-        load_w1(0, 0, 2)
+        for a in range(2):
+            nc.sync.dma_start(wo_raw[:, a, :].bitcast(I32), wo_words[a].bitcast(I32))
+        for i in range(3):
+            load_w1(0, 0, i, i + 1)
         for quad in range(4):
             nc.sync.dma_start(
                 tab_sc[32 * quad : 32 * quad + 16, :].bitcast(I32),
                 tab_scales[:, 4 * quad : 4 * quad + 4, :].bitcast(I32),
             )
-        load_tab(1)
-        load_w1(0, 1)
-        load_tab(2)
-        load_tab(3)
-        wo_raw = tile([P, 2, 2 * N], U8, "wo_raw")
-        nc.sync.dma_start(wo_raw[:].bitcast(I32), wo_words.rearrange("a p c -> p a c").bitcast(I32))
-        load_wg(0, 4, 0, S // 4)
-        for quad in range(4):
-            nc.sync.dma_start(
-                wo_sc_raw[32 * quad : 32 * quad + 4, :, :].bitcast(I32),
-                wo_scales[:, 4 * quad : 4 * quad + 4, :].rearrange("a q c -> q a c").bitcast(I32),
-            )
-        load_wg(0, 4, S // 4, S // 2)
-
-        w_codes = {}
-        w_scales = {}
-
-        def quantise_w1(a, b, shared):
-            grouped = tile([P, K_PASS, PACK], BF16, "w_bf%d%d" % (a, b), "w_bf%d" % b)
-            dst = grouped[:].rearrange("p (c u) i -> p c i u", u=4)
-            src = w_raw[a, b][:].rearrange("p i (c u) -> p c i u", u=4)
-            if shared:
-                nc.scalar.copy(dst[:, :48], src[:, :48])
-                nc.vector.tensor_copy(dst[:, 48:], src[:, 48:])
-            else:
-                nc.scalar.copy(dst, src)
-            w_codes[a, b] = tile([P, K_PASS], U32, "w_codes%d%d" % (a, b), "w_codes%d" % b)
-            w_scales[a, b] = tile([P, K_PASS], U8, "w_scales%d%d" % (a, b), "w_scales%d" % b)
-            nc.vector.quantize_mx(
-                out=w_codes[a, b][:].bitcast(FP8X4),
-                scales=w_scales[a, b][:],
-                in_=grouped[:].rearrange("p c i -> p (c i)"),
-            )
-
-        picked_sc = tile([P, S], U8, "picked_sc")
-        picked = [tile([P, S], U32, "picked%d" % a) for a in range(4)]
-
-        def gather_tab(a, cuts):
-            for j0, j1 in zip(cuts[:-1], cuts[1:]):
-                nc.vector.tensor_copy(picked[a][:, j0:j1], tab[a][:].bitcast(U32).indirect(entries(list1, j0, j1)))
-
-        gather_tab(0, [0, S])
-        nc.vector.tensor_copy(picked_sc[:], tab_sc[:].indirect(list1[:]))
-        quantise_w1(0, 0, False)
-        gather_tab(1, [0, S])
-        quantise_w1(0, 1, True)
-        gather_tab(2, [0, S // 2, S])
-        gather_tab(3, [0, S // 4, S // 2, S])
+        load_w1(0, 0, 3, 4)
+        load_w1(0, 1, 0, 4)
+        for a in range(4):
+            nc.sync.dma_start(tab[a][:], tab_words[a].rearrange("p t i -> p (t i)").bitcast(I32))
+        load_wg(0, 0, CHUNK)
+        load_wg(0, CHUNK, S)
 
         wo_codes = tile([P, 2, 2 * N], U8, "wo_codes")
-        wo_sc = tile([P, 2, N], U8, "wo_sc")
         for a in range(2):
             nc.vector.tensor_copy(
                 wo_codes[:, a, :].rearrange("p (t c b) -> p c t b", t=PACK, b=2),
                 wo_raw[:, a, :].rearrange("p (c t b) -> p c t b", t=PACK, b=2),
             )
+
+        w_codes = {}
+        w_scales = {}
+
+        def quantise_w1(g, b):
+            grouped = tile([P, 2, K_PASS // 2, PACK], BF16, "w_bf%d%d" % (g, b), "late%d" % b if g else None)
+            src = w_raw[g, b][:].rearrange("p i (m h u) -> p h m i u", h=2, u=2)
+            for tp in range(2):
+                nc.scalar.copy(grouped[:, tp].rearrange("p (m u) i -> p m i u", u=2), src[:, tp])
+            w_codes[g, b] = tile([P, K_PASS], U32, "w_codes%d%d" % (g, b))
+            w_scales[g, b] = tile([P, K_PASS], U8, "w_scales%d%d" % (g, b))
+            nc.vector.quantize_mx(
+                out=w_codes[g, b][:].bitcast(FP8X4),
+                scales=w_scales[g, b][:],
+                in_=grouped[:].rearrange("p h c i -> p (h c i)"),
+            )
+
+        picked_sc = tile([P, S], U8, "picked_sc")
+        picked = [tile([P, S], U32, "picked%d" % a) for a in range(4)]
+
+        def gather_tab(a, j0, j1):
+            nc.vector.tensor_copy(picked[a][:, j0:j1], tab[a][:].bitcast(U32).indirect(entries(list1, j0, j1)))
+
+        quantise_w1(0, 0)
+        nc.vector.tensor_copy(picked_sc[:], tab_sc[:].indirect(list1[:]))
+        quantise_w1(0, 1)
+        for a in range(3):
+            gather_tab(a, 0, S)
+        gather_tab(3, 0, CHUNK)
+        gather_tab(3, CHUNK, 2 * CHUNK)
+        gather_tab(3, 2 * CHUNK, S)
+
+        pages = [tile([P, T2], F32, "page%d" % u) for u in range(2)]
+        for u in range(2):
+            nc.vector.memset(pages[u][:].bitcast(I32), 0)
+
+        def product(g, tp, q, half, acc):
+            w_cols = slice(tp * CHUNK, (tp + 1) * CHUNK)
+            for s in range(2):
+                cols = slice(q * CHUNK + s * P, q * CHUNK + (s + 1) * P)
+                for b in range(2):
+                    k = 2 * half + b
+                    nc.tensor.matmul_mx(
+                        out=acc[:, s, :],
+                        lhsT=picked[k][:, cols].bitcast(FP8X4),
+                        lhsT_scale=picked_sc[4 * k :, cols],
+                        rhs=w_codes[g, b][:, w_cols].bitcast(FP8X4),
+                        rhs_scale=w_scales[g, b][:, w_cols],
+                        start=(b == 0),
+                        stop=(b == 1),
+                    )
+            return acc[:].rearrange("p s (m u) -> p s u m", u=2)
+
+        turns = []
+
+        def gaps(g, tp, q, h_cols):
+            n = 8 * g + 4 * tp + q
+            neg_mag = tile([P, 2, 2, P], F32, "neg_mag%d" % n, "neg_mag%d" % (n % 2))
+            abs_raw = tile([P, 2, 2, P], F32, "abs_raw%d" % n, "late%d" % (n - 3) if n in (3, 4) else "abs_raw%d" % (n % 2))
+            mag = bank(2 * n % 3, [P, 2, CHUNK], "mag%d" % n)
+            nc.scalar.activation(neg_mag[:], product(g, tp, q, 0, mag), COPY, scale=-1.0)
+            raw = bank((2 * n + 1) % 3, [P, 2, CHUNK], "raw%d" % n)
+            nc.scalar.activation(abs_raw[:], product(g, tp, q, 1, raw), ABS)
+            for rows in ([(0, 1), (1, 2)] if n == 0 else [(0, 2)]):
+                turns.append(n)
+                turned = bank(3 + len(turns) % 5, [P, 2, CHUNK], "turned%d" % len(turns))
+                for u in range(*rows):
+                    for s in range(2):
+                        dst = turned[:, u, s * P : (s + 1) * P]
+                        nc.tensor.matmul(dst, neg_mag[:, s, u, :], ident[:], start=True, stop=False, is_transpose=True)
+                        nc.tensor.matmul(dst, abs_raw[:, s, u, :], ident[:], start=False, stop=True, is_transpose=True)
+                nc.scalar.activation(h_cols[:, rows[0] : rows[1], :], turned[:, rows[0] : rows[1], :], COPY, scale=-1.0)
+
+        def scatter(u, h_row, tp, j0, j1):
+            nc.vector.tensor_tensor(pages[u][:].indirect(entries(list2, j0, j1)), h_row, wg[tp][:, u, j0:j1], MULT)
+
+        def fetch(dst, u, m0, m1):
+            nc.vector.tensor_copy(dst, pages[u][:].indirect(entries(list3, m0, m1)))
+
+        for q in range(4):
+            h_first = tile([P, 2, CHUNK], F32, "h_first%d" % q)
+            gaps(0, 0, q, h_first[:])
+            for u in range(2):
+                scatter(u, h_first[:, u, :], 0, q * CHUNK, (q + 1) * CHUNK)
+
+        load_w1(1, 0, 0, 4)
+        load_w1(1, 1, 0, 4)
+        load_wg(1, 0, S)
+        for quad in range(4):
+            nc.sync.dma_start(
+                wo_sc_raw[32 * quad : 32 * quad + 4, :, :].bitcast(I32),
+                wo_scales[:, 4 * quad : 4 * quad + 4, :].rearrange("a q c -> q a c").bitcast(I32),
+            )
+        thr_rows = thr.rearrange("(a p t) m -> a p t m", p=P, t=PACK)
+        thr_sb = {}
+        for g in range(2):
+            for i in range(2):
+                thr_sb[g, i] = tile([P, PACK, M // 2], F32, "thr%d_%d" % (g, i), "tab%d" % (2 * g + i))
+                nc.sync.dma_start(thr_sb[g, i][:], thr_rows[g][:, :, i * M // 2 : (i + 1) * M // 2])
+
+        x0 = tile([P, PACK, M], F32, "x0")
+        for u in range(2):
+            fetch(x0[:, u, :], u, 0, M)
+        quantise_w1(1, 0)
+
+        def put_rows(g, tp):
+            h = tile([P, 2, S], F32, "h%d%d" % (g, tp))
+            for q in range(4):
+                gaps(g, tp, q, h[:, :, q * CHUNK : (q + 1) * CHUNK])
+                if (g, tp, q) == (0, 1, 0):
+                    quantise_w1(1, 1)
+            for u in range(2):
+                scatter(u, h[:, u, :], tp, 0, S)
+
+        put_rows(0, 1)
+        for u in range(2):
+            fetch(x0[:, 2 + u, :], u, 0, M)
+
+        wo_sc = tile([P, 2, N], U8, "wo_sc")
         nc.vector.tensor_copy(
             wo_sc[:].rearrange("p a (t c) -> p a c t", t=PACK),
             wo_sc_raw[:].rearrange("p a (c t) -> p a c t", t=PACK),
         )
 
-        def product(a, jt, half):
-            name = "acc%d_%d_%d" % (a, jt, half)
-            acc = bank(6 + jt % 2, [P, K_PASS], name) if half else ring_bank([P, K_PASS], name)
-            cols = slice(jt * P, (jt + 1) * P)
-            for b in range(2):
-                k = 2 * half + b
-                nc.tensor.matmul_mx(
-                    out=acc[:],
-                    lhsT=picked[k][:, cols].bitcast(FP8X4),
-                    lhsT_scale=picked_sc[4 * k :, cols],
-                    rhs=w_codes[a, b][:].bitcast(FP8X4),
-                    rhs_scale=w_scales[a, b][:],
-                    start=(b == 0),
-                    stop=(b == 1),
-                )
-            return acc[:].rearrange("p (m t) -> p t m", t=PACK)
+        z_codes = [tile([P, M], U32, "z_codes%d" % g) for g in range(2)]
+        z_scales = [tile([P, M], U8, "z_scales%d" % g) for g in range(2)]
 
-        def gaps(a, q, h):
-            pair = (2 * q, 2 * q + 1)
-            neg_mag = {}
-            abs_raw = {}
-            for jt in pair:
-                neg_mag[jt] = tile([P, PACK, P], F32, "neg_mag%d_%d" % (a, jt), "neg_mag%d" % (jt % 4))
-                nc.scalar.activation(neg_mag[jt][:], product(a, jt, 0), COPY, scale=-1.0)
-            for jt in pair:
-                abs_raw[jt] = tile([P, PACK, P], F32, "abs_raw%d_%d" % (a, jt), "abs_raw%d" % (jt % 4))
-                nc.scalar.activation(abs_raw[jt][:], product(a, jt, 1), ABS)
-            for jt in pair:
-                turned = ring_bank([P, PACK, P], "turned%d_%d" % (a, jt))
-                for t in range(PACK):
-                    nc.tensor.matmul(turned[:, t, :], neg_mag[jt][:, t, :], ident[:], start=True, stop=False, is_transpose=True)
-                    nc.tensor.matmul(turned[:, t, :], abs_raw[jt][:, t, :], ident[:], start=False, stop=True, is_transpose=True)
-                nc.scalar.activation(h[:, :, jt * P : (jt + 1) * P], turned[:], COPY, scale=-1.0)
+        def threshold(grouped, x, g, m0, m1):
+            half, c0 = divmod(m0, M // 2)
+            nc.vector.tensor_tensor(
+                grouped.rearrange("p (c u) t -> p c t u", u=2),
+                x.rearrange("p t (c u) -> p c t u", u=2),
+                thr_sb[g, half][:, :, c0 : c0 + m1 - m0].rearrange("p t (c u) -> p c t u", u=2),
+                MAX,
+            )
 
-        def scatter(h, t, j0, j1):
-            nc.vector.tensor_tensor(pages[t][:].indirect(entries(list2, j0, j1)), h[:, t, j0:j1], wg[:, t, j0:j1], MULT)
-
-        h0 = tile([P, PACK, S], F32, "h0")
-        h1 = tile([P, PACK, S], F32, "h1")
-        Q = S // 4
-
-        for q in range(4):
-            gaps(0, q, h0)
-
-        load_w1(1, 0)
-        load_wg(0, 4, 2 * Q, 3 * Q)
-        load_w1(1, 1)
-        load_wg(0, 4, 3 * Q, S)
-        thr_rows = thr.rearrange("(a p t) m -> a p t m", p=P, t=PACK)
-        thr1 = [tile([P, PACK, M // 2], F32, "thr1_%d" % i, "tab%d" % i) for i in range(2)]
-        for i in range(2):
-            nc.sync.dma_start(thr1[i][:], thr_rows[1][:, :, i * M // 2 : (i + 1) * M // 2])
-
-        quantise_w1(1, 0, False)
-        quantise_w1(1, 1, False)
-        for j0 in range(0, S, Q):
-            for t in range(PACK):
-                scatter(h0, t, j0, j0 + Q)
-
-        thr0 = [tile([P, 2, M], F32, "thr0_%d" % i, "w_raw%d" % i) for i in range(2)]
-        for i in range(2):
-            nc.sync.dma_start(thr0[i][:], thr_rows[0][:, 2 * i : 2 * i + 2, :])
-
-        for q in range(4):
-            gaps(1, q, h1)
-
-        z_codes = [tile([P, M], U32, "z_codes%d" % a) for a in range(2)]
-        z_scales = [tile([P, M], U8, "z_scales%d" % a) for a in range(2)]
-        z0 = tile([P, PACK, M], BF16, "z0")
-        x0 = tile([P, PACK, M], F32, "x0")
-        for t in range(PACK):
-            nc.vector.tensor_copy(x0[:, t, :], pages[t][:].indirect(list3[:]))
-        for i in range(2):
-            nc.vector.tensor_tensor(z0[:, 2 * i : 2 * i + 2, :], x0[:, 2 * i : 2 * i + 2, :], thr0[i][:], MAX)
-
-        def interleave(copy, dst, src):
-            copy(dst.rearrange("p (c u) t -> p c t u", u=4), src.rearrange("p t (c u) -> p c t u", u=4))
-
-        def quantise_z(a, grouped, m0, m1):
+        def quantise_z(g, grouped, m0, m1):
             nc.vector.quantize_mx(
-                out=z_codes[a][:, m0:m1].bitcast(FP8X4),
-                scales=z_scales[a][:, m0:m1],
+                out=z_codes[g][:, m0:m1].bitcast(FP8X4),
+                scales=z_scales[g][:, m0:m1],
                 in_=grouped.rearrange("p m t -> p (m t)"),
             )
 
-        z0_grouped = [tile([P, M // 2, PACK], BF16, "z0_grouped%d" % i, "picked%d" % i) for i in range(2)]
+        z0_grouped = [tile([P, M // 2, PACK], BF16, "z0_grouped%d" % i) for i in range(2)]
         for i in range(2):
-            interleave(nc.scalar.copy, z0_grouped[i][:], z0[:, :, i * M // 2 : (i + 1) * M // 2])
-
-        for j0 in (0, S // 2):
-            for t in range(PACK):
-                scatter(h1, t, j0, j0 + S // 2)
-
+            threshold(z0_grouped[i][:], x0[:, :, i * M // 2 : (i + 1) * M // 2], 0, i * M // 2, (i + 1) * M // 2)
         for i in range(2):
             quantise_z(0, z0_grouped[i][:], i * M // 2, (i + 1) * M // 2)
+
+        chunks = M // CHUNK
+        last = chunks - 1
+        put_rows(1, 0)
+        x1 = [tile([P, PACK, CHUNK], F32, "x1_%d" % c, "picked%d" % c) for c in range(chunks)]
+        for c in range(chunks):
+            for u in range(2):
+                fetch(x1[c][:, u, :], u, c * CHUNK, (c + 1) * CHUNK)
+        put_rows(1, 1)
 
         y_banks = [bank(i, [P, PACK, P], "y%d" % i) for i in range(M // P)]
 
@@ -269,11 +274,15 @@ def tile_list_leakage_gap_audit_kernel(
         for i in range(M // P):
             output_pass(0, i)
 
-        y = tile([P, PACK, M], F32, "y", "h0")
+        y = [tile([P, PACK, M // 2], F32, "y%d" % i, "w_raw%d" % i) for i in range(2)]
         y_codes = tile([P, M], U32, "y_codes")
         y_scales = tile([P, M], U8, "y_scales")
         out_rows = out_0.rearrange("(p t) m -> p t m", t=PACK)
         out_words = out_1[0].rearrange("p m t -> p (m t)").bitcast(I32)
+
+        def y_cols(m0, m1):
+            half, c0 = divmod(m0, M // 2)
+            return y[half][:, :, c0 : c0 + m1 - m0]
 
         def quantise_y(grouped, m0, m1):
             nc.vector.quantize_mx(
@@ -282,34 +291,16 @@ def tile_list_leakage_gap_audit_kernel(
                 in_=grouped.rearrange("p m t -> p (m t)"),
             )
 
-        def store_words(m0, m1):
-            nc.sync.dma_start(out_words[:, m0:m1], y_codes[:, m0:m1].bitcast(I32))
-
-        def store_y(m0, m1):
-            nc.sync.dma_start(out_rows[:, :, m0:m1], y[:, :, m0:m1])
-
-        chunks = M // CHUNK
-        last = chunks - 1
-        x1 = {}
         z1_grouped = {}
-
-        def fetch(c):
-            x1[c] = tile([P, PACK, CHUNK], F32, "x1_%d" % c, "tab%d" % (2 + c % 2))
-            for t in range(PACK):
-                nc.vector.tensor_copy(x1[c][:, t, :], pages[t][:].indirect(entries(list3, c * CHUNK, (c + 1) * CHUNK)))
 
         def parts(c):
             step = P if c == last else CHUNK
             return [(s0, s0 + step) for s0 in range(0, CHUNK, step)]
 
-        def threshold(c):
-            z1 = tile([P, PACK, CHUNK], BF16, "z1_%d" % c, "w_bf0")
-            z1_grouped[c] = tile([P, CHUNK, PACK], BF16, "z1_grouped%d" % c, "picked%d" % (2 + c % 2))
-            half, t0 = divmod(c * CHUNK, M // 2)
+        def threshold_z1(c):
+            z1_grouped[c] = tile([P, CHUNK, PACK], BF16, "z1_grouped%d" % c, "z1_grouped%d" % (c % 2))
             for s0, s1 in parts(c):
-                nc.vector.tensor_tensor(z1[:, :, s0:s1], x1[c][:, :, s0:s1], thr1[half][:, :, t0 + s0 : t0 + s1], MAX)
-            for s0, s1 in parts(c):
-                interleave(nc.vector.tensor_copy if c == last else nc.scalar.copy, z1_grouped[c][:, s0:s1, :], z1[:, :, s0:s1])
+                threshold(z1_grouped[c][:, s0:s1, :], x1[c][:, :, s0:s1], 1, c * CHUNK + s0, c * CHUNK + s1)
 
         def quantise_z1(c):
             for s0, s1 in parts(c):
@@ -325,25 +316,26 @@ def tile_list_leakage_gap_audit_kernel(
                 sums = y_banks[i][:].rearrange("p t m -> p m t")
                 if c == last:
                     nc.vector.tensor_copy(rounded, sums)
-                    nc.scalar.copy(y[:, :, i * P : (i + 1) * P], y_banks[i][:])
+                    nc.scalar.copy(y_cols(i * P, (i + 1) * P), y_banks[i][:])
                     quantise_y(rounded, i * P, (i + 1) * P)
-                    store_y(i * P, (i + 1) * P)
+                    nc.sync.dma_start(out_rows[:, :, i * P : (i + 1) * P], y_cols(i * P, (i + 1) * P))
                 else:
-                    nc.scalar.copy(y[:, :, i * P : (i + 1) * P], y_banks[i][:])
                     nc.scalar.copy(rounded, sums)
+                    nc.scalar.copy(y_cols(i * P, (i + 1) * P), y_banks[i][:])
             if c != last:
                 quantise_y(y_grouped[:], m0, m0 + CHUNK)
-                store_y(m0, m0 + CHUNK)
-            store_words(m0, m0 + CHUNK)
+                nc.sync.dma_start(out_rows[:, :, m0 : m0 + CHUNK], y_cols(m0, m0 + CHUNK))
+            nc.sync.dma_start(out_words[:, m0 : m0 + CHUNK], y_codes[:, m0 : m0 + CHUNK].bitcast(I32))
 
         for c in range(chunks + 1):
             if c < chunks:
-                fetch(c)
+                fetch(x1[c][:, 2, :], 0, c * CHUNK, (c + 1) * CHUNK)
+            if c > 0:
+                threshold_z1(c - 1)
+            if c < chunks:
+                fetch(x1[c][:, 3, :], 1, c * CHUNK, (c + 1) * CHUNK)
             if c > 0:
                 quantise_z1(c - 1)
-            if c < chunks:
-                threshold(c)
-            if c > 0:
                 finish(c - 1)
         for quad in range(4):
             queue = nc.sync if quad % 2 == 0 else nc.scalar

@@ -58,12 +58,12 @@ def tile_list_leakage_gap_audit_kernel(
         tab = [tile([P, T], I32, "tab%d" % a) for a in range(4)]
         w_raw = {}
 
-        def load_w1(g, b, i0, i1):
-            if (g, b) not in w_raw:
-                w_raw[g, b] = tile([P, PACK, K_PASS], F32, "w_raw%d%d" % (g, b), "w_raw%d" % b)
-            rows = w1[b * K_PASS : (b + 1) * K_PASS, g * K_PASS : (g + 1) * K_PASS]
-            rows = rows.rearrange("(p i) c -> p i c", i=PACK)
-            nc.sync.dma_start(w_raw[g, b][:, i0:i1, :], rows[:, i0:i1, :])
+        def load_w1(g, b, e, i0=0, i1=PACK):
+            if (g, b, e) not in w_raw:
+                w_raw[g, b, e] = tile([P, PACK, CHUNK], F32, "w_raw%d%d%d" % (g, b, e), "w_raw%d" % (2 * b + e))
+            c0 = g * K_PASS + e * CHUNK
+            rows = w1[b * K_PASS : (b + 1) * K_PASS, c0 : c0 + CHUNK].rearrange("(p i) c -> p i c", i=PACK)
+            nc.sync.dma_start(w_raw[g, b, e][:, i0:i1, :], rows[:, i0:i1, :])
 
         wg = [tile([P, 2, S], F32, "wg%d" % tp) for tp in range(2)]
         wgs_rows = wgs.rearrange("(q t) j -> q t j", t=PACK)
@@ -76,37 +76,33 @@ def tile_list_leakage_gap_audit_kernel(
         nc.sync.dma_start(list1[:], offs)
         nc.sync.dma_start(list2[:], offs2)
         nc.sync.dma_start(list3[:], offs3)
-        for a in range(2):
-            nc.sync.dma_start(wo_raw[:, a, :].bitcast(I32), wo_words[a].bitcast(I32))
-        for i in range(3):
-            load_w1(0, 0, i, i + 1)
+        for e in range(2):
+            load_w1(0, 0, e, 0, 2)
+            load_w1(0, 0, e, 2, 4)
+        load_w1(0, 1, 0, 0, 2)
         for quad in range(4):
             nc.sync.dma_start(
                 tab_sc[32 * quad : 32 * quad + 16, :].bitcast(I32),
                 tab_scales[:, 4 * quad : 4 * quad + 4, :].bitcast(I32),
             )
-        load_w1(0, 0, 3, 4)
-        load_w1(0, 1, 0, 4)
+        load_w1(0, 1, 0, 2, 4)
+        load_w1(0, 1, 1)
         for a in range(4):
             nc.sync.dma_start(tab[a][:], tab_words[a].rearrange("p t i -> p (t i)").bitcast(I32))
+        nc.sync.dma_start(wo_raw[:].bitcast(I32), wo_words.rearrange("a p c -> p a c").bitcast(I32))
         load_wg(0, 0, CHUNK)
         load_wg(0, CHUNK, S)
-
-        wo_codes = tile([P, 2, 2 * N], U8, "wo_codes")
-        for a in range(2):
-            nc.vector.tensor_copy(
-                wo_codes[:, a, :].rearrange("p (t c b) -> p c t b", t=PACK, b=2),
-                wo_raw[:, a, :].rearrange("p (c t b) -> p c t b", t=PACK, b=2),
-            )
 
         w_codes = {}
         w_scales = {}
 
         def quantise_w1(g, b):
             grouped = tile([P, 2, K_PASS // 2, PACK], BF16, "w_bf%d%d" % (g, b), "late%d" % b if g else None)
-            src = w_raw[g, b][:].rearrange("p i (m h u) -> p h m i u", h=2, u=2)
-            for tp in range(2):
-                nc.scalar.copy(grouped[:, tp].rearrange("p (m u) i -> p m i u", u=2), src[:, tp])
+            for e in range(2):
+                nc.scalar.copy(
+                    grouped[:, :, e * P : (e + 1) * P, :].rearrange("p h (m u) i -> p h m i u", u=2),
+                    w_raw[g, b, e][:].rearrange("p i (m h u) -> p h m i u", h=2, u=2),
+                )
             w_codes[g, b] = tile([P, K_PASS], U32, "w_codes%d%d" % (g, b))
             w_scales[g, b] = tile([P, K_PASS], U8, "w_scales%d%d" % (g, b))
             nc.vector.quantize_mx(
@@ -123,12 +119,20 @@ def tile_list_leakage_gap_audit_kernel(
 
         quantise_w1(0, 0)
         nc.vector.tensor_copy(picked_sc[:], tab_sc[:].indirect(list1[:]))
+        gather_tab(0, 0, S)
         quantise_w1(0, 1)
-        for a in range(3):
+        for a in range(1, 3):
             gather_tab(a, 0, S)
         gather_tab(3, 0, CHUNK)
         gather_tab(3, CHUNK, 2 * CHUNK)
         gather_tab(3, 2 * CHUNK, S)
+
+        wo_codes = tile([P, 2, 2 * N], U8, "wo_codes")
+        for a in range(2):
+            nc.vector.tensor_copy(
+                wo_codes[:, a, :].rearrange("p (t c b) -> p c t b", t=PACK, b=2),
+                wo_raw[:, a, :].rearrange("p (c t b) -> p c t b", t=PACK, b=2),
+            )
 
         pages = [tile([P, T2], F32, "page%d" % u) for u in range(2)]
         for u in range(2):
@@ -136,18 +140,18 @@ def tile_list_leakage_gap_audit_kernel(
 
         def product(g, tp, q, half, acc):
             w_cols = slice(tp * CHUNK, (tp + 1) * CHUNK)
-            for s in range(2):
-                cols = slice(q * CHUNK + s * P, q * CHUNK + (s + 1) * P)
-                for b in range(2):
-                    k = 2 * half + b
+            for b in range(2):
+                k = 2 * half + b
+                for s in range(2):
+                    cols = slice(q * CHUNK + s * P, q * CHUNK + (s + 1) * P)
                     nc.tensor.matmul_mx(
                         out=acc[:, s, :],
                         lhsT=picked[k][:, cols].bitcast(FP8X4),
                         lhsT_scale=picked_sc[4 * k :, cols],
                         rhs=w_codes[g, b][:, w_cols].bitcast(FP8X4),
                         rhs_scale=w_scales[g, b][:, w_cols],
-                        start=(b == 0),
-                        stop=(b == 1),
+                        start=(b == 0 and s == 0),
+                        stop=(b == 1 and s == 1),
                     )
             return acc[:].rearrange("p s (m u) -> p s u m", u=2)
 
@@ -155,15 +159,16 @@ def tile_list_leakage_gap_audit_kernel(
 
         def gaps(g, tp, q, h_cols):
             n = 8 * g + 4 * tp + q
-            neg_mag = tile([P, 2, 2, P], F32, "neg_mag%d" % n, "neg_mag%d" % (n % 2))
-            abs_raw = tile([P, 2, 2, P], F32, "abs_raw%d" % n, "late%d" % (n - 3) if n in (3, 4) else "abs_raw%d" % (n % 2))
-            mag = bank(2 * n % 3, [P, 2, CHUNK], "mag%d" % n)
+            neg_mag = tile([P, 2, 2, P], F32, "neg_mag%d" % n, "neg_mag%d" % (n % 4))
+            abs_raw = tile([P, 2, 2, P], F32, "abs_raw%d" % n, "late%d" % (n - 3) if n in (3, 4) else "abs_raw%d" % (n % 3))
+            mag = bank((0, 2, 3, 7)[n] if n < 4 else 2 * (n % 2) + n // 2 % 2, [P, 2, CHUNK], "mag%d" % n)
             nc.scalar.activation(neg_mag[:], product(g, tp, q, 0, mag), COPY, scale=-1.0)
-            raw = bank((2 * n + 1) % 3, [P, 2, CHUNK], "raw%d" % n)
+            raw = bank((1, 1, 0, 2)[n] if n < 4 else 2 * (n % 2) + 1 - n // 2 % 2, [P, 2, CHUNK], "raw%d" % n)
             nc.scalar.activation(abs_raw[:], product(g, tp, q, 1, raw), ABS)
             for rows in ([(0, 1), (1, 2)] if n == 0 else [(0, 2)]):
+                k = len(turns)
                 turns.append(n)
-                turned = bank(3 + len(turns) % 5, [P, 2, CHUNK], "turned%d" % len(turns))
+                turned = bank(4 + (k % 3 if k < 5 else (k + 1) % 4), [P, 2, CHUNK], "turned%d" % k)
                 for u in range(*rows):
                     for s in range(2):
                         dst = turned[:, u, s * P : (s + 1) * P]
@@ -183,8 +188,9 @@ def tile_list_leakage_gap_audit_kernel(
             for u in range(2):
                 scatter(u, h_first[:, u, :], 0, q * CHUNK, (q + 1) * CHUNK)
 
-        load_w1(1, 0, 0, 4)
-        load_w1(1, 1, 0, 4)
+        for b in range(2):
+            for e in range(2):
+                load_w1(1, b, e)
         load_wg(1, 0, S)
         for quad in range(4):
             nc.sync.dma_start(
@@ -207,12 +213,16 @@ def tile_list_leakage_gap_audit_kernel(
             h = tile([P, 2, S], F32, "h%d%d" % (g, tp))
             for q in range(4):
                 gaps(g, tp, q, h[:, :, q * CHUNK : (q + 1) * CHUNK])
-                if (g, tp, q) == (0, 1, 0):
-                    quantise_w1(1, 1)
             for u in range(2):
                 scatter(u, h[:, u, :], tp, 0, S)
 
-        put_rows(0, 1)
+        for q in range(4):
+            h_second = tile([P, 2, CHUNK], F32, "h_second%d" % q)
+            gaps(0, 1, q, h_second[:])
+            if q == 0:
+                quantise_w1(1, 1)
+            for u in range(2):
+                scatter(u, h_second[:, u, :], 1, q * CHUNK, (q + 1) * CHUNK)
         for u in range(2):
             fetch(x0[:, 2 + u, :], u, 0, M)
 
@@ -222,7 +232,7 @@ def tile_list_leakage_gap_audit_kernel(
             wo_sc_raw[:].rearrange("p a (c t) -> p a c t", t=PACK),
         )
 
-        z_codes = [tile([P, M], U32, "z_codes%d" % g) for g in range(2)]
+        z_codes = {}
         z_scales = [tile([P, M], U8, "z_scales%d" % g) for g in range(2)]
 
         def threshold(grouped, x, g, m0, m1):
@@ -235,8 +245,12 @@ def tile_list_leakage_gap_audit_kernel(
             )
 
         def quantise_z(g, grouped, m0, m1):
+            c, c0 = divmod(m0, CHUNK)
+            if (g, c) not in z_codes:
+                tag = "picked%d" % (c - 1) if g == 0 and c > 0 else None
+                z_codes[g, c] = tile([P, CHUNK], U32, "z_codes%d_%d" % (g, c), tag)
             nc.vector.quantize_mx(
-                out=z_codes[g][:, m0:m1].bitcast(FP8X4),
+                out=z_codes[g, c][:, c0 : c0 + m1 - m0].bitcast(FP8X4),
                 scales=z_scales[g][:, m0:m1],
                 in_=grouped.rearrange("p m t -> p (m t)"),
             )
@@ -244,8 +258,12 @@ def tile_list_leakage_gap_audit_kernel(
         z0_grouped = [tile([P, M // 2, PACK], BF16, "z0_grouped%d" % i) for i in range(2)]
         for i in range(2):
             threshold(z0_grouped[i][:], x0[:, :, i * M // 2 : (i + 1) * M // 2], 0, i * M // 2, (i + 1) * M // 2)
-        for i in range(2):
-            quantise_z(0, z0_grouped[i][:], i * M // 2, (i + 1) * M // 2)
+
+        def quantise_z0(c):
+            half, c0 = divmod(c * CHUNK, M // 2)
+            quantise_z(0, z0_grouped[half][:, c0 : c0 + CHUNK, :], c * CHUNK, (c + 1) * CHUNK)
+
+        quantise_z0(0)
 
         chunks = M // CHUNK
         last = chunks - 1
@@ -265,24 +283,24 @@ def tile_list_leakage_gap_audit_kernel(
                     out=y_banks[i][:, t, :],
                     lhsT=wo_codes[:, a, 2 * P * t : 2 * P * (t + 1)].bitcast(FP4X4),
                     lhsT_scale=wo_sc[:, a, P * t : P * (t + 1)],
-                    rhs=z_codes[a][:, cols].bitcast(FP8X4),
+                    rhs=z_codes[a, i // 2][:, i % 2 * P : (i % 2 + 1) * P].bitcast(FP8X4),
                     rhs_scale=z_scales[a][:, cols],
                     start=(a == 0 and t == 0),
                     stop=(a == 1 and t == PACK - 1),
                 )
 
-        for i in range(M // P):
+        for i in range(2):
             output_pass(0, i)
 
-        y = [tile([P, PACK, M // 2], F32, "y%d" % i, "w_raw%d" % i) for i in range(2)]
+        y = [tile([P, PACK, CHUNK], F32, "y%d" % c, "w_raw%d" % c) for c in range(chunks)]
         y_codes = tile([P, M], U32, "y_codes")
         y_scales = tile([P, M], U8, "y_scales")
         out_rows = out_0.rearrange("(p t) m -> p t m", t=PACK)
         out_words = out_1[0].rearrange("p m t -> p (m t)").bitcast(I32)
 
         def y_cols(m0, m1):
-            half, c0 = divmod(m0, M // 2)
-            return y[half][:, :, c0 : c0 + m1 - m0]
+            c, c0 = divmod(m0, CHUNK)
+            return y[c][:, :, c0 : c0 + m1 - m0]
 
         def quantise_y(grouped, m0, m1):
             nc.vector.quantize_mx(
@@ -306,6 +324,8 @@ def tile_list_leakage_gap_audit_kernel(
             for s0, s1 in parts(c):
                 quantise_z(1, z1_grouped[c][:, s0:s1, :], c * CHUNK + s0, c * CHUNK + s1)
 
+        y_rounded = {}
+
         def finish(c):
             m0 = c * CHUNK
             y_grouped = tile([P, CHUNK, PACK], BF16, "y_grouped%d" % c, "y_grouped%d" % (c % 2))
@@ -323,20 +343,40 @@ def tile_list_leakage_gap_audit_kernel(
                     nc.scalar.copy(rounded, sums)
                     nc.scalar.copy(y_cols(i * P, (i + 1) * P), y_banks[i][:])
             if c != last:
-                quantise_y(y_grouped[:], m0, m0 + CHUNK)
                 nc.sync.dma_start(out_rows[:, :, m0 : m0 + CHUNK], y_cols(m0, m0 + CHUNK))
+            y_rounded[c] = y_grouped
+
+        def planes(c):
+            m0 = c * CHUNK
+            if c != last:
+                quantise_y(y_rounded[c][:], m0, m0 + CHUNK)
             nc.sync.dma_start(out_words[:, m0 : m0 + CHUNK], y_codes[:, m0 : m0 + CHUNK].bitcast(I32))
 
-        for c in range(chunks + 1):
-            if c < chunks:
-                fetch(x1[c][:, 2, :], 0, c * CHUNK, (c + 1) * CHUNK)
-            if c > 0:
-                threshold_z1(c - 1)
-            if c < chunks:
-                fetch(x1[c][:, 3, :], 1, c * CHUNK, (c + 1) * CHUNK)
-            if c > 0:
-                quantise_z1(c - 1)
-                finish(c - 1)
+        def fetch_last(c, u):
+            fetch(x1[c][:, 2 + u, :], u, c * CHUNK, (c + 1) * CHUNK)
+
+        fetch_last(0, 0)
+        fetch_last(0, 1)
+        for c in range(chunks):
+            if c == 0:
+                fetch_last(1, 0)
+            threshold_z1(c)
+            if c == 0:
+                fetch_last(1, 1)
+            elif c < last:
+                fetch_last(c + 1, 0)
+            quantise_z1(c)
+            if c == last:
+                planes(c - 1)
+            finish(c)
+            if c < last:
+                quantise_z0(c + 1)
+                for i in range(2):
+                    output_pass(0, 2 * c + 2 + i)
+            if 0 < c < last:
+                fetch_last(c + 1, 1)
+                planes(c - 1)
+        planes(last)
         for quad in range(4):
             queue = nc.sync if quad % 2 == 0 else nc.scalar
             queue.dma_start(

@@ -51,9 +51,6 @@ def tile_list_leakage_gap_audit_kernel(
         nc.gpsimd.memset(tab_sc[:].bitcast(I32), 0)
         nc.gpsimd.memset(wo_sc_raw[:].bitcast(I32), 0)
         make_identity(nc, ident[:])
-        warm = tile([P, 16], F32, "warm")
-        nc.vector.memset(warm[:, 0:1], 0.0)
-        nc.scalar.activation(warm[:, 8:9], warm[:, 0:1], ABS)
 
         tab = [tile([P, T], I32, "tab%d" % a) for a in range(4)]
         w_raw = {}
@@ -79,19 +76,26 @@ def tile_list_leakage_gap_audit_kernel(
         for e in range(2):
             load_w1(0, 0, e, 0, 2)
             load_w1(0, 0, e, 2, 4)
-        load_w1(0, 1, 0, 0, 2)
+        nc.sync.dma_start(wo_raw[:].bitcast(I32), wo_words.rearrange("a p c -> p a c").bitcast(I32))
         for quad in range(4):
             nc.sync.dma_start(
                 tab_sc[32 * quad : 32 * quad + 16, :].bitcast(I32),
                 tab_scales[:, 4 * quad : 4 * quad + 4, :].bitcast(I32),
             )
-        load_w1(0, 1, 0, 2, 4)
-        load_w1(0, 1, 1)
         for a in range(4):
             nc.sync.dma_start(tab[a][:], tab_words[a].rearrange("p t i -> p (t i)").bitcast(I32))
-        nc.sync.dma_start(wo_raw[:].bitcast(I32), wo_words.rearrange("a p c -> p a c").bitcast(I32))
+            if a == 0:
+                for e in range(2):
+                    load_w1(0, 1, e)
         load_wg(0, 0, CHUNK)
         load_wg(0, CHUNK, S)
+
+        wo_codes = tile([P, 2, 2 * N], U8, "wo_codes")
+        for a in range(2):
+            nc.vector.tensor_copy(
+                wo_codes[:, a, :].rearrange("p (t c b) -> p c t b", t=PACK, b=2),
+                wo_raw[:, a, :].rearrange("p (c t b) -> p c t b", t=PACK, b=2),
+            )
 
         w_codes = {}
         w_scales = {}
@@ -127,13 +131,6 @@ def tile_list_leakage_gap_audit_kernel(
         gather_tab(3, CHUNK, 2 * CHUNK)
         gather_tab(3, 2 * CHUNK, S)
 
-        wo_codes = tile([P, 2, 2 * N], U8, "wo_codes")
-        for a in range(2):
-            nc.vector.tensor_copy(
-                wo_codes[:, a, :].rearrange("p (t c b) -> p c t b", t=PACK, b=2),
-                wo_raw[:, a, :].rearrange("p (c t b) -> p c t b", t=PACK, b=2),
-            )
-
         pages = [tile([P, T2], F32, "page%d" % u) for u in range(2)]
         for u in range(2):
             nc.vector.memset(pages[u][:].bitcast(I32), 0)
@@ -161,14 +158,14 @@ def tile_list_leakage_gap_audit_kernel(
             n = 8 * g + 4 * tp + q
             neg_mag = tile([P, 2, 2, P], F32, "neg_mag%d" % n, "neg_mag%d" % (n % 4))
             abs_raw = tile([P, 2, 2, P], F32, "abs_raw%d" % n, "late%d" % (n - 3) if n in (3, 4) else "abs_raw%d" % (n % 3))
-            mag = bank((0, 2, 3, 7)[n] if n < 4 else 2 * (n % 2) + n // 2 % 2, [P, 2, CHUNK], "mag%d" % n)
+            mag = bank((0, 2, 3, 7)[n] if n < 4 else 2 * (n % 2), [P, 2, CHUNK], "mag%d" % n)
             nc.scalar.activation(neg_mag[:], product(g, tp, q, 0, mag), COPY, scale=-1.0)
-            raw = bank((1, 1, 0, 2)[n] if n < 4 else 2 * (n % 2) + 1 - n // 2 % 2, [P, 2, CHUNK], "raw%d" % n)
+            raw = bank(1 if n < 2 else 2 * (n % 2) if n < 4 else 2 * (n % 2) + 1, [P, 2, CHUNK], "raw%d" % n)
             nc.scalar.activation(abs_raw[:], product(g, tp, q, 1, raw), ABS)
             for rows in ([(0, 1), (1, 2)] if n == 0 else [(0, 2)]):
                 k = len(turns)
                 turns.append(n)
-                turned = bank(4 + (k % 3 if k < 5 else (k + 1) % 4), [P, 2, CHUNK], "turned%d" % k)
+                turned = bank((0, 4, 2, 3)[k] if k < 4 else 4 + (k - 3) % 4, [P, 2, CHUNK], "turned%d" % k)
                 for u in range(*rows):
                     for s in range(2):
                         dst = turned[:, u, s * P : (s + 1) * P]

@@ -55,6 +55,9 @@ def tile_list_leakage_gap_audit_kernel(
         tab = [tile([P, T], I32, "tab%d" % a) for a in range(4)]
         w_raw = {}
 
+        def load_tab(a, t0=0, t1=T):
+            nc.sync.dma_start(tab[a][:, t0:t1], tab_words[a].rearrange("p t i -> p (t i)").bitcast(I32)[:, t0:t1])
+
         def load_w1(g, b, e, i0=0, i1=PACK):
             if (g, b, e) not in w_raw:
                 w_raw[g, b, e] = tile([P, PACK, CHUNK], F32, "w_raw%d%d%d" % (g, b, e), "w_raw%d" % (2 * b + e))
@@ -62,58 +65,74 @@ def tile_list_leakage_gap_audit_kernel(
             rows = w1[b * K_PASS : (b + 1) * K_PASS, c0 : c0 + CHUNK].rearrange("(p i) c -> p i c", i=PACK)
             nc.sync.dma_start(w_raw[g, b, e][:, i0:i1, :], rows[:, i0:i1, :])
 
+        wg_plain = tile([P, S], F32, "wg_plain")
         wg = [tile([P, 2, S], F32, "wg%d" % tp) for tp in range(2)]
         wgs_rows = wgs.rearrange("(q t) j -> q t j", t=PACK)
-
-        def load_wg(tp, j0, j1):
-            for quad in (0, 2, 1, 3):
-                nc.sync.dma_start(wg[tp][32 * quad : 32 * quad + 32, :, j0:j1], wgs_rows[:, 2 * tp : 2 * tp + 2, j0:j1])
-
         wo_raw = tile([P, 2, 2 * N], U8, "wo_raw")
+
         nc.sync.dma_start(list1[:], offs)
+        load_tab(0, 0, T // 2)
+        load_tab(0, T // 2, T)
         nc.sync.dma_start(list2[:], offs2)
         nc.sync.dma_start(list3[:], offs3)
-        for e in range(2):
-            load_w1(0, 0, e, 0, 2)
-            load_w1(0, 0, e, 2, 4)
-        nc.sync.dma_start(wo_raw[:].bitcast(I32), wo_words.rearrange("a p c -> p a c").bitcast(I32))
+        nc.sync.dma_start(wg_plain[:, 0:CHUNK], wgs[:, 0:CHUNK])
+        load_w1(0, 0, 0, 0, 2)
+        load_w1(0, 0, 0, 2, 4)
         for quad in range(4):
             nc.sync.dma_start(
                 tab_sc[32 * quad : 32 * quad + 16, :].bitcast(I32),
                 tab_scales[:, 4 * quad : 4 * quad + 4, :].bitcast(I32),
             )
-        for a in range(4):
-            nc.sync.dma_start(tab[a][:], tab_words[a].rearrange("p t i -> p (t i)").bitcast(I32))
-            if a == 0:
-                for e in range(2):
-                    load_w1(0, 1, e)
-        load_wg(0, 0, CHUNK)
-        load_wg(0, CHUNK, S)
-
-        wo_codes = tile([P, 2, 2 * N], U8, "wo_codes")
-        for a in range(2):
-            nc.vector.tensor_copy(
-                wo_codes[:, a, :].rearrange("p (t c b) -> p c t b", t=PACK, b=2),
-                wo_raw[:, a, :].rearrange("p (c t b) -> p c t b", t=PACK, b=2),
+        load_tab(1)
+        load_w1(0, 1, 0)
+        load_tab(2)
+        load_tab(3)
+        nc.sync.dma_start(wo_raw[:].bitcast(I32), wo_words.rearrange("a p c -> p a c").bitcast(I32))
+        nc.sync.dma_start(wg_plain[:, CHUNK:S], wgs[:, CHUNK:S])
+        for quad in range(4):
+            nc.sync.dma_start(
+                wo_sc_raw[32 * quad : 32 * quad + 4, :, :].bitcast(I32),
+                wo_scales[:, 4 * quad : 4 * quad + 4, :].rearrange("a q c -> q a c").bitcast(I32),
             )
+        for b in range(2):
+            load_w1(0, b, 1)
+        for b in range(2):
+            for e in range(2):
+                load_w1(1, b, e)
+        for tp in range(2):
+            for quad in (0, 2, 1, 3):
+                nc.sync.dma_start(wg[tp][32 * quad : 32 * quad + 32, :, :], wgs_rows[:, 2 * tp : 2 * tp + 2, :])
 
         w_codes = {}
         w_scales = {}
 
-        def quantise_w1(g, b):
-            grouped = tile([P, 2, K_PASS // 2, PACK], BF16, "w_bf%d%d" % (g, b), "late%d" % b if g else None)
+        def quantise_words(key, grouped, width):
+            codes = tile([P, width], U32, "w_codes%d%d%d" % key)
+            scales = tile([P, width], U8, "w_scales%d%d%d" % key)
+            nc.vector.quantize_mx(out=codes[:].bitcast(FP8X4), scales=scales[:], in_=grouped)
+            return codes, scales
+
+        def quantise_w1_plain(b, tp):
+            grouped = tile([P, CHUNK, PACK], BF16, "w_bf0%d%d" % (b, tp))
+            nc.scalar.copy(
+                grouped[:].rearrange("p (m u) i -> p m i u", u=2),
+                w_raw[0, b, tp][:].rearrange("p i (m u) -> p m i u", u=2),
+            )
+            codes, scales = quantise_words((0, b, tp), grouped[:].rearrange("p c i -> p (c i)"), CHUNK)
+            w_codes[0, b, tp] = codes[:]
+            w_scales[0, b, tp] = scales[:]
+
+        def quantise_w1_dealt(b):
+            grouped = tile([P, 2, K_PASS // 2, PACK], BF16, "w_bf1%d" % b)
             for e in range(2):
                 nc.scalar.copy(
                     grouped[:, :, e * P : (e + 1) * P, :].rearrange("p h (m u) i -> p h m i u", u=2),
-                    w_raw[g, b, e][:].rearrange("p i (m h u) -> p h m i u", h=2, u=2),
+                    w_raw[1, b, e][:].rearrange("p i (m h u) -> p h m i u", h=2, u=2),
                 )
-            w_codes[g, b] = tile([P, K_PASS], U32, "w_codes%d%d" % (g, b))
-            w_scales[g, b] = tile([P, K_PASS], U8, "w_scales%d%d" % (g, b))
-            nc.vector.quantize_mx(
-                out=w_codes[g, b][:].bitcast(FP8X4),
-                scales=w_scales[g, b][:],
-                in_=grouped[:].rearrange("p h c i -> p (h c i)"),
-            )
+            codes, scales = quantise_words((1, b, 0), grouped[:].rearrange("p h c i -> p (h c i)"), K_PASS)
+            for tp in range(2):
+                w_codes[1, b, tp] = codes[:, tp * CHUNK : (tp + 1) * CHUNK]
+                w_scales[1, b, tp] = scales[:, tp * CHUNK : (tp + 1) * CHUNK]
 
         picked_sc = tile([P, S], U8, "picked_sc")
         picked = [tile([P, S], U32, "picked%d" % a) for a in range(4)]
@@ -121,22 +140,39 @@ def tile_list_leakage_gap_audit_kernel(
         def gather_tab(a, j0, j1):
             nc.vector.tensor_copy(picked[a][:, j0:j1], tab[a][:].bitcast(U32).indirect(entries(list1, j0, j1)))
 
-        quantise_w1(0, 0)
-        nc.vector.tensor_copy(picked_sc[:], tab_sc[:].indirect(list1[:]))
-        gather_tab(0, 0, S)
-        quantise_w1(0, 1)
-        for a in range(1, 3):
-            gather_tab(a, 0, S)
-        gather_tab(3, 0, CHUNK)
-        gather_tab(3, CHUNK, 2 * CHUNK)
-        gather_tab(3, 2 * CHUNK, S)
-
         pages = [tile([P, T2], F32, "page%d" % u) for u in range(2)]
         for u in range(2):
             nc.vector.memset(pages[u][:].bitcast(I32), 0)
 
+        gather_tab(0, 0, S)
+        quantise_w1_plain(0, 0)
+        nc.vector.tensor_copy(picked_sc[:], tab_sc[:].indirect(list1[:]))
+        gather_tab(1, 0, S)
+        quantise_w1_plain(1, 0)
+        gather_tab(2, 0, S)
+        gather_tab(3, 0, CHUNK)
+        gather_tab(3, CHUNK, 2 * CHUNK)
+        gather_tab(3, 2 * CHUNK, S)
+
+        wo_codes = tile([P, 2, 2 * N], U8, "wo_codes")
+        nc.vector.tensor_copy(
+            wo_codes[:].bitcast(U16).rearrange("p a (t c) -> p a c t", t=PACK),
+            wo_raw[:].bitcast(U16).rearrange("p a (c t) -> p a c t", t=PACK),
+        )
+        wo_sc = tile([P, 2, N], U8, "wo_sc")
+        nc.vector.tensor_copy(
+            wo_sc[:].rearrange("p a (t c) -> p a c t", t=PACK),
+            wo_sc_raw[:].rearrange("p a (c t) -> p a c t", t=PACK),
+        )
+
+        thr_rows = thr.rearrange("(a p t) m -> a p t m", p=P, t=PACK)
+        thr_sb = {}
+        for g in range(2):
+            for i in range(2):
+                thr_sb[g, i] = tile([P, PACK, M // 2], F32, "thr%d_%d" % (g, i), "tab%d" % (2 * g + i))
+                nc.sync.dma_start(thr_sb[g, i][:], thr_rows[g][:, :, i * M // 2 : (i + 1) * M // 2])
+
         def product(g, tp, q, half, acc):
-            w_cols = slice(tp * CHUNK, (tp + 1) * CHUNK)
             for b in range(2):
                 k = 2 * half + b
                 for s in range(2):
@@ -145,11 +181,13 @@ def tile_list_leakage_gap_audit_kernel(
                         out=acc[:, s, :],
                         lhsT=picked[k][:, cols].bitcast(FP8X4),
                         lhsT_scale=picked_sc[4 * k :, cols],
-                        rhs=w_codes[g, b][:, w_cols].bitcast(FP8X4),
-                        rhs_scale=w_scales[g, b][:, w_cols],
+                        rhs=w_codes[g, b, tp].bitcast(FP8X4),
+                        rhs_scale=w_scales[g, b, tp],
                         start=(b == 0 and s == 0),
                         stop=(b == 1 and s == 1),
                     )
+            if g == 0:
+                return acc[:].rearrange("p s (u m) -> p s u m", u=2)
             return acc[:].rearrange("p s (m u) -> p s u m", u=2)
 
         turns = []
@@ -157,15 +195,15 @@ def tile_list_leakage_gap_audit_kernel(
         def gaps(g, tp, q, h_cols):
             n = 8 * g + 4 * tp + q
             neg_mag = tile([P, 2, 2, P], F32, "neg_mag%d" % n, "neg_mag%d" % (n % 4))
-            abs_raw = tile([P, 2, 2, P], F32, "abs_raw%d" % n, "late%d" % (n - 3) if n in (3, 4) else "abs_raw%d" % (n % 3))
-            mag = bank((0, 2, 3, 7)[n] if n < 4 else 2 * (n % 2), [P, 2, CHUNK], "mag%d" % n)
+            abs_raw = tile([P, 2, 2, P], F32, "abs_raw%d" % n, "abs_raw%d" % (n % 3))
+            mag = bank(n if n < 4 else 5 if n in (4, 8) else 2 * (n % 2), [P, 2, CHUNK], "mag%d" % n)
             nc.scalar.activation(neg_mag[:], product(g, tp, q, 0, mag), COPY, scale=-1.0)
-            raw = bank(1 if n < 2 else 2 * (n % 2) if n < 4 else 2 * (n % 2) + 1, [P, 2, CHUNK], "raw%d" % n)
+            raw = bank(4 + n % 2 if n < 4 or n == 7 else 2 * (n % 2) + 1, [P, 2, CHUNK], "raw%d" % n)
             nc.scalar.activation(abs_raw[:], product(g, tp, q, 1, raw), ABS)
             for rows in ([(0, 1), (1, 2)] if n == 0 else [(0, 2)]):
                 k = len(turns)
                 turns.append(n)
-                turned = bank((0, 4, 2, 3)[k] if k < 4 else 4 + (k - 3) % 4, [P, 2, CHUNK], "turned%d" % k)
+                turned = bank(6 + k % 2, [P, 2, CHUNK], "turned%d" % k)
                 for u in range(*rows):
                     for s in range(2):
                         dst = turned[:, u, s * P : (s + 1) * P]
@@ -173,64 +211,50 @@ def tile_list_leakage_gap_audit_kernel(
                         nc.tensor.matmul(dst, abs_raw[:, s, u, :], ident[:], start=False, stop=True, is_transpose=True)
                 nc.scalar.activation(h_cols[:, rows[0] : rows[1], :], turned[:, rows[0] : rows[1], :], COPY, scale=-1.0)
 
-        def scatter(u, h_row, tp, j0, j1):
-            nc.vector.tensor_tensor(pages[u][:].indirect(entries(list2, j0, j1)), h_row, wg[tp][:, u, j0:j1], MULT)
+        def scatter(u, h_row, weights, j0, j1):
+            nc.vector.tensor_tensor(pages[u][:].indirect(entries(list2, j0, j1)), h_row, weights, MULT)
 
         def fetch(dst, u, m0, m1):
             nc.vector.tensor_copy(dst, pages[u][:].indirect(entries(list3, m0, m1)))
 
-        for q in range(4):
-            h_first = tile([P, 2, CHUNK], F32, "h_first%d" % q)
-            gaps(0, 0, q, h_first[:])
-            for u in range(2):
-                scatter(u, h_first[:, u, :], 0, q * CHUNK, (q + 1) * CHUNK)
-
-        for b in range(2):
-            for e in range(2):
-                load_w1(1, b, e)
-        load_wg(1, 0, S)
-        for quad in range(4):
-            nc.sync.dma_start(
-                wo_sc_raw[32 * quad : 32 * quad + 4, :, :].bitcast(I32),
-                wo_scales[:, 4 * quad : 4 * quad + 4, :].rearrange("a q c -> q a c").bitcast(I32),
-            )
-        thr_rows = thr.rearrange("(a p t) m -> a p t m", p=P, t=PACK)
-        thr_sb = {}
-        for g in range(2):
-            for i in range(2):
-                thr_sb[g, i] = tile([P, PACK, M // 2], F32, "thr%d_%d" % (g, i), "tab%d" % (2 * g + i))
-                nc.sync.dma_start(thr_sb[g, i][:], thr_rows[g][:, :, i * M // 2 : (i + 1) * M // 2])
-
         x0 = tile([P, PACK, M], F32, "x0")
-        for u in range(2):
-            fetch(x0[:, u, :], u, 0, M)
-        quantise_w1(1, 0)
+
+        def plain_pair(tp):
+            h = tile([P, 2, S], F32, "h0%d" % tp)
+            for q in range(4):
+                cols = slice(q * CHUNK, (q + 1) * CHUNK)
+                gaps(0, tp, q, h[:, :, cols])
+                for u in range(2):
+                    scatter(u, h[:, u, cols], wg_plain[:, cols], q * CHUNK, (q + 1) * CHUNK)
+                if q == 0:
+                    if tp == 0:
+                        quantise_w1_plain(0, 1)
+                        quantise_w1_plain(1, 1)
+                    else:
+                        quantise_w1_dealt(0)
+                        quantise_w1_dealt(1)
+            x_plain = tile([P, 2, M], F32, "x_plain%d" % tp, "h0%d" % tp)
+            for u in range(2):
+                fetch(x_plain[:, u, :], u, 0, M)
+                c = 2 * tp + u
+                for t in range(PACK):
+                    nc.sync.dma_start(x0[32 * c : 32 * c + 32, t, :], x_plain[t:P:PACK, u, :])
+
+        plain_pair(0)
+        plain_pair(1)
 
         def put_rows(g, tp):
             h = tile([P, 2, S], F32, "h%d%d" % (g, tp))
             for q in range(4):
                 gaps(g, tp, q, h[:, :, q * CHUNK : (q + 1) * CHUNK])
             for u in range(2):
-                scatter(u, h[:, u, :], tp, 0, S)
-
-        for q in range(4):
-            h_second = tile([P, 2, CHUNK], F32, "h_second%d" % q)
-            gaps(0, 1, q, h_second[:])
-            if q == 0:
-                quantise_w1(1, 1)
-            for u in range(2):
-                scatter(u, h_second[:, u, :], 1, q * CHUNK, (q + 1) * CHUNK)
-        for u in range(2):
-            fetch(x0[:, 2 + u, :], u, 0, M)
-
-        wo_sc = tile([P, 2, N], U8, "wo_sc")
-        nc.vector.tensor_copy(
-            wo_sc[:].rearrange("p a (t c) -> p a c t", t=PACK),
-            wo_sc_raw[:].rearrange("p a (c t) -> p a c t", t=PACK),
-        )
+                scatter(u, h[:, u, :], wg[tp][:, u, :], 0, S)
 
         z_codes = {}
         z_scales = [tile([P, M], U8, "z_scales%d" % g) for g in range(2)]
+
+        def x1_tag(c):
+            return "picked%d" % c if c else "x0"
 
         def threshold(grouped, x, g, m0, m1):
             half, c0 = divmod(m0, M // 2)
@@ -244,7 +268,7 @@ def tile_list_leakage_gap_audit_kernel(
         def quantise_z(g, grouped, m0, m1):
             c, c0 = divmod(m0, CHUNK)
             if (g, c) not in z_codes:
-                tag = "picked%d" % (c - 1) if g == 0 and c > 0 else None
+                tag = x1_tag(c - 1) if g == 0 and c > 0 else None
                 z_codes[g, c] = tile([P, CHUNK], U32, "z_codes%d_%d" % (g, c), tag)
             nc.vector.quantize_mx(
                 out=z_codes[g, c][:, c0 : c0 + m1 - m0].bitcast(FP8X4),
@@ -252,20 +276,19 @@ def tile_list_leakage_gap_audit_kernel(
                 in_=grouped.rearrange("p m t -> p (m t)"),
             )
 
-        z0_grouped = [tile([P, M // 2, PACK], BF16, "z0_grouped%d" % i) for i in range(2)]
-        for i in range(2):
-            threshold(z0_grouped[i][:], x0[:, :, i * M // 2 : (i + 1) * M // 2], 0, i * M // 2, (i + 1) * M // 2)
-
-        def quantise_z0(c):
-            half, c0 = divmod(c * CHUNK, M // 2)
-            quantise_z(0, z0_grouped[half][:, c0 : c0 + CHUNK, :], c * CHUNK, (c + 1) * CHUNK)
-
-        quantise_z0(0)
-
         chunks = M // CHUNK
         last = chunks - 1
         put_rows(1, 0)
-        x1 = [tile([P, PACK, CHUNK], F32, "x1_%d" % c, "picked%d" % c) for c in range(chunks)]
+        z0_grouped = tile([P, M, PACK], BF16, "z0_grouped", "h10")
+        for i in range(2):
+            cols = slice(i * M // 2, (i + 1) * M // 2)
+            threshold(z0_grouped[:, cols, :], x0[:, :, cols], 0, i * M // 2, (i + 1) * M // 2)
+
+        def quantise_z0(c):
+            quantise_z(0, z0_grouped[:, c * CHUNK : (c + 1) * CHUNK, :], c * CHUNK, (c + 1) * CHUNK)
+
+        quantise_z0(0)
+        x1 = [tile([P, PACK, CHUNK], F32, "x1_%d" % c, x1_tag(c)) for c in range(chunks)]
         for c in range(chunks):
             for u in range(2):
                 fetch(x1[c][:, u, :], u, c * CHUNK, (c + 1) * CHUNK)

@@ -159,6 +159,7 @@ def tile_list_leakage_gap_audit_kernel(
             wo_codes[:].bitcast(U16).rearrange("p a (t c) -> p a c t", t=PACK),
             wo_raw[:].bitcast(U16).rearrange("p a (c t) -> p a c t", t=PACK),
         )
+
         wo_sc = tile([P, 2, N], U8, "wo_sc")
         nc.vector.tensor_copy(
             wo_sc[:].rearrange("p a (t c) -> p a c t", t=PACK),
@@ -167,10 +168,13 @@ def tile_list_leakage_gap_audit_kernel(
 
         thr_rows = thr.rearrange("(a p t) m -> a p t m", p=P, t=PACK)
         thr_sb = {}
+        thr_width = (M // 2, CHUNK)
+        thr_tags = (("tab0", "tab1"), ("tab2", "tab3", "thr1_2", "thr1_3"))
         for g in range(2):
-            for i in range(2):
-                thr_sb[g, i] = tile([P, PACK, M // 2], F32, "thr%d_%d" % (g, i), "tab%d" % (2 * g + i))
-                nc.sync.dma_start(thr_sb[g, i][:], thr_rows[g][:, :, i * M // 2 : (i + 1) * M // 2])
+            width = thr_width[g]
+            for i in range(M // width):
+                thr_sb[g, i] = tile([P, PACK, width], F32, "thr%d_%d" % (g, i), thr_tags[g][i])
+                nc.sync.dma_start(thr_sb[g, i][:], thr_rows[g][:, :, i * width : (i + 1) * width])
 
         def product(g, tp, q, half, acc):
             for b in range(2):
@@ -253,11 +257,8 @@ def tile_list_leakage_gap_audit_kernel(
         z_codes = {}
         z_scales = [tile([P, M], U8, "z_scales%d" % g) for g in range(2)]
 
-        def x1_tag(c):
-            return "picked%d" % c if c else "x0"
-
         def threshold(grouped, x, g, m0, m1):
-            half, c0 = divmod(m0, M // 2)
+            half, c0 = divmod(m0, thr_width[g])
             nc.vector.tensor_tensor(
                 grouped.rearrange("p (c u) t -> p c t u", u=2),
                 x.rearrange("p t (c u) -> p c t u", u=2),
@@ -268,7 +269,7 @@ def tile_list_leakage_gap_audit_kernel(
         def quantise_z(g, grouped, m0, m1):
             c, c0 = divmod(m0, CHUNK)
             if (g, c) not in z_codes:
-                tag = x1_tag(c - 1) if g == 0 and c > 0 else None
+                tag = thr_tags[1][c - 1] if g == 0 and c > 0 else None
                 z_codes[g, c] = tile([P, CHUNK], U32, "z_codes%d_%d" % (g, c), tag)
             nc.vector.quantize_mx(
                 out=z_codes[g, c][:, c0 : c0 + m1 - m0].bitcast(FP8X4),
@@ -288,7 +289,8 @@ def tile_list_leakage_gap_audit_kernel(
             quantise_z(0, z0_grouped[:, c * CHUNK : (c + 1) * CHUNK, :], c * CHUNK, (c + 1) * CHUNK)
 
         quantise_z0(0)
-        x1 = [tile([P, PACK, CHUNK], F32, "x1_%d" % c, x1_tag(c)) for c in range(chunks)]
+        x1_rows = [tile([P, PACK + 2, CHUNK], F32, "x1_rows%d" % e, None if e else "x0") for e in range(2)]
+        x1 = [x1_rows[c % 2][:, 2 - c // 2 * 2 : PACK + 2 - c // 2 * 2, :] for c in range(chunks)]
         for c in range(chunks):
             for u in range(2):
                 fetch(x1[c][:, u, :], u, c * CHUNK, (c + 1) * CHUNK)
@@ -349,20 +351,24 @@ def tile_list_leakage_gap_audit_kernel(
         def finish(c):
             m0 = c * CHUNK
             y_grouped = tile([P, CHUNK, PACK], BF16, "y_grouped%d" % c, "y_grouped%d" % (c % 2))
-            for s0 in range(0, CHUNK, P):
-                i = (m0 + s0) // P
+            banks = [(m0 // P + k, y_grouped[:, k * P : (k + 1) * P, :]) for k in range(CHUNK // P)]
+            for i, rounded in banks:
                 output_pass(1, i)
-                rounded = y_grouped[:, s0 : s0 + P, :]
-                sums = y_banks[i][:].rearrange("p t m -> p m t")
-                if c == last:
-                    nc.vector.tensor_copy(rounded, sums)
-                    nc.scalar.copy(y_cols(i * P, (i + 1) * P), y_banks[i][:])
+            if c == last:
+                for i, rounded in banks:
+                    values = y_cols(i * P, (i + 1) * P)
+                    nc.scalar.copy(values, y_banks[i][:])
+                    nc.sync.dma_start(out_rows[:, :, i * P : (i + 1) * P], values)
+                    nc.vector.tensor_copy(
+                        rounded.rearrange("p (m u) t -> p m t u", u=2), values.rearrange("p t (m u) -> p m t u", u=2)
+                    )
+                for i, rounded in banks:
                     quantise_y(rounded, i * P, (i + 1) * P)
-                    nc.sync.dma_start(out_rows[:, :, i * P : (i + 1) * P], y_cols(i * P, (i + 1) * P))
-                else:
-                    nc.scalar.copy(rounded, sums)
+            else:
+                for i, rounded in banks:
+                    nc.scalar.copy(rounded, y_banks[i][:].rearrange("p t m -> p m t"))
+                for i, rounded in banks:
                     nc.scalar.copy(y_cols(i * P, (i + 1) * P), y_banks[i][:])
-            if c != last:
                 nc.sync.dma_start(out_rows[:, :, m0 : m0 + CHUNK], y_cols(m0, m0 + CHUNK))
             y_rounded[c] = y_grouped
 

@@ -168,13 +168,11 @@ def tile_list_leakage_gap_audit_kernel(
 
         thr_rows = thr.rearrange("(a p t) m -> a p t m", p=P, t=PACK)
         thr_sb = {}
-        thr_width = (M // 2, CHUNK)
-        thr_tags = (("tab0", "tab1"), ("tab2", "tab3", "thr1_2", "thr1_3"))
+        thr_tags = (("tab0", "tab1", "thr0_2", "thr0_3"), ("tab2", "tab3", "thr1_2", "thr1_3"))
         for g in range(2):
-            width = thr_width[g]
-            for i in range(M // width):
-                thr_sb[g, i] = tile([P, PACK, width], F32, "thr%d_%d" % (g, i), thr_tags[g][i])
-                nc.sync.dma_start(thr_sb[g, i][:], thr_rows[g][:, :, i * width : (i + 1) * width])
+            for c in range(M // CHUNK):
+                thr_sb[g, c] = tile([P, PACK, CHUNK], F32, "thr%d_%d" % (g, c), thr_tags[g][c])
+                nc.sync.dma_start(thr_sb[g, c][:], thr_rows[g][:, :, c * CHUNK : (c + 1) * CHUNK])
 
         def product(g, tp, q, half, acc):
             for b in range(2):
@@ -258,19 +256,18 @@ def tile_list_leakage_gap_audit_kernel(
         z_scales = [tile([P, M], U8, "z_scales%d" % g) for g in range(2)]
 
         def threshold(grouped, x, g, m0, m1):
-            half, c0 = divmod(m0, thr_width[g])
+            c, c0 = divmod(m0, CHUNK)
             nc.vector.tensor_tensor(
                 grouped.rearrange("p (c u) t -> p c t u", u=2),
                 x.rearrange("p t (c u) -> p c t u", u=2),
-                thr_sb[g, half][:, :, c0 : c0 + m1 - m0].rearrange("p t (c u) -> p c t u", u=2),
+                thr_sb[g, c][:, :, c0 : c0 + m1 - m0].rearrange("p t (c u) -> p c t u", u=2),
                 MAX,
             )
 
         def quantise_z(g, grouped, m0, m1):
             c, c0 = divmod(m0, CHUNK)
             if (g, c) not in z_codes:
-                tag = thr_tags[1][c - 1] if g == 0 and c > 0 else None
-                z_codes[g, c] = tile([P, CHUNK], U32, "z_codes%d_%d" % (g, c), tag)
+                z_codes[g, c] = tile([P, CHUNK], U32, "z_codes%d_%d" % (g, c), None if g else "picked%d" % c)
             nc.vector.quantize_mx(
                 out=z_codes[g, c][:, c0 : c0 + m1 - m0].bitcast(FP8X4),
                 scales=z_scales[g][:, m0:m1],
@@ -280,38 +277,57 @@ def tile_list_leakage_gap_audit_kernel(
         chunks = M // CHUNK
         last = chunks - 1
         put_rows(1, 0)
-        z0_grouped = tile([P, M, PACK], BF16, "z0_grouped", "h10")
-        for i in range(2):
-            cols = slice(i * M // 2, (i + 1) * M // 2)
-            threshold(z0_grouped[:, cols, :], x0[:, :, cols], 0, i * M // 2, (i + 1) * M // 2)
+        z0_grouped = {}
+
+        z0_early = tile([P, 2, CHUNK, PACK], BF16, "z0_early", "h10")
+
+        def threshold_z0(c):
+            if c < 2:
+                z0_grouped[c] = z0_early[:, c]
+            else:
+                z0_grouped[c] = tile([P, CHUNK, PACK], BF16, "z0_grouped%d" % c, thr_tags[1][c - 2])[:]
+            threshold(z0_grouped[c], x0[:, :, c * CHUNK : (c + 1) * CHUNK], 0, c * CHUNK, (c + 1) * CHUNK)
 
         def quantise_z0(c):
-            quantise_z(0, z0_grouped[:, c * CHUNK : (c + 1) * CHUNK, :], c * CHUNK, (c + 1) * CHUNK)
+            quantise_z(0, z0_grouped[c], c * CHUNK, (c + 1) * CHUNK)
 
-        quantise_z0(0)
-        x1_rows = [tile([P, PACK + 2, CHUNK], F32, "x1_rows%d" % e, None if e else "x0") for e in range(2)]
-        x1 = [x1_rows[c % 2][:, 2 - c // 2 * 2 : PACK + 2 - c // 2 * 2, :] for c in range(chunks)]
+        threshold_z0(0)
+        threshold_z0(1)
+        x1_rows = tile([P, 2 * PACK, CHUNK], F32, "x1_rows", thr_tags[0][1])
+        x1_second = tile([P, PACK, CHUNK], F32, "x1_second", "wg_plain")
+        x1 = [x1_rows[:, 4:8, :], x1_second[:], x1_rows[:, 2:6, :], x1_rows[:, 0:4, :]]
         for c in range(chunks):
             for u in range(2):
                 fetch(x1[c][:, u, :], u, c * CHUNK, (c + 1) * CHUNK)
+        quantise_z0(0)
+        quantise_z0(1)
         put_rows(1, 1)
 
-        y_banks = [bank(i, [P, PACK, P], "y%d" % i) for i in range(M // P)]
+        y_banks = {}
+
+        def y_groups(i):
+            return [(i, 0, 2), (0, 2, PACK)] if i == M // P - 1 else [(i, 0, PACK)]
 
         def output_pass(a, i):
+            for index, t0, t1 in y_groups(i):
+                if a == 0:
+                    y_banks[i, t0] = bank(index, [P, t1 - t0, P], "y%d_%d" % (i, t0))
+                output_group(a, i, t0, t1)
+
+        def output_group(a, i, t0, t1):
             cols = slice(i * P, (i + 1) * P)
-            for t in range(PACK):
+            for t in range(t0, t1):
                 nc.tensor.matmul_mx(
-                    out=y_banks[i][:, t, :],
+                    out=y_banks[i, t0][:, t - t0, :],
                     lhsT=wo_codes[:, a, 2 * P * t : 2 * P * (t + 1)].bitcast(FP4X4),
                     lhsT_scale=wo_sc[:, a, P * t : P * (t + 1)],
                     rhs=z_codes[a, i // 2][:, i % 2 * P : (i % 2 + 1) * P].bitcast(FP8X4),
                     rhs_scale=z_scales[a][:, cols],
-                    start=(a == 0 and t == 0),
-                    stop=(a == 1 and t == PACK - 1),
+                    start=(a == 0 and t == t0),
+                    stop=(a == 1 and t == t1 - 1),
                 )
 
-        for i in range(2):
+        for i in range(4):
             output_pass(0, i)
 
         y = [tile([P, PACK, CHUNK], F32, "y%d" % c, "w_raw%d" % c) for c in range(chunks)]
@@ -357,7 +373,8 @@ def tile_list_leakage_gap_audit_kernel(
             if c == last:
                 for i, rounded in banks:
                     values = y_cols(i * P, (i + 1) * P)
-                    nc.scalar.copy(values, y_banks[i][:])
+                    for index, t0, t1 in y_groups(i):
+                        nc.scalar.copy(values[:, t0:t1, :], y_banks[i, t0][:])
                     nc.sync.dma_start(out_rows[:, :, i * P : (i + 1) * P], values)
                     nc.vector.tensor_copy(
                         rounded.rearrange("p (m u) t -> p m t u", u=2), values.rearrange("p t (m u) -> p m t u", u=2)
@@ -366,9 +383,9 @@ def tile_list_leakage_gap_audit_kernel(
                     quantise_y(rounded, i * P, (i + 1) * P)
             else:
                 for i, rounded in banks:
-                    nc.scalar.copy(rounded, y_banks[i][:].rearrange("p t m -> p m t"))
+                    nc.scalar.copy(rounded, y_banks[i, 0][:].rearrange("p t m -> p m t"))
                 for i, rounded in banks:
-                    nc.scalar.copy(y_cols(i * P, (i + 1) * P), y_banks[i][:])
+                    nc.scalar.copy(y_cols(i * P, (i + 1) * P), y_banks[i, 0][:])
                 nc.sync.dma_start(out_rows[:, :, m0 : m0 + CHUNK], y_cols(m0, m0 + CHUNK))
             y_rounded[c] = y_grouped
 
@@ -381,27 +398,34 @@ def tile_list_leakage_gap_audit_kernel(
         def fetch_last(c, u):
             fetch(x1[c][:, 2 + u, :], u, c * CHUNK, (c + 1) * CHUNK)
 
+        def first_pass(c):
+            quantise_z0(c)
+            for i in range(2):
+                output_pass(0, 2 * c + i)
+
         fetch_last(0, 0)
         fetch_last(0, 1)
-        for c in range(chunks):
-            if c == 0:
-                fetch_last(1, 0)
+        fetch_last(1, 0)
+        threshold_z1(0)
+        fetch_last(1, 1)
+        quantise_z1(0)
+        finish(0)
+        fetch_last(2, 0)
+        fetch_last(2, 1)
+        for c in range(1, last):
+            threshold_z0(c + 1)
             threshold_z1(c)
-            if c == 0:
-                fetch_last(1, 1)
-            elif c < last:
-                fetch_last(c + 1, 0)
+            first_pass(c + 1)
             quantise_z1(c)
-            if c == last:
-                planes(c - 1)
             finish(c)
-            if c < last:
-                quantise_z0(c + 1)
-                for i in range(2):
-                    output_pass(0, 2 * c + 2 + i)
-            if 0 < c < last:
-                fetch_last(c + 1, 1)
-                planes(c - 1)
+            if c + 1 == last:
+                fetch_last(last, 0)
+                fetch_last(last, 1)
+            planes(c - 1)
+        threshold_z1(last)
+        quantise_z1(last)
+        planes(last - 1)
+        finish(last)
         planes(last)
         for quad in range(4):
             queue = nc.sync if quad % 2 == 0 else nc.scalar

@@ -252,55 +252,51 @@ def tile_list_leakage_gap_audit_kernel(
             for u in range(2):
                 scatter(u, h[:, u, :], wg[tp][:, u, :], 0, S)
 
+        chunks = M // CHUNK
+        pieces = [(c * CHUNK, (c + 1) * CHUNK) for c in range(chunks - 1)] + [(M - CHUNK, M - P), (M - P, M)]
+        z_grouped = {}
         z_codes = {}
         z_scales = [tile([P, M], U8, "z_scales%d" % g) for g in range(2)]
+        z_tags = {(0, 0): "h10", (0, 1): "h01", (0, 2): thr_tags[1][1], (0, 3): thr_tags[1][2]}
 
-        def threshold(grouped, x, g, m0, m1):
-            c, c0 = divmod(m0, CHUNK)
+        def in_chunk(k):
+            c, s0 = divmod(pieces[k][0], CHUNK)
+            return c, slice(s0, s0 + pieces[k][1] - pieces[k][0])
+
+        def threshold(g, k):
+            c, cols = in_chunk(k)
+            if (g, c) not in z_grouped:
+                z_grouped[g, c] = tile([P, CHUNK, PACK], BF16, "z_grouped%d%d" % (g, c), z_tags.get((g, c)))
+            x = x1[c][:, :, cols] if g else x0[:, :, pieces[k][0] : pieces[k][1]]
             nc.vector.tensor_tensor(
-                grouped.rearrange("p (c u) t -> p c t u", u=2),
+                z_grouped[g, c][:, cols, :].rearrange("p (c u) t -> p c t u", u=2),
                 x.rearrange("p t (c u) -> p c t u", u=2),
-                thr_sb[g, c][:, :, c0 : c0 + m1 - m0].rearrange("p t (c u) -> p c t u", u=2),
+                thr_sb[g, c][:, :, cols].rearrange("p t (c u) -> p c t u", u=2),
                 MAX,
             )
 
-        def quantise_z(g, grouped, m0, m1):
-            c, c0 = divmod(m0, CHUNK)
+        def quantise_z(g, k):
+            c, cols = in_chunk(k)
             if (g, c) not in z_codes:
                 z_codes[g, c] = tile([P, CHUNK], U32, "z_codes%d_%d" % (g, c), None if g else "picked%d" % c)
             nc.vector.quantize_mx(
-                out=z_codes[g, c][:, c0 : c0 + m1 - m0].bitcast(FP8X4),
-                scales=z_scales[g][:, m0:m1],
-                in_=grouped.rearrange("p m t -> p (m t)"),
+                out=z_codes[g, c][:, cols].bitcast(FP8X4),
+                scales=z_scales[g][:, pieces[k][0] : pieces[k][1]],
+                in_=z_grouped[g, c][:, cols, :].rearrange("p m t -> p (m t)"),
             )
 
-        chunks = M // CHUNK
-        last = chunks - 1
         put_rows(1, 0)
-        z0_grouped = {}
-
-        z0_early = tile([P, 2, CHUNK, PACK], BF16, "z0_early", "h10")
-
-        def threshold_z0(c):
-            if c < 2:
-                z0_grouped[c] = z0_early[:, c]
-            else:
-                z0_grouped[c] = tile([P, CHUNK, PACK], BF16, "z0_grouped%d" % c, thr_tags[1][c - 2])[:]
-            threshold(z0_grouped[c], x0[:, :, c * CHUNK : (c + 1) * CHUNK], 0, c * CHUNK, (c + 1) * CHUNK)
-
-        def quantise_z0(c):
-            quantise_z(0, z0_grouped[c], c * CHUNK, (c + 1) * CHUNK)
-
-        threshold_z0(0)
-        threshold_z0(1)
+        x1 = []
+        threshold(0, 0)
+        threshold(0, 1)
         x1_rows = tile([P, 2 * PACK, CHUNK], F32, "x1_rows", thr_tags[0][1])
         x1_second = tile([P, PACK, CHUNK], F32, "x1_second", "wg_plain")
-        x1 = [x1_rows[:, 4:8, :], x1_second[:], x1_rows[:, 2:6, :], x1_rows[:, 0:4, :]]
+        x1.extend([x1_rows[:, 4:8, :], x1_second[:], x1_rows[:, 2:6, :], x1_rows[:, 0:4, :]])
         for c in range(chunks):
             for u in range(2):
                 fetch(x1[c][:, u, :], u, c * CHUNK, (c + 1) * CHUNK)
-        quantise_z0(0)
-        quantise_z0(1)
+        quantise_z(0, 0)
+        quantise_z(0, 1)
         put_rows(1, 1)
 
         y_banks = {}
@@ -308,125 +304,107 @@ def tile_list_leakage_gap_audit_kernel(
         def y_groups(i):
             return [(i, 0, 2), (0, 2, PACK)] if i == M // P - 1 else [(i, 0, PACK)]
 
-        def output_pass(a, i):
-            for index, t0, t1 in y_groups(i):
-                if a == 0:
-                    y_banks[i, t0] = bank(index, [P, t1 - t0, P], "y%d_%d" % (i, t0))
-                output_group(a, i, t0, t1)
+        def output_pass(a, k):
+            for i in range(pieces[k][0] // P, pieces[k][1] // P):
+                for index, t0, t1 in y_groups(i):
+                    if a == 0:
+                        y_banks[i, t0] = bank(index, [P, t1 - t0, P], "y%d_%d" % (i, t0))
+                    for t in range(t0, t1):
+                        nc.tensor.matmul_mx(
+                            out=y_banks[i, t0][:, t - t0, :],
+                            lhsT=wo_codes[:, a, 2 * P * t : 2 * P * (t + 1)].bitcast(FP4X4),
+                            lhsT_scale=wo_sc[:, a, P * t : P * (t + 1)],
+                            rhs=z_codes[a, i // 2][:, i % 2 * P : (i % 2 + 1) * P].bitcast(FP8X4),
+                            rhs_scale=z_scales[a][:, i * P : (i + 1) * P],
+                            start=(a == 0 and t == t0),
+                            stop=(a == 1 and t == t1 - 1),
+                        )
 
-        def output_group(a, i, t0, t1):
-            cols = slice(i * P, (i + 1) * P)
-            for t in range(t0, t1):
-                nc.tensor.matmul_mx(
-                    out=y_banks[i, t0][:, t - t0, :],
-                    lhsT=wo_codes[:, a, 2 * P * t : 2 * P * (t + 1)].bitcast(FP4X4),
-                    lhsT_scale=wo_sc[:, a, P * t : P * (t + 1)],
-                    rhs=z_codes[a, i // 2][:, i % 2 * P : (i % 2 + 1) * P].bitcast(FP8X4),
-                    rhs_scale=z_scales[a][:, cols],
-                    start=(a == 0 and t == t0),
-                    stop=(a == 1 and t == t1 - 1),
-                )
-
-        for i in range(4):
-            output_pass(0, i)
+        output_pass(0, 0)
+        output_pass(0, 1)
 
         y = [tile([P, PACK, CHUNK], F32, "y%d" % c, "w_raw%d" % c) for c in range(chunks)]
+        y_grouped = [tile([P, CHUNK, PACK], BF16, "y_grouped%d" % c, "neg_mag%d" % c) for c in range(chunks)]
         y_codes = tile([P, M], U32, "y_codes")
         y_scales = tile([P, M], U8, "y_scales")
         out_rows = out_0.rearrange("(p t) m -> p t m", t=PACK)
         out_words = out_1[0].rearrange("p m t -> p (m t)").bitcast(I32)
 
-        def y_cols(m0, m1):
-            c, c0 = divmod(m0, CHUNK)
-            return y[c][:, :, c0 : c0 + m1 - m0]
+        def first_pass(k):
+            quantise_z(0, k)
+            output_pass(0, k)
 
-        def quantise_y(grouped, m0, m1):
+        def second_pass(k):
+            quantise_z(1, k)
+            output_pass(1, k)
+            c, cols = in_chunk(k)
+            m0, m1 = pieces[k]
+            if m1 - m0 == CHUNK:
+                for s in range(2):
+                    sums = y_banks[2 * c + s, 0][:].rearrange("p t m -> p m t")
+                    nc.scalar.copy(y_grouped[c][:, s * P : (s + 1) * P, :], sums)
+                for s in range(2):
+                    nc.scalar.copy(y[c][:, :, s * P : (s + 1) * P], y_banks[2 * c + s, 0][:])
+                nc.sync.dma_start(out_rows[:, :, m0:m1], y[c][:])
+            else:
+                for index, t0, t1 in y_groups(m0 // P):
+                    nc.scalar.copy(y[c][:, t0:t1, cols], y_banks[m0 // P, t0][:])
+                nc.sync.dma_start(out_rows[:, :, m0:m1], y[c][:, :, cols])
+
+        def round_y(k):
+            c, cols = in_chunk(k)
+            nc.vector.tensor_copy(
+                y_grouped[c][:, cols, :].rearrange("p (m u) t -> p m t u", u=2),
+                y[c][:, :, cols].rearrange("p t (m u) -> p m t u", u=2),
+            )
+
+        words_from = {1: 0, 2: 2 * CHUNK, 4: 3 * CHUNK}
+
+        def planes(k):
+            c, cols = in_chunk(k)
+            m0, m1 = pieces[k]
             nc.vector.quantize_mx(
                 out=y_codes[:, m0:m1].bitcast(FP8X4),
                 scales=y_scales[:, m0:m1],
-                in_=grouped.rearrange("p m t -> p (m t)"),
+                in_=y_grouped[c][:, cols, :].rearrange("p m t -> p (m t)"),
             )
-
-        z1_grouped = {}
-
-        def parts(c):
-            step = P if c == last else CHUNK
-            return [(s0, s0 + step) for s0 in range(0, CHUNK, step)]
-
-        def threshold_z1(c):
-            z1_grouped[c] = tile([P, CHUNK, PACK], BF16, "z1_grouped%d" % c, "z1_grouped%d" % (c % 2))
-            for s0, s1 in parts(c):
-                threshold(z1_grouped[c][:, s0:s1, :], x1[c][:, :, s0:s1], 1, c * CHUNK + s0, c * CHUNK + s1)
-
-        def quantise_z1(c):
-            for s0, s1 in parts(c):
-                quantise_z(1, z1_grouped[c][:, s0:s1, :], c * CHUNK + s0, c * CHUNK + s1)
-
-        y_rounded = {}
-
-        def finish(c):
-            m0 = c * CHUNK
-            y_grouped = tile([P, CHUNK, PACK], BF16, "y_grouped%d" % c, "y_grouped%d" % (c % 2))
-            banks = [(m0 // P + k, y_grouped[:, k * P : (k + 1) * P, :]) for k in range(CHUNK // P)]
-            for i, rounded in banks:
-                output_pass(1, i)
-            if c == last:
-                for i, rounded in banks:
-                    values = y_cols(i * P, (i + 1) * P)
-                    for index, t0, t1 in y_groups(i):
-                        nc.scalar.copy(values[:, t0:t1, :], y_banks[i, t0][:])
-                    nc.sync.dma_start(out_rows[:, :, i * P : (i + 1) * P], values)
-                    nc.vector.tensor_copy(
-                        rounded.rearrange("p (m u) t -> p m t u", u=2), values.rearrange("p t (m u) -> p m t u", u=2)
-                    )
-                for i, rounded in banks:
-                    quantise_y(rounded, i * P, (i + 1) * P)
-            else:
-                for i, rounded in banks:
-                    nc.scalar.copy(rounded, y_banks[i, 0][:].rearrange("p t m -> p m t"))
-                for i, rounded in banks:
-                    nc.scalar.copy(y_cols(i * P, (i + 1) * P), y_banks[i, 0][:])
-                nc.sync.dma_start(out_rows[:, :, m0 : m0 + CHUNK], y_cols(m0, m0 + CHUNK))
-            y_rounded[c] = y_grouped
-
-        def planes(c):
-            m0 = c * CHUNK
-            if c != last:
-                quantise_y(y_rounded[c][:], m0, m0 + CHUNK)
-            nc.sync.dma_start(out_words[:, m0 : m0 + CHUNK], y_codes[:, m0 : m0 + CHUNK].bitcast(I32))
+            if k in words_from:
+                nc.sync.dma_start(out_words[:, words_from[k] : m1], y_codes[:, words_from[k] : m1].bitcast(I32))
 
         def fetch_last(c, u):
             fetch(x1[c][:, 2 + u, :], u, c * CHUNK, (c + 1) * CHUNK)
 
-        def first_pass(c):
-            quantise_z0(c)
-            for i in range(2):
-                output_pass(0, 2 * c + i)
-
         fetch_last(0, 0)
         fetch_last(0, 1)
         fetch_last(1, 0)
-        threshold_z1(0)
+        threshold(1, 0)
         fetch_last(1, 1)
-        quantise_z1(0)
-        finish(0)
+        second_pass(0)
+        threshold(1, 1)
         fetch_last(2, 0)
+        second_pass(1)
         fetch_last(2, 1)
-        for c in range(1, last):
-            threshold_z0(c + 1)
-            threshold_z1(c)
-            first_pass(c + 1)
-            quantise_z1(c)
-            finish(c)
-            if c + 1 == last:
-                fetch_last(last, 0)
-                fetch_last(last, 1)
-            planes(c - 1)
-        threshold_z1(last)
-        quantise_z1(last)
-        planes(last - 1)
-        finish(last)
-        planes(last)
+        threshold(0, 2)
+        threshold(1, 2)
+        first_pass(2)
+        second_pass(2)
+        fetch_last(3, 0)
+        fetch_last(3, 1)
+        threshold(0, 3)
+        threshold(1, 3)
+        first_pass(3)
+        planes(0)
+        second_pass(3)
+        threshold(0, 4)
+        planes(1)
+        first_pass(4)
+        threshold(1, 4)
+        planes(2)
+        second_pass(4)
+        round_y(3)
+        planes(3)
+        round_y(4)
+        planes(4)
         for quad in range(4):
             queue = nc.sync if quad % 2 == 0 else nc.scalar
             queue.dma_start(

@@ -71,11 +71,11 @@ def tile_list_leakage_gap_audit_kernel(
         wo_raw = tile([P, 2, 2 * N], U8, "wo_raw")
 
         nc.sync.dma_start(list1[:], offs)
-        load_tab(0, 0, T // 2)
+        load_tab(0, 0, T // 4)
+        load_tab(0, T // 4, T // 2)
         load_tab(0, T // 2, T)
         nc.sync.dma_start(list2[:], offs2)
         nc.sync.dma_start(list3[:], offs3)
-        nc.sync.dma_start(wg_plain[:, 0:CHUNK], wgs[:, 0:CHUNK])
         load_w1(0, 0, 0, 0, 2)
         load_w1(0, 0, 0, 2, 4)
         for quad in range(4):
@@ -87,6 +87,7 @@ def tile_list_leakage_gap_audit_kernel(
         load_w1(0, 1, 0)
         load_tab(2)
         load_tab(3)
+        nc.sync.dma_start(wg_plain[:, 0:CHUNK], wgs[:, 0:CHUNK])
         nc.sync.dma_start(wo_raw[:].bitcast(I32), wo_words.rearrange("a p c -> p a c").bitcast(I32))
         nc.sync.dma_start(wg_plain[:, CHUNK:S], wgs[:, CHUNK:S])
         for quad in range(4):
@@ -201,8 +202,9 @@ def tile_list_leakage_gap_audit_kernel(
             mag = bank(n if n < 4 else 5 if n in (4, 8) else 2 * (n % 2), [P, 2, CHUNK], "mag%d" % n)
             nc.scalar.activation(neg_mag[:], product(g, tp, q, 0, mag), COPY, scale=-1.0)
             raw = bank(4 + n % 2 if n < 4 or n == 7 else 2 * (n % 2) + 1, [P, 2, CHUNK], "raw%d" % n)
-            nc.scalar.activation(abs_raw[:], product(g, tp, q, 1, raw), ABS)
+            raw_sums = product(g, tp, q, 1, raw)
             for rows in ([(0, 1), (1, 2)] if n == 0 else [(0, 2)]):
+                nc.scalar.activation(abs_raw[:, :, rows[0] : rows[1], :], raw_sums[:, :, rows[0] : rows[1], :], ABS)
                 k = len(turns)
                 turns.append(n)
                 turned = bank(6 + k % 2, [P, 2, CHUNK], "turned%d" % k)
@@ -347,29 +349,34 @@ def tile_list_leakage_gap_audit_kernel(
                     nc.scalar.copy(y[c][:, :, s * P : (s + 1) * P], y_banks[2 * c + s, 0][:])
                 nc.sync.dma_start(out_rows[:, :, m0:m1], y[c][:])
             else:
-                for index, t0, t1 in y_groups(m0 // P):
-                    nc.scalar.copy(y[c][:, t0:t1, cols], y_banks[m0 // P, t0][:])
+                groups = y_groups(m0 // P)
+                for index, t0, t1 in groups:
+                    step = P // 2 if t0 else P
+                    for s0 in range(0, P, step):
+                        dst = y[c][:, t0:t1, cols.start + s0 : cols.start + s0 + step]
+                        nc.scalar.copy(dst, y_banks[m0 // P, t0][:, :, s0 : s0 + step])
                 nc.sync.dma_start(out_rows[:, :, m0:m1], y[c][:, :, cols])
 
-        def round_y(k):
-            c, cols = in_chunk(k)
+        def round_y(m0, m1):
+            c, s0 = divmod(m0, CHUNK)
+            cols = slice(s0, s0 + m1 - m0)
             nc.vector.tensor_copy(
                 y_grouped[c][:, cols, :].rearrange("p (m u) t -> p m t u", u=2),
                 y[c][:, :, cols].rearrange("p t (m u) -> p m t u", u=2),
             )
 
-        words_from = {1: 0, 2: 2 * CHUNK, 4: 3 * CHUNK}
+        words_from = {2 * CHUNK: 0, 3 * CHUNK: 2 * CHUNK, M: 3 * CHUNK}
 
-        def planes(k):
-            c, cols = in_chunk(k)
-            m0, m1 = pieces[k]
+        def planes(m0, m1):
+            c, s0 = divmod(m0, CHUNK)
+            cols = slice(s0, s0 + m1 - m0)
             nc.vector.quantize_mx(
                 out=y_codes[:, m0:m1].bitcast(FP8X4),
                 scales=y_scales[:, m0:m1],
                 in_=y_grouped[c][:, cols, :].rearrange("p m t -> p (m t)"),
             )
-            if k in words_from:
-                nc.sync.dma_start(out_words[:, words_from[k] : m1], y_codes[:, words_from[k] : m1].bitcast(I32))
+            if m1 in words_from:
+                nc.sync.dma_start(out_words[:, words_from[m1] : m1], y_codes[:, words_from[m1] : m1].bitcast(I32))
 
         def fetch_last(c, u):
             fetch(x1[c][:, 2 + u, :], u, c * CHUNK, (c + 1) * CHUNK)
@@ -393,18 +400,21 @@ def tile_list_leakage_gap_audit_kernel(
         threshold(0, 3)
         threshold(1, 3)
         first_pass(3)
-        planes(0)
+        planes(*pieces[0])
         second_pass(3)
         threshold(0, 4)
-        planes(1)
+        planes(*pieces[1])
         first_pass(4)
         threshold(1, 4)
-        planes(2)
+        planes(*pieces[2])
         second_pass(4)
-        round_y(3)
-        planes(3)
-        round_y(4)
-        planes(4)
+        round_y(*pieces[3])
+        planes(*pieces[3])
+        halves = [(M - P, M - P // 2), (M - P // 2, M)]
+        for half in halves:
+            round_y(*half)
+        for half in halves:
+            planes(*half)
         for quad in range(4):
             queue = nc.sync if quad % 2 == 0 else nc.scalar
             queue.dma_start(

@@ -237,7 +237,7 @@ def tile_list_leakage_gap_audit_kernel(
                     else:
                         quantise_w1_dealt(0)
                         quantise_w1_dealt(1)
-            x_plain = tile([P, 2, M], F32, "x_plain%d" % tp, "h0%d" % tp)
+            x_plain = tile([P, 2, M], F32, "x_plain%d" % tp, "h00" if tp else "h11")
             for u in range(2):
                 fetch(x_plain[:, u, :], u, 0, M)
                 c = 2 * tp + u
@@ -259,7 +259,7 @@ def tile_list_leakage_gap_audit_kernel(
         z_grouped = {}
         z_codes = {}
         z_scales = [tile([P, M], U8, "z_scales%d" % g) for g in range(2)]
-        z_tags = {(0, 0): "h10", (0, 1): "h01", (0, 2): thr_tags[1][1], (0, 3): thr_tags[1][2]}
+        z_tags = {(0, 0): "h10", (0, 1): "h00", (0, 2): thr_tags[1][1], (0, 3): thr_tags[1][2]}
 
         def in_chunk(k):
             c, s0 = divmod(pieces[k][0], CHUNK)

@@ -89,12 +89,12 @@ def tile_list_leakage_gap_audit_kernel(
         load_tab(3)
         nc.sync.dma_start(wg_plain[:, 0:CHUNK], wgs[:, 0:CHUNK])
         nc.sync.dma_start(wo_raw[:].bitcast(I32), wo_words.rearrange("a p c -> p a c").bitcast(I32))
-        nc.sync.dma_start(wg_plain[:, CHUNK:S], wgs[:, CHUNK:S])
         for quad in range(4):
             nc.sync.dma_start(
                 wo_sc_raw[32 * quad : 32 * quad + 4, :, :].bitcast(I32),
                 wo_scales[:, 4 * quad : 4 * quad + 4, :].rearrange("a q c -> q a c").bitcast(I32),
             )
+        nc.sync.dma_start(wg_plain[:, CHUNK:S], wgs[:, CHUNK:S])
         for b in range(2):
             load_w1(0, b, 1)
         for b in range(2):
@@ -169,11 +169,15 @@ def tile_list_leakage_gap_audit_kernel(
 
         thr_rows = thr.rearrange("(a p t) m -> a p t m", p=P, t=PACK)
         thr_sb = {}
+        x1_rows = tile([P, 10, CHUNK], F32, "x1_rows", "tab0")
         thr_tags = (("tab0", "tab1", "thr0_2", "thr0_3"), ("tab2", "tab3", "thr1_2", "thr1_3"))
         for g in range(2):
             for c in range(M // CHUNK):
-                thr_sb[g, c] = tile([P, PACK, CHUNK], F32, "thr%d_%d" % (g, c), thr_tags[g][c])
-                nc.sync.dma_start(thr_sb[g, c][:], thr_rows[g][:, :, c * CHUNK : (c + 1) * CHUNK])
+                if (g, c) == (0, 0):
+                    thr_sb[g, c] = x1_rows[:, 0:10:3, :]
+                else:
+                    thr_sb[g, c] = tile([P, PACK, CHUNK], F32, "thr%d_%d" % (g, c), thr_tags[g][c])[:]
+                nc.sync.dma_start(thr_sb[g, c], thr_rows[g][:, :, c * CHUNK : (c + 1) * CHUNK])
 
         def product(g, tp, q, half, acc):
             for b in range(2):
@@ -288,15 +292,15 @@ def tile_list_leakage_gap_audit_kernel(
             )
 
         put_rows(1, 0)
-        x1 = []
+        x1_second = tile([P, PACK, CHUNK], F32, "x1_second", "wg_plain")
+        x1 = [x1_rows[:, 4:8, :], x1_second[:], x1_rows[:, 2:6, :], x1_rows[:, 0:4, :]]
+        for c in range(chunks - 1):
+            fetch(x1[c][:, 0, :], 0, c * CHUNK, (c + 1) * CHUNK)
         threshold(0, 0)
         threshold(0, 1)
-        x1_rows = tile([P, 2 * PACK, CHUNK], F32, "x1_rows", thr_tags[0][1])
-        x1_second = tile([P, PACK, CHUNK], F32, "x1_second", "wg_plain")
-        x1.extend([x1_rows[:, 4:8, :], x1_second[:], x1_rows[:, 2:6, :], x1_rows[:, 0:4, :]])
+        fetch(x1[chunks - 1][:, 0, :], 0, M - CHUNK, M)
         for c in range(chunks):
-            for u in range(2):
-                fetch(x1[c][:, u, :], u, c * CHUNK, (c + 1) * CHUNK)
+            fetch(x1[c][:, 1, :], 1, c * CHUNK, (c + 1) * CHUNK)
         quantise_z(0, 0)
         quantise_z(0, 1)
         put_rows(1, 1)
@@ -365,7 +369,7 @@ def tile_list_leakage_gap_audit_kernel(
                 y[c][:, :, cols].rearrange("p t (m u) -> p m t u", u=2),
             )
 
-        words_from = {2 * CHUNK: 0, 3 * CHUNK: 2 * CHUNK, M: 3 * CHUNK}
+        words_from = {CHUNK: 0, 3 * CHUNK: CHUNK, M: 3 * CHUNK}
 
         def planes(m0, m1):
             c, s0 = divmod(m0, CHUNK)
@@ -387,25 +391,25 @@ def tile_list_leakage_gap_audit_kernel(
         threshold(1, 0)
         fetch_last(1, 1)
         second_pass(0)
-        threshold(1, 1)
         fetch_last(2, 0)
-        second_pass(1)
+        threshold(1, 1)
         fetch_last(2, 1)
+        second_pass(1)
         threshold(0, 2)
         threshold(1, 2)
         first_pass(2)
+        planes(*pieces[0])
         second_pass(2)
         fetch_last(3, 0)
         fetch_last(3, 1)
         threshold(0, 3)
         threshold(1, 3)
         first_pass(3)
-        planes(*pieces[0])
-        second_pass(3)
         threshold(0, 4)
-        planes(*pieces[1])
-        first_pass(4)
+        second_pass(3)
         threshold(1, 4)
+        first_pass(4)
+        planes(*pieces[1])
         planes(*pieces[2])
         second_pass(4)
         round_y(*pieces[3])

@@ -88,15 +88,15 @@ def tile_list_leakage_gap_audit_kernel(
         load_tab(2)
         load_tab(3)
         nc.sync.dma_start(wg_plain[:, 0:CHUNK], wgs[:, 0:CHUNK])
+        nc.sync.dma_start(wg_plain[:, CHUNK:S], wgs[:, CHUNK:S])
+        for b in range(2):
+            load_w1(0, b, 1)
         nc.sync.dma_start(wo_raw[:].bitcast(I32), wo_words.rearrange("a p c -> p a c").bitcast(I32))
         for quad in range(4):
             nc.sync.dma_start(
                 wo_sc_raw[32 * quad : 32 * quad + 4, :, :].bitcast(I32),
                 wo_scales[:, 4 * quad : 4 * quad + 4, :].rearrange("a q c -> q a c").bitcast(I32),
             )
-        nc.sync.dma_start(wg_plain[:, CHUNK:S], wgs[:, CHUNK:S])
-        for b in range(2):
-            load_w1(0, b, 1)
         for b in range(2):
             for e in range(2):
                 load_w1(1, b, e)
@@ -114,7 +114,7 @@ def tile_list_leakage_gap_audit_kernel(
             return codes, scales
 
         def quantise_w1_plain(b, tp):
-            grouped = tile([P, CHUNK, PACK], BF16, "w_bf0%d%d" % (b, tp))
+            grouped = tile([P, CHUNK, PACK], BF16, "w_bf0%d%d" % (b, tp), "neg_mag%d" % b if tp else None)
             nc.scalar.copy(
                 grouped[:].rearrange("p (m u) i -> p m i u", u=2),
                 w_raw[0, b, tp][:].rearrange("p i (m u) -> p m i u", u=2),
@@ -155,18 +155,6 @@ def tile_list_leakage_gap_audit_kernel(
         gather_tab(3, CHUNK, 2 * CHUNK)
         gather_tab(3, 2 * CHUNK, S)
 
-        wo_codes = tile([P, 2, 2 * N], U8, "wo_codes")
-        nc.vector.tensor_copy(
-            wo_codes[:].bitcast(U16).rearrange("p a (t c) -> p a c t", t=PACK),
-            wo_raw[:].bitcast(U16).rearrange("p a (c t) -> p a c t", t=PACK),
-        )
-
-        wo_sc = tile([P, 2, N], U8, "wo_sc")
-        nc.vector.tensor_copy(
-            wo_sc[:].rearrange("p a (t c) -> p a c t", t=PACK),
-            wo_sc_raw[:].rearrange("p a (c t) -> p a c t", t=PACK),
-        )
-
         thr_rows = thr.rearrange("(a p t) m -> a p t m", p=P, t=PACK)
         thr_sb = {}
         x1_rows = tile([P, 10, CHUNK], F32, "x1_rows", "tab0")
@@ -179,7 +167,8 @@ def tile_list_leakage_gap_audit_kernel(
                     thr_sb[g, c] = tile([P, PACK, CHUNK], F32, "thr%d_%d" % (g, c), thr_tags[g][c])[:]
                 nc.sync.dma_start(thr_sb[g, c], thr_rows[g][:, :, c * CHUNK : (c + 1) * CHUNK])
 
-        def product(g, tp, q, half, acc):
+        def product(g, tp, q, half, acc, rows=(0, 2)):
+            w_cols = slice(rows[0] * P, rows[1] * P)
             for b in range(2):
                 k = 2 * half + b
                 for s in range(2):
@@ -188,13 +177,13 @@ def tile_list_leakage_gap_audit_kernel(
                         out=acc[:, s, :],
                         lhsT=picked[k][:, cols].bitcast(FP8X4),
                         lhsT_scale=picked_sc[4 * k :, cols],
-                        rhs=w_codes[g, b, tp].bitcast(FP8X4),
-                        rhs_scale=w_scales[g, b, tp],
+                        rhs=w_codes[g, b, tp][:, w_cols].bitcast(FP8X4),
+                        rhs_scale=w_scales[g, b, tp][:, w_cols],
                         start=(b == 0 and s == 0),
                         stop=(b == 1 and s == 1),
                     )
             if g == 0:
-                return acc[:].rearrange("p s (u m) -> p s u m", u=2)
+                return acc[:].rearrange("p s (u m) -> p s u m", m=P)
             return acc[:].rearrange("p s (m u) -> p s u m", u=2)
 
         turns = []
@@ -203,20 +192,26 @@ def tile_list_leakage_gap_audit_kernel(
             n = 8 * g + 4 * tp + q
             neg_mag = tile([P, 2, 2, P], F32, "neg_mag%d" % n, "neg_mag%d" % (n % 4))
             abs_raw = tile([P, 2, 2, P], F32, "abs_raw%d" % n, "abs_raw%d" % (n % 3))
-            mag = bank(n if n < 4 else 5 if n in (4, 8) else 2 * (n % 2), [P, 2, CHUNK], "mag%d" % n)
+            mag = bank(n if n < 4 else 4 if n == 4 else 5 if n == 8 else 2 * (n % 2), [P, 2, CHUNK], "mag%d" % n)
             nc.scalar.activation(neg_mag[:], product(g, tp, q, 0, mag), COPY, scale=-1.0)
-            raw = bank(4 + n % 2 if n < 4 or n == 7 else 2 * (n % 2) + 1, [P, 2, CHUNK], "raw%d" % n)
-            raw_sums = product(g, tp, q, 1, raw)
             for rows in ([(0, 1), (1, 2)] if n == 0 else [(0, 2)]):
-                nc.scalar.activation(abs_raw[:, :, rows[0] : rows[1], :], raw_sums[:, :, rows[0] : rows[1], :], ABS)
                 k = len(turns)
                 turns.append(n)
+                width = (rows[1] - rows[0]) * P
+                raw = bank(4 + k % 2 if n < 4 else 5 if n == 7 else 2 * (n % 2) + 1, [P, 2, width], "raw%d" % k)
+                nc.scalar.activation(abs_raw[:, :, rows[0] : rows[1], :], product(g, tp, q, 1, raw, rows), ABS)
                 turned = bank(6 + k % 2, [P, 2, CHUNK], "turned%d" % k)
-                for u in range(*rows):
-                    for s in range(2):
-                        dst = turned[:, u, s * P : (s + 1) * P]
-                        nc.tensor.matmul(dst, neg_mag[:, s, u, :], ident[:], start=True, stop=False, is_transpose=True)
-                        nc.tensor.matmul(dst, abs_raw[:, s, u, :], ident[:], start=False, stop=True, is_transpose=True)
+                blocks = [(u, s) for u in range(*rows) for s in range(2)]
+                for part in (neg_mag, abs_raw):
+                    for u, s in blocks:
+                        nc.tensor.matmul(
+                            turned[:, u, s * P : (s + 1) * P],
+                            part[:, s, u, :],
+                            ident[:],
+                            start=(part is neg_mag and (u, s) == blocks[0]),
+                            stop=(part is abs_raw and (u, s) == blocks[-1]),
+                            is_transpose=True,
+                        )
                 nc.scalar.activation(h_cols[:, rows[0] : rows[1], :], turned[:, rows[0] : rows[1], :], COPY, scale=-1.0)
 
         def scatter(u, h_row, weights, j0, j1):
@@ -227,20 +222,39 @@ def tile_list_leakage_gap_audit_kernel(
 
         x0 = tile([P, PACK, M], F32, "x0")
 
+        wo_dealt = {}
+
+        def deal_wo_words():
+            wo_dealt["codes"] = tile([P, 2, 2 * N], U8, "wo_codes", "h_last0")
+            nc.gpsimd.tensor_copy(
+                wo_dealt["codes"][:].rearrange("p a (t c b) -> p a t c b", t=PACK, b=2),
+                wo_raw[:].rearrange("p a (c t b) -> p a t c b", t=PACK, b=2),
+            )
+
+        def deal_wo_scales():
+            wo_dealt["scales"] = tile([P, 2, N], U8, "wo_sc", "h_last1")
+            nc.gpsimd.tensor_copy(
+                wo_dealt["scales"][:].rearrange("p a (t c) -> p a t c", t=PACK),
+                wo_sc_raw[:].rearrange("p a (c t) -> p a t c", t=PACK),
+            )
+
         def plain_pair(tp):
             h = tile([P, 2, S], F32, "h0%d" % tp)
             for q in range(4):
                 cols = slice(q * CHUNK, (q + 1) * CHUNK)
-                gaps(0, tp, q, h[:, :, cols])
+                h_cols = tile([P, 2, CHUNK], F32, "h_last%d" % tp)[:] if q == 3 else h[:, :, cols]
+                gaps(0, tp, q, h_cols)
                 for u in range(2):
-                    scatter(u, h[:, u, cols], wg_plain[:, cols], q * CHUNK, (q + 1) * CHUNK)
-                if q == 0:
-                    if tp == 0:
-                        quantise_w1_plain(0, 1)
-                        quantise_w1_plain(1, 1)
-                    else:
-                        quantise_w1_dealt(0)
-                        quantise_w1_dealt(1)
+                    scatter(u, h_cols[:, u, :], wg_plain[:, cols], q * CHUNK, (q + 1) * CHUNK)
+                if tp == 0 and q < 2:
+                    quantise_w1_plain(q, 1)
+                if tp == 1 and q == 0:
+                    quantise_w1_dealt(0)
+                    quantise_w1_dealt(1)
+            if tp == 0:
+                deal_wo_words()
+            else:
+                deal_wo_scales()
             x_plain = tile([P, 2, M], F32, "x_plain%d" % tp, "h00" if tp else "h11")
             for u in range(2):
                 fetch(x_plain[:, u, :], u, 0, M)
@@ -318,8 +332,8 @@ def tile_list_leakage_gap_audit_kernel(
                     for t in range(t0, t1):
                         nc.tensor.matmul_mx(
                             out=y_banks[i, t0][:, t - t0, :],
-                            lhsT=wo_codes[:, a, 2 * P * t : 2 * P * (t + 1)].bitcast(FP4X4),
-                            lhsT_scale=wo_sc[:, a, P * t : P * (t + 1)],
+                            lhsT=wo_dealt["codes"][:, a, 2 * P * t : 2 * P * (t + 1)].bitcast(FP4X4),
+                            lhsT_scale=wo_dealt["scales"][:, a, P * t : P * (t + 1)],
                             rhs=z_codes[a, i // 2][:, i % 2 * P : (i % 2 + 1) * P].bitcast(FP8X4),
                             rhs_scale=z_scales[a][:, i * P : (i + 1) * P],
                             start=(a == 0 and t == t0),

@@ -16,6 +16,7 @@ FP8X4 = mybir.dt.float8_e4m3fn_x4
 FP4X4 = mybir.dt.float4_e2m1fn_x4
 COPY = mybir.ActivationFunctionType.Copy
 ABS = mybir.ActivationFunctionType.Abs
+RELU = mybir.ActivationFunctionType.Relu
 MULT = mybir.AluOpType.mult
 MAX = mybir.AluOpType.max
 
@@ -100,9 +101,6 @@ def tile_list_leakage_gap_audit_kernel(
         for b in range(2):
             for e in range(2):
                 load_w1(1, b, e)
-        for tp in range(2):
-            for quad in (0, 2, 1, 3):
-                nc.sync.dma_start(wg[tp][32 * quad : 32 * quad + 32, :, :], wgs_rows[:, 2 * tp : 2 * tp + 2, :])
 
         w_codes = {}
         w_scales = {}
@@ -155,17 +153,21 @@ def tile_list_leakage_gap_audit_kernel(
         gather_tab(3, CHUNK, 2 * CHUNK)
         gather_tab(3, 2 * CHUNK, S)
 
-        thr_rows = thr.rearrange("(a p t) m -> a p t m", p=P, t=PACK)
-        thr_sb = {}
-        x1_rows = tile([P, 10, CHUNK], F32, "x1_rows", "tab0")
-        thr_tags = (("tab0", "tab1", "thr0_2", "thr0_3"), ("tab2", "tab3", "thr1_2", "thr1_3"))
-        for g in range(2):
-            for c in range(M // CHUNK):
-                if (g, c) == (0, 0):
-                    thr_sb[g, c] = x1_rows[:, 0:10:3, :]
-                else:
-                    thr_sb[g, c] = tile([P, PACK, CHUNK], F32, "thr%d_%d" % (g, c), thr_tags[g][c])[:]
-                nc.sync.dma_start(thr_sb[g, c], thr_rows[g][:, :, c * CHUNK : (c + 1) * CHUNK])
+        neg_thr = [tile([P, 2, M], F32, "neg_thr%d" % tp, "tab%d" % tp) for tp in range(2)]
+        thr_rows = thr[K_PASS:, :].rearrange("(p t) m -> p t m", t=PACK)
+        thr_hi = [tile([P, 2, PACK, CHUNK], F32, "thr_hi%d" % e, "tab%d" % (2 + e)) for e in range(2)]
+
+        def load_thr_plain(tp):
+            rows = thr[tp * CHUNK : (tp + 1) * CHUNK, :].rearrange("(u q) m -> q u m", q=P)
+            nc.sync.dma_start(neg_thr[tp][:], rows)
+
+        load_thr_plain(0)
+        for tp in range(2):
+            for quad in (0, 2, 1, 3):
+                nc.sync.dma_start(wg[tp][32 * quad : 32 * quad + 32, :, :], wgs_rows[:, 2 * tp : 2 * tp + 2, :])
+        load_thr_plain(1)
+        for c in range(M // CHUNK):
+            nc.sync.dma_start(thr_hi[c // 2][:, c % 2, :, :], thr_rows[:, :, c * CHUNK : (c + 1) * CHUNK])
 
         def product(g, tp, q, half, acc, rows=(0, 2)):
             w_cols = slice(rows[0] * P, rows[1] * P)
@@ -220,15 +222,15 @@ def tile_list_leakage_gap_audit_kernel(
         def fetch(dst, u, m0, m1):
             nc.vector.tensor_copy(dst, pages[u][:].indirect(entries(list3, m0, m1)))
 
-        x0 = tile([P, PACK, M], F32, "x0")
+        x_plain = {}
 
         wo_dealt = {}
 
         def deal_wo_words():
             wo_dealt["codes"] = tile([P, 2, 2 * N], U8, "wo_codes", "h_last0")
-            nc.gpsimd.tensor_copy(
-                wo_dealt["codes"][:].rearrange("p a (t c b) -> p a t c b", t=PACK, b=2),
-                wo_raw[:].rearrange("p a (c t b) -> p a t c b", t=PACK, b=2),
+            nc.scalar.copy(
+                wo_dealt["codes"][:].bitcast(U16).rearrange("p a (t c) -> p a t c", t=PACK),
+                wo_raw[:].bitcast(U16).rearrange("p a (c t) -> p a t c", t=PACK),
             )
 
         def deal_wo_scales():
@@ -255,74 +257,115 @@ def tile_list_leakage_gap_audit_kernel(
                 deal_wo_words()
             else:
                 deal_wo_scales()
-            x_plain = tile([P, 2, M], F32, "x_plain%d" % tp, "h00" if tp else "h11")
+            x_plain[tp] = tile([P, 2, M], F32, "x_plain%d" % tp, "h00" if tp else "h11")
             for u in range(2):
-                fetch(x_plain[:, u, :], u, 0, M)
-                c = 2 * tp + u
-                for t in range(PACK):
-                    nc.sync.dma_start(x0[32 * c : 32 * c + 32, t, :], x_plain[t:P:PACK, u, :])
+                fetch(x_plain[tp][:, u, :], u, 0, M)
+
+        x_turned = tile([P, M // P, PACK, P], F32, "x_turned")
+        lift_turned = tile([P, M // P, PACK, P], F32, "lift_turned")
+
+        def turn(dst, src, start, stop):
+            nc.tensor.matmul(dst, src, ident[:], start=start, stop=stop, is_transpose=True)
+
+        def forward(tp, banks):
+            blocks = [(s, u) for s in range(2) for u in range(2)]
+            for c in range(M // CHUNK):
+                cols = slice(c * CHUNK, (c + 1) * CHUNK)
+                nc.scalar.activation(neg_thr[tp][:, :, cols], neg_thr[tp][:, :, cols], COPY, scale=-1.0)
+            for c in range(M // CHUNK):
+                rows = slice(64 * tp, 64 * tp + 64)
+                for index, parts, dst, func, scale in (
+                    (banks[0], (x_plain[tp],), x_turned, COPY, 1.0),
+                    (banks[1], (x_plain[tp], neg_thr[tp]), lift_turned, RELU, -1.0),
+                ):
+                    acc = bank(index, [P, 2, CHUNK], "forward%d_%d_%d" % (tp, c, index))
+                    for part in parts:
+                        for s, u in blocks:
+                            m0 = c * CHUNK + s * P
+                            first = part is parts[0] and (s, u) == blocks[0]
+                            last = part is parts[-1] and (s, u) == blocks[-1]
+                            turn(acc[:, s, u * P : (u + 1) * P], part[:, u, m0 : m0 + P], first, last)
+                    by_word = acc[:].rearrange("m s (j t) -> m s t j", t=PACK)
+                    nc.scalar.activation(dst[:, 2 * c : 2 * c + 2, :, rows], by_word, func, scale=scale)
 
         plain_pair(0)
         plain_pair(1)
+        forward(0, (4, 5))
 
-        def put_rows(g, tp):
-            h = tile([P, 2, S], F32, "h%d%d" % (g, tp))
-            for q in range(4):
-                gaps(g, tp, q, h[:, :, q * CHUNK : (q + 1) * CHUNK])
-            for u in range(2):
-                scatter(u, h[:, u, :], wg[tp][:, u, :], 0, S)
+        h_dealt = {}
+
+        def put_rows(tp, quarters, step):
+            if tp not in h_dealt:
+                h_dealt[tp] = tile([P, 2, S], F32, "h1%d" % tp)
+            h = h_dealt[tp]
+            for q in quarters:
+                gaps(1, tp, q, h[:, :, q * CHUNK : (q + 1) * CHUNK])
+            for j0 in range(quarters[0] * CHUNK, (quarters[-1] + 1) * CHUNK, step):
+                for u in range(2):
+                    scatter(u, h[:, u, j0 : j0 + step], wg[tp][:, u, j0 : j0 + step], j0, j0 + step)
 
         chunks = M // CHUNK
         pieces = [(c * CHUNK, (c + 1) * CHUNK) for c in range(chunks - 1)] + [(M - CHUNK, M - P), (M - P, M)]
         z_grouped = {}
         z_codes = {}
         z_scales = [tile([P, M], U8, "z_scales%d" % g) for g in range(2)]
-        z_tags = {(0, 0): "h10", (0, 1): "h00", (0, 2): thr_tags[1][1], (0, 3): thr_tags[1][2]}
 
         def in_chunk(k):
             c, s0 = divmod(pieces[k][0], CHUNK)
             return c, slice(s0, s0 + pieces[k][1] - pieces[k][0])
 
-        def threshold(g, k):
+        def threshold(k):
             c, cols = in_chunk(k)
-            if (g, c) not in z_grouped:
-                z_grouped[g, c] = tile([P, CHUNK, PACK], BF16, "z_grouped%d%d" % (g, c), z_tags.get((g, c)))
-            x = x1[c][:, :, cols] if g else x0[:, :, pieces[k][0] : pieces[k][1]]
+            if (1, c) not in z_grouped:
+                z_grouped[1, c] = tile([P, CHUNK, PACK], BF16, "z_grouped1%d" % c)[:]
             nc.vector.tensor_tensor(
-                z_grouped[g, c][:, cols, :].rearrange("p (c u) t -> p c t u", u=2),
-                x.rearrange("p t (c u) -> p c t u", u=2),
-                thr_sb[g, c][:, :, cols].rearrange("p t (c u) -> p c t u", u=2),
+                z_grouped[1, c][:, cols, :].rearrange("p (c u) t -> p c t u", u=2),
+                x1[c][:, :, cols].rearrange("p t (c u) -> p c t u", u=2),
+                thr_hi[c // 2][:, c % 2, :, cols].rearrange("p t (c u) -> p c t u", u=2),
                 MAX,
             )
 
-        def quantise_z(g, k):
-            c, cols = in_chunk(k)
+        def backward():
+            z_low = tile([P, M, PACK], BF16, "z_low", "tab1")
+            for c in range(chunks):
+                z_grouped[0, c] = z_low[:, c * CHUNK : (c + 1) * CHUNK, :]
+            for i in range(M // P):
+                acc = bank(i % 4, [P, PACK, P], "backward%d" % i)
+                for part in (x_turned, lift_turned):
+                    for t in range(PACK):
+                        first = part is x_turned and t == 0
+                        turn(acc[:, t, :], part[:, i, t, :], first, part is lift_turned and t == PACK - 1)
+                nc.scalar.copy(z_low[:, i * P : (i + 1) * P, :], acc[:].rearrange("p t m -> p m t"))
+
+        def quantise_z(g, m0, m1):
+            c, s0 = divmod(m0, CHUNK)
+            cols = slice(s0, s0 + m1 - m0)
             if (g, c) not in z_codes:
-                z_codes[g, c] = tile([P, CHUNK], U32, "z_codes%d_%d" % (g, c), None if g else "picked%d" % c)
+                z_codes[g, c] = tile([P, CHUNK], U32, "z_codes%d_%d" % (g, c))
             nc.vector.quantize_mx(
                 out=z_codes[g, c][:, cols].bitcast(FP8X4),
-                scales=z_scales[g][:, pieces[k][0] : pieces[k][1]],
+                scales=z_scales[g][:, m0:m1],
                 in_=z_grouped[g, c][:, cols, :].rearrange("p m t -> p (m t)"),
             )
 
-        put_rows(1, 0)
-        x1_second = tile([P, PACK, CHUNK], F32, "x1_second", "wg_plain")
-        x1 = [x1_rows[:, 4:8, :], x1_second[:], x1_rows[:, 2:6, :], x1_rows[:, 0:4, :]]
-        for c in range(chunks - 1):
-            fetch(x1[c][:, 0, :], 0, c * CHUNK, (c + 1) * CHUNK)
-        threshold(0, 0)
-        threshold(0, 1)
-        fetch(x1[chunks - 1][:, 0, :], 0, M - CHUNK, M)
+        put_rows(0, range(4), 2 * CHUNK)
+        x1_rows = [tile([P, 6, CHUNK], F32, "x1_rows%d" % e, ("tab0", "wg_plain")[e]) for e in range(2)]
+        x1 = [x1_rows[c % 2][:, 0:4, :] if c >= 2 else x1_rows[c % 2][:, 2:6, :] for c in range(chunks)]
+        for u in range(2):
+            for c in range(chunks):
+                fetch(x1[c][:, u, :], u, c * CHUNK, (c + 1) * CHUNK)
+        put_rows(1, range(2), 2 * CHUNK)
+        forward(1, (6, 7))
+        backward()
         for c in range(chunks):
-            fetch(x1[c][:, 1, :], 1, c * CHUNK, (c + 1) * CHUNK)
-        quantise_z(0, 0)
-        quantise_z(0, 1)
-        put_rows(1, 1)
+            quantise_z(0, c * CHUNK, (c + 1) * CHUNK)
+        put_rows(1, range(2, 4), CHUNK)
 
         y_banks = {}
 
         def y_groups(i):
-            return [(i, 0, 2), (0, 2, PACK)] if i == M // P - 1 else [(i, 0, PACK)]
+            index = 3 - i if i < 4 else i
+            return [(index, 0, 2), (3, 2, PACK)] if i == M // P - 1 else [(index, 0, PACK)]
 
         def output_pass(a, k):
             for i in range(pieces[k][0] // P, pieces[k][1] // P):
@@ -340,9 +383,6 @@ def tile_list_leakage_gap_audit_kernel(
                             stop=(a == 1 and t == t1 - 1),
                         )
 
-        output_pass(0, 0)
-        output_pass(0, 1)
-
         y = [tile([P, PACK, CHUNK], F32, "y%d" % c, "w_raw%d" % c) for c in range(chunks)]
         y_grouped = [tile([P, CHUNK, PACK], BF16, "y_grouped%d" % c, "neg_mag%d" % c) for c in range(chunks)]
         y_codes = tile([P, M], U32, "y_codes")
@@ -350,16 +390,12 @@ def tile_list_leakage_gap_audit_kernel(
         out_rows = out_0.rearrange("(p t) m -> p t m", t=PACK)
         out_words = out_1[0].rearrange("p m t -> p (m t)").bitcast(I32)
 
-        def first_pass(k):
-            quantise_z(0, k)
-            output_pass(0, k)
-
         def second_pass(k):
-            quantise_z(1, k)
+            quantise_z(1, *pieces[k])
             output_pass(1, k)
             c, cols = in_chunk(k)
             m0, m1 = pieces[k]
-            if m1 - m0 == CHUNK:
+            if k < 2:
                 for s in range(2):
                     sums = y_banks[2 * c + s, 0][:].rearrange("p t m -> p m t")
                     nc.scalar.copy(y_grouped[c][:, s * P : (s + 1) * P, :], sums)
@@ -367,12 +403,12 @@ def tile_list_leakage_gap_audit_kernel(
                     nc.scalar.copy(y[c][:, :, s * P : (s + 1) * P], y_banks[2 * c + s, 0][:])
                 nc.sync.dma_start(out_rows[:, :, m0:m1], y[c][:])
             else:
-                groups = y_groups(m0 // P)
-                for index, t0, t1 in groups:
-                    step = P // 2 if t0 else P
-                    for s0 in range(0, P, step):
-                        dst = y[c][:, t0:t1, cols.start + s0 : cols.start + s0 + step]
-                        nc.scalar.copy(dst, y_banks[m0 // P, t0][:, :, s0 : s0 + step])
+                for i in range(m0 // P, m1 // P):
+                    for index, t0, t1 in y_groups(i):
+                        step = P // 2 if t0 else P
+                        for s0 in range(0, P, step):
+                            dst = y[c][:, t0:t1, i % 2 * P + s0 : i % 2 * P + s0 + step]
+                            nc.scalar.copy(dst, y_banks[i, t0][:, :, s0 : s0 + step])
                 nc.sync.dma_start(out_rows[:, :, m0:m1], y[c][:, :, cols])
 
         def round_y(m0, m1):
@@ -399,34 +435,32 @@ def tile_list_leakage_gap_audit_kernel(
         def fetch_last(c, u):
             fetch(x1[c][:, 2 + u, :], u, c * CHUNK, (c + 1) * CHUNK)
 
+        for k in range(len(pieces) - 1):
+            output_pass(0, k)
         fetch_last(0, 0)
         fetch_last(0, 1)
         fetch_last(1, 0)
-        threshold(1, 0)
+        threshold(0)
         fetch_last(1, 1)
         second_pass(0)
         fetch_last(2, 0)
-        threshold(1, 1)
+        threshold(1)
         fetch_last(2, 1)
         second_pass(1)
-        threshold(0, 2)
-        threshold(1, 2)
-        first_pass(2)
-        planes(*pieces[0])
-        second_pass(2)
         fetch_last(3, 0)
+        threshold(2)
         fetch_last(3, 1)
-        threshold(0, 3)
-        threshold(1, 3)
-        first_pass(3)
-        threshold(0, 4)
+        second_pass(2)
+        planes(*pieces[0])
+        threshold(3)
+        threshold(4)
         second_pass(3)
-        threshold(1, 4)
-        first_pass(4)
         planes(*pieces[1])
-        planes(*pieces[2])
+        output_pass(0, 4)
         second_pass(4)
+        round_y(*pieces[2])
         round_y(*pieces[3])
+        planes(*pieces[2])
         planes(*pieces[3])
         halves = [(M - P, M - P // 2), (M - P // 2, M)]
         for half in halves:

@@ -92,12 +92,6 @@ def tile_list_leakage_gap_audit_kernel(
         nc.sync.dma_start(wg_plain[:, CHUNK:S], wgs[:, CHUNK:S])
         for b in range(2):
             load_w1(0, b, 1)
-        nc.sync.dma_start(wo_raw[:].bitcast(I32), wo_words.rearrange("a p c -> p a c").bitcast(I32))
-        for quad in range(4):
-            nc.sync.dma_start(
-                wo_sc_raw[32 * quad : 32 * quad + 4, :, :].bitcast(I32),
-                wo_scales[:, 4 * quad : 4 * quad + 4, :].rearrange("a q c -> q a c").bitcast(I32),
-            )
         for b in range(2):
             for e in range(2):
                 load_w1(1, b, e)
@@ -168,6 +162,12 @@ def tile_list_leakage_gap_audit_kernel(
         load_thr_plain(1)
         for c in range(M // CHUNK):
             nc.sync.dma_start(thr_hi[c // 2][:, c % 2, :, :], thr_rows[:, :, c * CHUNK : (c + 1) * CHUNK])
+        nc.sync.dma_start(wo_raw[:].bitcast(I32), wo_words.rearrange("a p c -> p a c").bitcast(I32))
+        for quad in range(4):
+            nc.sync.dma_start(
+                wo_sc_raw[32 * quad : 32 * quad + 4, :, :].bitcast(I32),
+                wo_scales[:, 4 * quad : 4 * quad + 4, :].rearrange("a q c -> q a c").bitcast(I32),
+            )
 
         def product(g, tp, q, half, acc, rows=(0, 2)):
             w_cols = slice(rows[0] * P, rows[1] * P)
@@ -227,7 +227,7 @@ def tile_list_leakage_gap_audit_kernel(
         wo_dealt = {}
 
         def deal_wo_words():
-            wo_dealt["codes"] = tile([P, 2, 2 * N], U8, "wo_codes", "h_last0")
+            wo_dealt["codes"] = tile([P, 2, 2 * N], U8, "wo_codes", "w_bf000")
             nc.scalar.copy(
                 wo_dealt["codes"][:].bitcast(U16).rearrange("p a (t c) -> p a t c", t=PACK),
                 wo_raw[:].bitcast(U16).rearrange("p a (c t) -> p a t c", t=PACK),
@@ -250,16 +250,19 @@ def tile_list_leakage_gap_audit_kernel(
                     scatter(u, h_cols[:, u, :], wg_plain[:, cols], q * CHUNK, (q + 1) * CHUNK)
                 if tp == 0 and q < 2:
                     quantise_w1_plain(q, 1)
-                if tp == 1 and q == 0:
+                if tp == 0 and q == 3:
                     quantise_w1_dealt(0)
                     quantise_w1_dealt(1)
-            if tp == 0:
+            if tp == 1:
                 deal_wo_words()
-            else:
                 deal_wo_scales()
-            x_plain[tp] = tile([P, 2, M], F32, "x_plain%d" % tp, "h00" if tp else "h11")
+            if tp == 0:
+                x_plain[tp] = [tile([P, M], F32, "x_plain0%d" % u, "w_bf1%d" % u)[:] for u in range(2)]
+            else:
+                x_second = tile([P, 2, M], F32, "x_plain1", "h00")
+                x_plain[tp] = [x_second[:, u, :] for u in range(2)]
             for u in range(2):
-                fetch(x_plain[tp][:, u, :], u, 0, M)
+                fetch(x_plain[tp][u], u, 0, M)
 
         x_turned = tile([P, M // P, PACK, P], F32, "x_turned")
         lift_turned = tile([P, M // P, PACK, P], F32, "lift_turned")
@@ -272,11 +275,12 @@ def tile_list_leakage_gap_audit_kernel(
             for c in range(M // CHUNK):
                 cols = slice(c * CHUNK, (c + 1) * CHUNK)
                 nc.scalar.activation(neg_thr[tp][:, :, cols], neg_thr[tp][:, :, cols], COPY, scale=-1.0)
+            neg_rows = [neg_thr[tp][:, u, :] for u in range(2)]
             for c in range(M // CHUNK):
                 rows = slice(64 * tp, 64 * tp + 64)
                 for index, parts, dst, func, scale in (
                     (banks[0], (x_plain[tp],), x_turned, COPY, 1.0),
-                    (banks[1], (x_plain[tp], neg_thr[tp]), lift_turned, RELU, -1.0),
+                    (banks[1], (x_plain[tp], neg_rows), lift_turned, RELU, -1.0),
                 ):
                     acc = bank(index, [P, 2, CHUNK], "forward%d_%d_%d" % (tp, c, index))
                     for part in parts:
@@ -284,13 +288,12 @@ def tile_list_leakage_gap_audit_kernel(
                             m0 = c * CHUNK + s * P
                             first = part is parts[0] and (s, u) == blocks[0]
                             last = part is parts[-1] and (s, u) == blocks[-1]
-                            turn(acc[:, s, u * P : (u + 1) * P], part[:, u, m0 : m0 + P], first, last)
+                            turn(acc[:, s, u * P : (u + 1) * P], part[u][:, m0 : m0 + P], first, last)
                     by_word = acc[:].rearrange("m s (j t) -> m s t j", t=PACK)
                     nc.scalar.activation(dst[:, 2 * c : 2 * c + 2, :, rows], by_word, func, scale=scale)
 
         plain_pair(0)
         plain_pair(1)
-        forward(0, (4, 5))
 
         h_dealt = {}
 
@@ -325,17 +328,17 @@ def tile_list_leakage_gap_audit_kernel(
                 MAX,
             )
 
-        def backward():
-            z_low = tile([P, M, PACK], BF16, "z_low", "tab1")
-            for c in range(chunks):
-                z_grouped[0, c] = z_low[:, c * CHUNK : (c + 1) * CHUNK, :]
-            for i in range(M // P):
+        def backward(tiles):
+            for i in tiles:
                 acc = bank(i % 4, [P, PACK, P], "backward%d" % i)
                 for part in (x_turned, lift_turned):
                     for t in range(PACK):
                         first = part is x_turned and t == 0
                         turn(acc[:, t, :], part[:, i, t, :], first, part is lift_turned and t == PACK - 1)
                 nc.scalar.copy(z_low[:, i * P : (i + 1) * P, :], acc[:].rearrange("p t m -> p m t"))
+                if i % 2:
+                    z_grouped[0, i // 2] = z_low[:, (i - 1) * P : (i + 1) * P, :]
+                    quantise_z(0, (i - 1) * P, (i + 1) * P)
 
         def quantise_z(g, m0, m1):
             c, s0 = divmod(m0, CHUNK)
@@ -348,18 +351,21 @@ def tile_list_leakage_gap_audit_kernel(
                 in_=z_grouped[g, c][:, cols, :].rearrange("p m t -> p (m t)"),
             )
 
-        put_rows(0, range(4), 2 * CHUNK)
+        put_rows(0, range(2), CHUNK)
+        forward(0, (6, 7))
+        put_rows(0, range(2, 4), CHUNK)
         x1_rows = [tile([P, 6, CHUNK], F32, "x1_rows%d" % e, ("tab0", "wg_plain")[e]) for e in range(2)]
         x1 = [x1_rows[c % 2][:, 0:4, :] if c >= 2 else x1_rows[c % 2][:, 2:6, :] for c in range(chunks)]
         for u in range(2):
             for c in range(chunks):
                 fetch(x1[c][:, u, :], u, c * CHUNK, (c + 1) * CHUNK)
-        put_rows(1, range(2), 2 * CHUNK)
+        put_rows(1, range(2), CHUNK)
         forward(1, (6, 7))
-        backward()
-        for c in range(chunks):
-            quantise_z(0, c * CHUNK, (c + 1) * CHUNK)
-        put_rows(1, range(2, 4), CHUNK)
+        z_low = tile([P, M, PACK], BF16, "z_low", "tab1")
+        put_rows(1, range(2, 3), CHUNK)
+        backward(range(4))
+        put_rows(1, range(3, 4), CHUNK)
+        backward(range(4, 8))
 
         y_banks = {}
 

@@ -18,6 +18,7 @@ COPY = mybir.ActivationFunctionType.Copy
 ABS = mybir.ActivationFunctionType.Abs
 RELU = mybir.ActivationFunctionType.Relu
 MULT = mybir.AluOpType.mult
+ADD = mybir.AluOpType.add
 MAX = mybir.AluOpType.max
 
 P = 128
@@ -147,21 +148,22 @@ def tile_list_leakage_gap_audit_kernel(
         gather_tab(3, CHUNK, 2 * CHUNK)
         gather_tab(3, 2 * CHUNK, S)
 
-        neg_thr = [tile([P, 2, M], F32, "neg_thr%d" % tp, "tab%d" % tp) for tp in range(2)]
+        thr_turn = [tile([P, 2, M], F32, "thr_turn%d" % tp, "tab%d" % tp) for tp in range(3)]
         thr_rows = thr[K_PASS:, :].rearrange("(p t) m -> p t m", t=PACK)
-        thr_hi = [tile([P, 2, PACK, CHUNK], F32, "thr_hi%d" % e, "tab%d" % (2 + e)) for e in range(2)]
+        thr_hi = [tile([P, 2, CHUNK], F32, "thr_hi%d" % c) for c in range(M // CHUNK)]
 
         def load_thr_plain(tp):
             rows = thr[tp * CHUNK : (tp + 1) * CHUNK, :].rearrange("(u q) m -> q u m", q=P)
-            nc.sync.dma_start(neg_thr[tp][:], rows)
+            nc.sync.dma_start(thr_turn[tp][:], rows)
 
         load_thr_plain(0)
         for tp in range(2):
             for quad in (0, 2, 1, 3):
                 nc.sync.dma_start(wg[tp][32 * quad : 32 * quad + 32, :, :], wgs_rows[:, 2 * tp : 2 * tp + 2, :])
         load_thr_plain(1)
+        nc.sync.dma_start(thr_turn[2][:], thr_rows[:, 0:2, :])
         for c in range(M // CHUNK):
-            nc.sync.dma_start(thr_hi[c // 2][:, c % 2, :, :], thr_rows[:, :, c * CHUNK : (c + 1) * CHUNK])
+            nc.sync.dma_start(thr_hi[c][:], thr_rows[:, 2:4, c * CHUNK : (c + 1) * CHUNK])
         nc.sync.dma_start(wo_raw[:].bitcast(I32), wo_words.rearrange("a p c -> p a c").bitcast(I32))
         for quad in range(4):
             nc.sync.dma_start(
@@ -222,6 +224,11 @@ def tile_list_leakage_gap_audit_kernel(
         def fetch(dst, u, m0, m1):
             nc.vector.tensor_copy(dst, pages[u][:].indirect(entries(list3, m0, m1)))
 
+        def fetch_negated(dst, u):
+            for m0 in range(0, M, M // 2):
+                window = pages[u][:].indirect(entries(list3, m0, m0 + M // 2))
+                nc.vector.tensor_scalar(dst[:, m0 : m0 + M // 2], window, -1.0, 0.0, MULT, ADD)
+
         x_plain = {}
 
         wo_dealt = {}
@@ -262,7 +269,7 @@ def tile_list_leakage_gap_audit_kernel(
                 x_second = tile([P, 2, M], F32, "x_plain1", "h00")
                 x_plain[tp] = [x_second[:, u, :] for u in range(2)]
             for u in range(2):
-                fetch(x_plain[tp][u], u, 0, M)
+                fetch_negated(x_plain[tp][u], u)
 
         x_turned = tile([P, M // P, PACK, P], F32, "x_turned")
         lift_turned = tile([P, M // P, PACK, P], F32, "lift_turned")
@@ -270,27 +277,33 @@ def tile_list_leakage_gap_audit_kernel(
         def turn(dst, src, start, stop):
             nc.tensor.matmul(dst, src, ident[:], start=start, stop=stop, is_transpose=True)
 
-        def forward(tp, banks):
+        def forward(tp, c, banks, x_out, lift_out, order):
             blocks = [(s, u) for s in range(2) for u in range(2)]
+            thr_pair = [thr_turn[tp][:, u, :] for u in range(2)]
+            for index, parts, dst, func, scale in (
+                (banks[0], (x_plain[tp],), x_out, COPY, -1.0),
+                (banks[1], (x_plain[tp], thr_pair), lift_out, RELU, 1.0),
+            ):
+                acc = bank(index, [P, 2, CHUNK], "forward%d_%d_%d" % (tp, c, index))
+                for part in parts:
+                    for s, u in blocks:
+                        m0 = c * CHUNK + s * P
+                        first = part is parts[0] and (s, u) == blocks[0]
+                        last = part is parts[-1] and (s, u) == blocks[-1]
+                        turn(acc[:, s, u * P : (u + 1) * P], part[u][:, m0 : m0 + P], first, last)
+                nc.scalar.activation(dst, order(acc[:]), func, scale=scale)
+
+        def forward_plain(tp):
+            rows = slice(64 * tp, 64 * tp + 64)
             for c in range(M // CHUNK):
-                cols = slice(c * CHUNK, (c + 1) * CHUNK)
-                nc.scalar.activation(neg_thr[tp][:, :, cols], neg_thr[tp][:, :, cols], COPY, scale=-1.0)
-            neg_rows = [neg_thr[tp][:, u, :] for u in range(2)]
-            for c in range(M // CHUNK):
-                rows = slice(64 * tp, 64 * tp + 64)
-                for index, parts, dst, func, scale in (
-                    (banks[0], (x_plain[tp],), x_turned, COPY, 1.0),
-                    (banks[1], (x_plain[tp], neg_rows), lift_turned, RELU, -1.0),
-                ):
-                    acc = bank(index, [P, 2, CHUNK], "forward%d_%d_%d" % (tp, c, index))
-                    for part in parts:
-                        for s, u in blocks:
-                            m0 = c * CHUNK + s * P
-                            first = part is parts[0] and (s, u) == blocks[0]
-                            last = part is parts[-1] and (s, u) == blocks[-1]
-                            turn(acc[:, s, u * P : (u + 1) * P], part[u][:, m0 : m0 + P], first, last)
-                    by_word = acc[:].rearrange("m s (j t) -> m s t j", t=PACK)
-                    nc.scalar.activation(dst[:, 2 * c : 2 * c + 2, :, rows], by_word, func, scale=scale)
+                forward(
+                    tp,
+                    c,
+                    (2, 3) if c % 2 else (6, 7),
+                    x_turned[:, 2 * c : 2 * c + 2, :, rows],
+                    lift_turned[:, 2 * c : 2 * c + 2, :, rows],
+                    lambda acc: acc.rearrange("m s (j t) -> m s t j", t=PACK),
+                )
 
         plain_pair(0)
         plain_pair(1)
@@ -319,59 +332,75 @@ def tile_list_leakage_gap_audit_kernel(
 
         def threshold(k):
             c, cols = in_chunk(k)
-            if (1, c) not in z_grouped:
-                z_grouped[1, c] = tile([P, CHUNK, PACK], BF16, "z_grouped1%d" % c)[:]
             nc.vector.tensor_tensor(
-                z_grouped[1, c][:, cols, :].rearrange("p (c u) t -> p c t u", u=2),
-                x1[c][:, :, cols].rearrange("p t (c u) -> p c t u", u=2),
-                thr_hi[c // 2][:, c % 2, :, cols].rearrange("p t (c u) -> p c t u", u=2),
+                z_grouped[1, c][:, cols, 2:4].rearrange("p (c u) t -> p c t u", u=2),
+                x_last[c][:, :, cols].rearrange("p t (c u) -> p c t u", u=2),
+                thr_hi[c][:, :, cols].rearrange("p t (c u) -> p c t u", u=2),
                 MAX,
             )
 
+        z_tags = ("w_bf010", "h_last0", "wg_plain", "tab1")
+
         def backward(tiles):
             for i in tiles:
-                acc = bank(i % 4, [P, PACK, P], "backward%d" % i)
+                acc = bank((i + 2) % 4, [P, PACK, P], "backward%d" % i)
                 for part in (x_turned, lift_turned):
                     for t in range(PACK):
                         first = part is x_turned and t == 0
                         turn(acc[:, t, :], part[:, i, t, :], first, part is lift_turned and t == PACK - 1)
-                nc.scalar.copy(z_low[:, i * P : (i + 1) * P, :], acc[:].rearrange("p t m -> p m t"))
-                if i % 2:
-                    z_grouped[0, i // 2] = z_low[:, (i - 1) * P : (i + 1) * P, :]
-                    quantise_z(0, (i - 1) * P, (i + 1) * P)
+                c, s = divmod(i, 2)
+                if s == 0:
+                    z_grouped[0, c] = tile([P, CHUNK, PACK], BF16, "z_grouped0%d" % c, z_tags[c])[:]
+                nc.scalar.copy(z_grouped[0, c][:, s * P : (s + 1) * P, :], acc[:].rearrange("p t m -> p m t"))
 
         def quantise_z(g, m0, m1):
             c, s0 = divmod(m0, CHUNK)
             cols = slice(s0, s0 + m1 - m0)
             if (g, c) not in z_codes:
-                z_codes[g, c] = tile([P, CHUNK], U32, "z_codes%d_%d" % (g, c))
+                z_codes[g, c] = tile([P, CHUNK], U32, "z_codes%d_%d" % (g, c), "thr_hi%d" % (c - 1) if g == 0 and c else None)
             nc.vector.quantize_mx(
                 out=z_codes[g, c][:, cols].bitcast(FP8X4),
                 scales=z_scales[g][:, m0:m1],
                 in_=z_grouped[g, c][:, cols, :].rearrange("p m t -> p (m t)"),
             )
 
+        def dealt_maximum(c):
+            tiles = slice(2 * c, 2 * c + 2)
+            forward(2, c, (2, 3) if c % 2 else (0, 1), x_turned2[:, tiles, :], lift_turned2[:, tiles, :], lambda acc: acc)
+            acc = bank(6 + c % 2, [P, 2, 2, P], "backward1%d" % c)
+            blocks = [(s, u) for s in range(2) for u in range(2)]
+            for part in (x_turned2, lift_turned2):
+                for s, u in blocks:
+                    first = part is x_turned2 and (s, u) == blocks[0]
+                    last = part is lift_turned2 and (s, u) == blocks[-1]
+                    turn(acc[:, s, u, :], part[:, 2 * c + s, u * P : (u + 1) * P], first, last)
+            z_grouped[1, c] = tile([P, CHUNK, PACK], BF16, "z_grouped1%d" % c, "picked%d" % c)[:]
+            nc.scalar.copy(
+                z_grouped[1, c][:, :, 0:2].rearrange("p (s m) u -> p s m u", s=2),
+                acc[:].rearrange("p s u m -> p s m u"),
+            )
+
         put_rows(0, range(2), CHUNK)
-        forward(0, (6, 7))
+        forward_plain(0)
         put_rows(0, range(2, 4), CHUNK)
-        x1_rows = [tile([P, 6, CHUNK], F32, "x1_rows%d" % e, ("tab0", "wg_plain")[e]) for e in range(2)]
-        x1 = [x1_rows[c % 2][:, 0:4, :] if c >= 2 else x1_rows[c % 2][:, 2:6, :] for c in range(chunks)]
+        x_third = tile([P, 2, M], F32, "x_plain2", "tab0")
+        x_plain[2] = [x_third[:, u, :] for u in range(2)]
         for u in range(2):
-            for c in range(chunks):
-                fetch(x1[c][:, u, :], u, c * CHUNK, (c + 1) * CHUNK)
-        put_rows(1, range(2), CHUNK)
-        forward(1, (6, 7))
-        z_low = tile([P, M, PACK], BF16, "z_low", "tab1")
-        put_rows(1, range(2, 3), CHUNK)
-        backward(range(4))
-        put_rows(1, range(3, 4), CHUNK)
-        backward(range(4, 8))
+            fetch_negated(x_plain[2][u], u)
+        put_rows(1, range(4), CHUNK)
+        forward_plain(1)
+        backward(range(M // P))
+        quantise_z(0, 0, CHUNK)
+        x_turned2 = tile([P, M // P, CHUNK], F32, "x_turned2", "tab3")
+        lift_turned2 = tile([P, M // P, CHUNK], F32, "lift_turned2", "h01")
+        for c in range(chunks):
+            dealt_maximum(c)
 
         y_banks = {}
 
         def y_groups(i):
-            index = 3 - i if i < 4 else i
-            return [(index, 0, 2), (3, 2, PACK)] if i == M // P - 1 else [(index, 0, PACK)]
+            index = M // P - 1 - i
+            return [(index, 0, 2), (M // P - 1, 2, PACK)] if index == 0 else [(index, 0, PACK)]
 
         def output_pass(a, k):
             for i in range(pieces[k][0] // P, pieces[k][1] // P):
@@ -396,6 +425,10 @@ def tile_list_leakage_gap_audit_kernel(
         out_rows = out_0.rearrange("(p t) m -> p t m", t=PACK)
         out_words = out_1[0].rearrange("p m t -> p (m t)").bitcast(I32)
 
+        def first_pass(c):
+            quantise_z(0, c * CHUNK, (c + 1) * CHUNK)
+            output_pass(0, c)
+
         def second_pass(k):
             quantise_z(1, *pieces[k])
             output_pass(1, k)
@@ -403,11 +436,11 @@ def tile_list_leakage_gap_audit_kernel(
             m0, m1 = pieces[k]
             if k < 2:
                 for s in range(2):
-                    sums = y_banks[2 * c + s, 0][:].rearrange("p t m -> p m t")
-                    nc.scalar.copy(y_grouped[c][:, s * P : (s + 1) * P, :], sums)
-                for s in range(2):
                     nc.scalar.copy(y[c][:, :, s * P : (s + 1) * P], y_banks[2 * c + s, 0][:])
                 nc.sync.dma_start(out_rows[:, :, m0:m1], y[c][:])
+                for s in range(2):
+                    sums = y_banks[2 * c + s, 0][:].rearrange("p t m -> p m t")
+                    nc.scalar.copy(y_grouped[c][:, s * P : (s + 1) * P, :], sums)
             else:
                 for i in range(m0 // P, m1 // P):
                     for index, t0, t1 in y_groups(i):
@@ -438,32 +471,31 @@ def tile_list_leakage_gap_audit_kernel(
             if m1 in words_from:
                 nc.sync.dma_start(out_words[:, words_from[m1] : m1], y_codes[:, words_from[m1] : m1].bitcast(I32))
 
-        def fetch_last(c, u):
-            fetch(x1[c][:, 2 + u, :], u, c * CHUNK, (c + 1) * CHUNK)
+        x_last = {}
 
-        for k in range(len(pieces) - 1):
-            output_pass(0, k)
+        def fetch_last(c, u):
+            if c not in x_last:
+                x_last[c] = tile([P, 2, CHUNK], F32, "x_last%d" % c, ("tab0", "tab2")[c % 2])
+            fetch(x_last[c][:, u, :], u, c * CHUNK, (c + 1) * CHUNK)
+
+        output_pass(0, 0)
         fetch_last(0, 0)
         fetch_last(0, 1)
         fetch_last(1, 0)
-        threshold(0)
-        fetch_last(1, 1)
-        second_pass(0)
-        fetch_last(2, 0)
-        threshold(1)
-        fetch_last(2, 1)
-        second_pass(1)
-        fetch_last(3, 0)
-        threshold(2)
-        fetch_last(3, 1)
-        second_pass(2)
-        planes(*pieces[0])
+        for c in range(chunks - 1):
+            threshold(c)
+            fetch_last(c + 1, 1)
+            second_pass(c)
+            first_pass(c + 1)
+            if c + 2 < chunks:
+                fetch_last(c + 2, 0)
         threshold(3)
         threshold(4)
         second_pass(3)
-        planes(*pieces[1])
+        planes(*pieces[0])
         output_pass(0, 4)
         second_pass(4)
+        planes(*pieces[1])
         round_y(*pieces[2])
         round_y(*pieces[3])
         planes(*pieces[2])

@@ -100,8 +100,8 @@ def tile_list_leakage_gap_audit_kernel(
         w_codes = {}
         w_scales = {}
 
-        def quantise_words(key, grouped, width):
-            codes = tile([P, width], U32, "w_codes%d%d%d" % key)
+        def quantise_words(key, grouped, width, tag=None):
+            codes = tile([P, width], U32, "w_codes%d%d%d" % key, tag)
             scales = tile([P, width], U8, "w_scales%d%d%d" % key)
             nc.vector.quantize_mx(out=codes[:].bitcast(FP8X4), scales=scales[:], in_=grouped)
             return codes, scales
@@ -116,17 +116,20 @@ def tile_list_leakage_gap_audit_kernel(
             w_codes[0, b, tp] = codes[:]
             w_scales[0, b, tp] = scales[:]
 
-        def quantise_w1_dealt(b):
-            grouped = tile([P, 2, K_PASS // 2, PACK], BF16, "w_bf1%d" % b)
-            for e in range(2):
-                nc.scalar.copy(
-                    grouped[:, :, e * P : (e + 1) * P, :].rearrange("p h (m u) i -> p h m i u", u=2),
-                    w_raw[1, b, e][:].rearrange("p i (m h u) -> p h m i u", h=2, u=2),
-                )
-            codes, scales = quantise_words((1, b, 0), grouped[:].rearrange("p h c i -> p (h c i)"), K_PASS)
-            for tp in range(2):
-                w_codes[1, b, tp] = codes[:, tp * CHUNK : (tp + 1) * CHUNK]
-                w_scales[1, b, tp] = scales[:, tp * CHUNK : (tp + 1) * CHUNK]
+        def quantise_w1_dealt():
+            grouped = [tile([P, 2, K_PASS // 2, PACK], BF16, "w_bf1%d" % b) for b in range(2)]
+            for b in range(2):
+                for e in range(2):
+                    nc.scalar.copy(
+                        grouped[b][:, :, e * P : (e + 1) * P, :].rearrange("p h (m u) i -> p h m i u", u=2),
+                        w_raw[1, b, e][:].rearrange("p i (m h u) -> p h m i u", h=2, u=2),
+                    )
+            for b in range(2):
+                flat = grouped[b][:].rearrange("p h c i -> p (h c i)")
+                codes, scales = quantise_words((1, b, 0), flat, K_PASS, None if b else "w_raw3")
+                for tp in range(2):
+                    w_codes[1, b, tp] = codes[:, tp * CHUNK : (tp + 1) * CHUNK]
+                    w_scales[1, b, tp] = scales[:, tp * CHUNK : (tp + 1) * CHUNK]
 
         picked_sc = tile([P, S], U8, "picked_sc")
         picked = [tile([P, S], U32, "picked%d" % a) for a in range(4)]
@@ -240,11 +243,11 @@ def tile_list_leakage_gap_audit_kernel(
                 wo_raw[:].bitcast(U16).rearrange("p a (c t) -> p a t c", t=PACK),
             )
 
-        def deal_wo_scales():
-            wo_dealt["scales"] = tile([P, 2, N], U8, "wo_sc", "h_last1")
+        def deal_wo_scales(a, tag):
+            wo_dealt["scales", a] = tile([P, N], U8, "wo_sc%d" % a, tag)
             nc.gpsimd.tensor_copy(
-                wo_dealt["scales"][:].rearrange("p a (t c) -> p a t c", t=PACK),
-                wo_sc_raw[:].rearrange("p a (c t) -> p a t c", t=PACK),
+                wo_dealt["scales", a][:].rearrange("p (t c) -> p t c", t=PACK),
+                wo_sc_raw[:, a, :].rearrange("p (c t) -> p t c", t=PACK),
             )
 
         def plain_pair(tp):
@@ -258,11 +261,10 @@ def tile_list_leakage_gap_audit_kernel(
                 if tp == 0 and q < 2:
                     quantise_w1_plain(q, 1)
                 if tp == 0 and q == 3:
-                    quantise_w1_dealt(0)
-                    quantise_w1_dealt(1)
+                    quantise_w1_dealt()
             if tp == 1:
                 deal_wo_words()
-                deal_wo_scales()
+                deal_wo_scales(0, "h_last1")
             if tp == 0:
                 x_plain[tp] = [tile([P, M], F32, "x_plain0%d" % u, "w_bf1%d" % u)[:] for u in range(2)]
             else:
@@ -383,6 +385,7 @@ def tile_list_leakage_gap_audit_kernel(
         put_rows(0, range(2), CHUNK)
         forward_plain(0)
         put_rows(0, range(2, 4), CHUNK)
+        deal_wo_scales(1, "wg0")
         x_third = tile([P, 2, M], F32, "x_plain2", "tab0")
         x_plain[2] = [x_third[:, u, :] for u in range(2)]
         for u in range(2):
@@ -411,7 +414,7 @@ def tile_list_leakage_gap_audit_kernel(
                         nc.tensor.matmul_mx(
                             out=y_banks[i, t0][:, t - t0, :],
                             lhsT=wo_dealt["codes"][:, a, 2 * P * t : 2 * P * (t + 1)].bitcast(FP4X4),
-                            lhsT_scale=wo_dealt["scales"][:, a, P * t : P * (t + 1)],
+                            lhsT_scale=wo_dealt["scales", a][:, P * t : P * (t + 1)],
                             rhs=z_codes[a, i // 2][:, i % 2 * P : (i % 2 + 1) * P].bitcast(FP8X4),
                             rhs_scale=z_scales[a][:, i * P : (i + 1) * P],
                             start=(a == 0 and t == t0),

@@ -20,6 +20,7 @@ RELU = mybir.ActivationFunctionType.Relu
 MULT = mybir.AluOpType.mult
 ADD = mybir.AluOpType.add
 MAX = mybir.AluOpType.max
+SUB = mybir.AluOpType.subtract
 
 P = 128
 PACK = 4
@@ -62,7 +63,7 @@ def tile_list_leakage_gap_audit_kernel(
 
         def load_w1(g, b, e, i0=0, i1=PACK):
             if (g, b, e) not in w_raw:
-                w_raw[g, b, e] = tile([P, PACK, CHUNK], F32, "w_raw%d%d%d" % (g, b, e), "w_raw%d" % (2 * b + e))
+                w_raw[g, b, e] = tile([P, PACK, CHUNK], F32, "w_raw%d%d%d" % (g, b, e), "w_raw%d" % (4 if (g, b, e) == (0, 1, 1) else 2 * b + e))
             c0 = g * K_PASS + e * CHUNK
             rows = w1[b * K_PASS : (b + 1) * K_PASS, c0 : c0 + CHUNK].rearrange("(p i) c -> p i c", i=PACK)
             nc.sync.dma_start(w_raw[g, b, e][:, i0:i1, :], rows[:, i0:i1, :])
@@ -74,23 +75,22 @@ def tile_list_leakage_gap_audit_kernel(
 
         nc.sync.dma_start(list1[:], offs)
         load_tab(0, 0, T // 4)
-        load_tab(0, T // 4, T // 2)
-        load_tab(0, T // 2, T)
-        nc.sync.dma_start(list2[:], offs2)
-        nc.sync.dma_start(list3[:], offs3)
-        load_w1(0, 0, 0, 0, 2)
-        load_w1(0, 0, 0, 2, 4)
         for quad in range(4):
             nc.sync.dma_start(
                 tab_sc[32 * quad : 32 * quad + 16, :].bitcast(I32),
                 tab_scales[:, 4 * quad : 4 * quad + 4, :].bitcast(I32),
             )
+        load_tab(0, T // 4, T // 2)
+        load_w1(0, 0, 0)
+        load_tab(0, T // 2, T)
         load_tab(1)
         load_w1(0, 1, 0)
         load_tab(2)
         load_tab(3)
+        nc.sync.dma_start(list2[:], offs2)
         nc.sync.dma_start(wg_plain[:, 0:CHUNK], wgs[:, 0:CHUNK])
         nc.sync.dma_start(wg_plain[:, CHUNK:S], wgs[:, CHUNK:S])
+        nc.sync.dma_start(list3[:], offs3)
         for b in range(2):
             load_w1(0, b, 1)
         for b in range(2):
@@ -107,7 +107,7 @@ def tile_list_leakage_gap_audit_kernel(
             return codes, scales
 
         def quantise_w1_plain(b, tp):
-            grouped = tile([P, CHUNK, PACK], BF16, "w_bf0%d%d" % (b, tp), "neg_mag%d" % b if tp else None)
+            grouped = tile([P, CHUNK, PACK], BF16, "w_bf0%d%d" % (b, tp), "neg_mag%d" % (3 * b) if tp else None)
             nc.scalar.copy(
                 grouped[:].rearrange("p (m u) i -> p m i u", u=2),
                 w_raw[0, b, tp][:].rearrange("p i (m u) -> p m i u", u=2),
@@ -141,15 +141,35 @@ def tile_list_leakage_gap_audit_kernel(
         for u in range(2):
             nc.vector.memset(pages[u][:].bitcast(I32), 0)
 
+        nc.vector.tensor_copy(picked_sc[:], tab_sc[:].indirect(list1[:]))
         gather_tab(0, 0, S)
         quantise_w1_plain(0, 0)
-        nc.vector.tensor_copy(picked_sc[:], tab_sc[:].indirect(list1[:]))
         gather_tab(1, 0, S)
         quantise_w1_plain(1, 0)
         gather_tab(2, 0, S)
         gather_tab(3, 0, CHUNK)
         gather_tab(3, CHUNK, 2 * CHUNK)
         gather_tab(3, 2 * CHUNK, S)
+
+        def first_gaps(h_row):
+            sums = []
+            for half in range(2):
+                acc = bank(6 + half, [P, CHUNK], "first%d" % half)
+                for b in range(2):
+                    k = 2 * half + b
+                    nc.tensor.matmul_mx(
+                        out=acc[:],
+                        lhsT=w_codes[0, b, 0][:, 0:P].bitcast(FP8X4),
+                        lhsT_scale=w_scales[0, b, 0][:, 0:P],
+                        rhs=picked[k][:, 0:CHUNK].bitcast(FP8X4),
+                        rhs_scale=picked_sc[4 * k :, 0:CHUNK],
+                        start=(b == 0),
+                        stop=(b == 1),
+                    )
+                sums.append(acc)
+            abs_first = tile([P, CHUNK], F32, "abs_first")
+            nc.scalar.activation(abs_first[:], sums[1][:], ABS)
+            nc.vector.tensor_tensor(h_row, sums[0][:], abs_first[:], SUB)
 
         thr_turn = [tile([P, 2, M], F32, "thr_turn%d" % tp, "tab%d" % tp) for tp in range(3)]
         thr_rows = thr[K_PASS:, :].rearrange("(p t) m -> p t m", t=PACK)
@@ -193,18 +213,17 @@ def tile_list_leakage_gap_audit_kernel(
                 return acc[:].rearrange("p s (u m) -> p s u m", m=P)
             return acc[:].rearrange("p s (m u) -> p s u m", u=2)
 
-        turns = []
-
         def gaps(g, tp, q, h_cols):
             n = 8 * g + 4 * tp + q
             neg_mag = tile([P, 2, 2, P], F32, "neg_mag%d" % n, "neg_mag%d" % (n % 4))
             abs_raw = tile([P, 2, 2, P], F32, "abs_raw%d" % n, "abs_raw%d" % (n % 3))
-            mag = bank(n if n < 4 else 4 if n == 4 else 5 if n == 8 else 2 * (n % 2), [P, 2, CHUNK], "mag%d" % n)
-            nc.scalar.activation(neg_mag[:], product(g, tp, q, 0, mag), COPY, scale=-1.0)
-            for rows in ([(0, 1), (1, 2)] if n == 0 else [(0, 2)]):
-                k = len(turns)
-                turns.append(n)
-                width = (rows[1] - rows[0]) * P
+            rows = (1, 2) if n == 0 else (0, 2)
+            width = (rows[1] - rows[0]) * P
+            if n == 0:
+                first_gaps(h_cols[:, 0, :])
+            mag = bank(n if n < 4 else 4 if n == 4 else 5 if n == 8 else 2 * (n % 2), [P, 2, width], "mag%d" % n)
+            nc.scalar.activation(neg_mag[:, :, rows[0] : rows[1], :], product(g, tp, q, 0, mag, rows), COPY, scale=-1.0)
+            for k in [n + 1]:
                 raw = bank(4 + k % 2 if n < 4 else 5 if n == 7 else 2 * (n % 2) + 1, [P, 2, width], "raw%d" % k)
                 nc.scalar.activation(abs_raw[:, :, rows[0] : rows[1], :], product(g, tp, q, 1, raw, rows), ABS)
                 turned = bank(6 + k % 2, [P, 2, CHUNK], "turned%d" % k)
@@ -258,18 +277,16 @@ def tile_list_leakage_gap_audit_kernel(
                 gaps(0, tp, q, h_cols)
                 for u in range(2):
                     scatter(u, h_cols[:, u, :], wg_plain[:, cols], q * CHUNK, (q + 1) * CHUNK)
-                if tp == 0 and q < 2:
-                    quantise_w1_plain(q, 1)
+                if tp == 0 and q == 0:
+                    quantise_w1_plain(0, 1)
                 if tp == 0 and q == 3:
+                    quantise_w1_plain(1, 1)
                     quantise_w1_dealt()
             if tp == 1:
                 deal_wo_words()
                 deal_wo_scales(0, "h_last1")
-            if tp == 0:
-                x_plain[tp] = [tile([P, M], F32, "x_plain0%d" % u, "w_bf1%d" % u)[:] for u in range(2)]
-            else:
-                x_second = tile([P, 2, M], F32, "x_plain1", "h00")
-                x_plain[tp] = [x_second[:, u, :] for u in range(2)]
+            x_pair = tile([P, 2, M], F32, "x_plain%d" % tp, ("tab3", "h00")[tp])
+            x_plain[tp] = [x_pair[:, u, :] for u in range(2)]
             for u in range(2):
                 fetch_negated(x_plain[tp][u], u)
 

@@ -340,17 +340,16 @@ def tile_list_leakage_gap_audit_kernel(
                     scatter(u, h[:, u, j0 : j0 + step], wg[tp][:, u, j0 : j0 + step], j0, j0 + step)
 
         chunks = M // CHUNK
-        pieces = [(c * CHUNK, (c + 1) * CHUNK) for c in range(chunks - 1)] + [(M - CHUNK, M - P), (M - P, M)]
         z_grouped = {}
         z_codes = {}
         z_scales = [tile([P, M], U8, "z_scales%d" % g) for g in range(2)]
 
-        def in_chunk(k):
-            c, s0 = divmod(pieces[k][0], CHUNK)
-            return c, slice(s0, s0 + pieces[k][1] - pieces[k][0])
+        def in_chunk(m0, m1):
+            c, s0 = divmod(m0, CHUNK)
+            return c, slice(s0, s0 + m1 - m0)
 
-        def threshold(k):
-            c, cols = in_chunk(k)
+        def threshold(m0, m1):
+            c, cols = in_chunk(m0, m1)
             nc.vector.tensor_tensor(
                 z_grouped[1, c][:, cols, 2:4].rearrange("p (c u) t -> p c t u", u=2),
                 x_last[c][:, :, cols].rearrange("p t (c u) -> p c t u", u=2),
@@ -376,7 +375,7 @@ def tile_list_leakage_gap_audit_kernel(
             c, s0 = divmod(m0, CHUNK)
             cols = slice(s0, s0 + m1 - m0)
             if (g, c) not in z_codes:
-                z_codes[g, c] = tile([P, CHUNK], U32, "z_codes%d_%d" % (g, c), "thr_hi%d" % (c - 1) if g == 0 and c else None)
+                z_codes[g, c] = tile([P, CHUNK], U32, "z_codes%d_%d" % (g, c), None if g else "thr_hi%d" % (c - 1) if c else "w_raw4")
             nc.vector.quantize_mx(
                 out=z_codes[g, c][:, cols].bitcast(FP8X4),
                 scales=z_scales[g][:, m0:m1],
@@ -403,14 +402,12 @@ def tile_list_leakage_gap_audit_kernel(
         forward_plain(0)
         put_rows(0, range(2, 4), CHUNK)
         deal_wo_scales(1, "wg0")
-        x_third = tile([P, 2, M], F32, "x_plain2", "tab0")
-        x_plain[2] = [x_third[:, u, :] for u in range(2)]
+        x_plain[2] = [tile([P, M], F32, "x_plain2%d" % u, ("tab0", "w_raw4")[u])[:] for u in range(2)]
         for u in range(2):
             fetch_negated(x_plain[2][u], u)
         put_rows(1, range(4), CHUNK)
         forward_plain(1)
         backward(range(M // P))
-        quantise_z(0, 0, CHUNK)
         x_turned2 = tile([P, M // P, CHUNK], F32, "x_turned2", "tab3")
         lift_turned2 = tile([P, M // P, CHUNK], F32, "lift_turned2", "h01")
         for c in range(chunks):
@@ -422,8 +419,28 @@ def tile_list_leakage_gap_audit_kernel(
             index = M // P - 1 - i
             return [(index, 0, 2), (M // P - 1, 2, PACK)] if index == 0 else [(index, 0, PACK)]
 
-        def output_pass(a, k):
-            for i in range(pieces[k][0] // P, pieces[k][1] // P):
+        def output_pass_by_rows(a, c):
+            for pair in range(2):
+                if a == 0:
+                    y_banks[c, "rows", pair] = bank(M // P - 1 - 2 * c - pair, [P, 2, CHUNK], "y_rows%d" % pair)
+                for u in range(2):
+                    t = 2 * pair + u
+                    nc.tensor.matmul_mx(
+                        out=y_banks[c, "rows", pair][:, u, :],
+                        lhsT=wo_dealt["codes"][:, a, 2 * P * t : 2 * P * (t + 1)].bitcast(FP4X4),
+                        lhsT_scale=wo_dealt["scales", a][:, P * t : P * (t + 1)],
+                        rhs=z_codes[a, c][:].bitcast(FP8X4),
+                        rhs_scale=z_scales[a][:, c * CHUNK : (c + 1) * CHUNK],
+                        start=(a == 0 and u == 0),
+                        stop=(a == 1 and u == 1),
+                    )
+                if a == 1:
+                    rows = slice(2 * pair, 2 * pair + 2)
+                    nc.scalar.copy(y[c][:, rows, :], y_banks[c, "rows", pair][:])
+                    nc.sync.dma_start(out_rows[:, rows, c * CHUNK : (c + 1) * CHUNK], y[c][:, rows, :])
+
+        def output_pass(a, m0, m1):
+            for i in range(m0 // P, m1 // P):
                 for index, t0, t1 in y_groups(i):
                     if a == 0:
                         y_banks[i, t0] = bank(index, [P, t1 - t0, P], "y%d_%d" % (i, t0))
@@ -445,40 +462,39 @@ def tile_list_leakage_gap_audit_kernel(
         out_rows = out_0.rearrange("(p t) m -> p t m", t=PACK)
         out_words = out_1[0].rearrange("p m t -> p (m t)").bitcast(I32)
 
-        def first_pass(c):
-            quantise_z(0, c * CHUNK, (c + 1) * CHUNK)
-            output_pass(0, c)
+        def first_pass(m0, m1):
+            quantise_z(0, m0, m1)
+            output_pass(0, m0, min(m1, M - P))
 
-        def second_pass(k):
-            quantise_z(1, *pieces[k])
-            output_pass(1, k)
-            c, cols = in_chunk(k)
-            m0, m1 = pieces[k]
-            if k < 2:
-                for s in range(2):
-                    nc.scalar.copy(y[c][:, :, s * P : (s + 1) * P], y_banks[2 * c + s, 0][:])
-                nc.sync.dma_start(out_rows[:, :, m0:m1], y[c][:])
-                for s in range(2):
-                    sums = y_banks[2 * c + s, 0][:].rearrange("p t m -> p m t")
-                    nc.scalar.copy(y_grouped[c][:, s * P : (s + 1) * P, :], sums)
-            else:
-                for i in range(m0 // P, m1 // P):
-                    for index, t0, t1 in y_groups(i):
-                        step = P // 2 if t0 else P
-                        for s0 in range(0, P, step):
-                            dst = y[c][:, t0:t1, i % 2 * P + s0 : i % 2 * P + s0 + step]
-                            nc.scalar.copy(dst, y_banks[i, t0][:, :, s0 : s0 + step])
-                nc.sync.dma_start(out_rows[:, :, m0:m1], y[c][:, :, cols])
+        def second_pass(m0, m1):
+            quantise_z(1, m0, m1)
+            output_pass(1, m0, m1)
+            c = m0 // CHUNK
+            for i in range(m0 // P, m1 // P):
+                for index, t0, t1 in y_groups(i):
+                    step = P // 2 if t0 else P
+                    for s0 in range(0, P, step):
+                        dst = y[c][:, t0:t1, i % 2 * P + s0 : i % 2 * P + s0 + step]
+                        nc.scalar.copy(dst, y_banks[i, t0][:, :, s0 : s0 + step])
+
+        def store_y(m0, m1):
+            c, cols = in_chunk(m0, m1)
+            nc.sync.dma_start(out_rows[:, :, m0:m1], y[c][:, :, cols])
+
+        def round_sums(c):
+            for s in range(2):
+                sums = y_banks[2 * c + s, 0][:].rearrange("p t m -> p m t")
+                nc.scalar.copy(y_grouped[c][:, s * P : (s + 1) * P, :], sums)
 
         def round_y(m0, m1):
             c, s0 = divmod(m0, CHUNK)
             cols = slice(s0, s0 + m1 - m0)
             nc.vector.tensor_copy(
-                y_grouped[c][:, cols, :].rearrange("p (m u) t -> p m t u", u=2),
-                y[c][:, :, cols].rearrange("p t (m u) -> p m t u", u=2),
+                y_grouped[c][:, cols, :].rearrange("p (m u) t -> p m t u", u=PACK),
+                y[c][:, :, cols].rearrange("p t (m u) -> p m t u", u=PACK),
             )
 
-        words_from = {CHUNK: 0, 3 * CHUNK: CHUNK, M: 3 * CHUNK}
+        words_from = {3 * CHUNK: 0, M: 3 * CHUNK}
 
         def planes(m0, m1):
             c, s0 = divmod(m0, CHUNK)
@@ -493,38 +509,59 @@ def tile_list_leakage_gap_audit_kernel(
 
         x_last = {}
 
-        def fetch_last(c, u):
+        def fetch_last(u, m0, m1):
+            c, cols = in_chunk(m0, m1)
             if c not in x_last:
                 x_last[c] = tile([P, 2, CHUNK], F32, "x_last%d" % c, ("tab0", "tab2")[c % 2])
-            fetch(x_last[c][:, u, :], u, c * CHUNK, (c + 1) * CHUNK)
+            fetch(x_last[c][:, u, cols], u, m0, m1)
 
-        output_pass(0, 0)
-        fetch_last(0, 0)
-        fetch_last(0, 1)
-        fetch_last(1, 0)
-        for c in range(chunks - 1):
-            threshold(c)
-            fetch_last(c + 1, 1)
-            second_pass(c)
-            first_pass(c + 1)
-            if c + 2 < chunks:
-                fetch_last(c + 2, 0)
-        threshold(3)
-        threshold(4)
-        second_pass(3)
-        planes(*pieces[0])
-        output_pass(0, 4)
-        second_pass(4)
-        planes(*pieces[1])
-        round_y(*pieces[2])
-        round_y(*pieces[3])
-        planes(*pieces[2])
-        planes(*pieces[3])
+        chunk = [(c * CHUNK, (c + 1) * CHUNK) for c in range(chunks)]
+        half = [(i * P, (i + 1) * P) for i in range(M // P)]
+        fetch_last(0, *chunk[0])
+        fetch_last(1, *half[0])
+        fetch_last(1, *half[1])
+        first_pass(*chunk[0])
+        threshold(*half[0])
+        threshold(*half[1])
+        second_pass(*half[0])
+        fetch_last(0, *chunk[1])
+        second_pass(*half[1])
+        store_y(*chunk[0])
+        round_sums(0)
+        fetch_last(1, *chunk[1])
+        first_pass(*chunk[1])
+        fetch_last(0, *chunk[2])
+        threshold(*chunk[1])
+        fetch_last(1, *chunk[2])
+        second_pass(*chunk[1])
+        store_y(*chunk[1])
+        round_sums(1)
+        quantise_z(0, *chunk[2])
+        output_pass_by_rows(0, 2)
+        fetch_last(0, *chunk[3])
+        threshold(*chunk[2])
+        fetch_last(1, *chunk[3])
+        quantise_z(1, *chunk[2])
+        output_pass_by_rows(1, 2)
+        first_pass(*chunk[3])
+        threshold(*half[6])
+        threshold(*half[7])
+        second_pass(*half[6])
+        store_y(*half[6])
+        planes(*chunk[0])
+        output_pass(0, *half[7])
+        second_pass(*half[7])
+        store_y(*half[7])
+        planes(*chunk[1])
+        round_y(*chunk[2])
+        round_y(*half[6])
+        planes(*chunk[2])
+        planes(*half[6])
         halves = [(M - P, M - P // 2), (M - P // 2, M)]
-        for half in halves:
-            round_y(*half)
-        for half in halves:
-            planes(*half)
+        for cols in halves:
+            round_y(*cols)
+        for cols in halves:
+            planes(*cols)
         for quad in range(4):
             queue = nc.sync if quad % 2 == 0 else nc.scalar
             queue.dma_start(

@@ -107,7 +107,7 @@ def tile_list_leakage_gap_audit_kernel(
             return codes, scales
 
         def quantise_w1_plain(b, tp):
-            grouped = tile([P, CHUNK, PACK], BF16, "w_bf0%d%d" % (b, tp), "neg_mag%d" % (3 * b) if tp else None)
+            grouped = tile([P, CHUNK, PACK], BF16, "w_bf0%d%d" % (b, tp), "neg_mag%d" % b if tp else None)
             nc.scalar.copy(
                 grouped[:].rearrange("p (m u) i -> p m i u", u=2),
                 w_raw[0, b, tp][:].rearrange("p i (m u) -> p m i u", u=2),
@@ -146,7 +146,8 @@ def tile_list_leakage_gap_audit_kernel(
         quantise_w1_plain(0, 0)
         gather_tab(1, 0, S)
         quantise_w1_plain(1, 0)
-        gather_tab(2, 0, S)
+        gather_tab(2, 0, S // 2)
+        gather_tab(2, S // 2, S)
         gather_tab(3, 0, CHUNK)
         gather_tab(3, CHUNK, 2 * CHUNK)
         gather_tab(3, 2 * CHUNK, S)
@@ -221,12 +222,12 @@ def tile_list_leakage_gap_audit_kernel(
             width = (rows[1] - rows[0]) * P
             if n == 0:
                 first_gaps(h_cols[:, 0, :])
-            mag = bank(n if n < 4 else 4 if n == 4 else 5 if n == 8 else 2 * (n % 2), [P, 2, width], "mag%d" % n)
+            mag = bank((0, 1, 2, 3, 4, 3, 2, 4)[n] if n < 8 else (3, 5)[n % 2], [P, 2, width], "mag%d" % n)
             nc.scalar.activation(neg_mag[:, :, rows[0] : rows[1], :], product(g, tp, q, 0, mag, rows), COPY, scale=-1.0)
             for k in [n + 1]:
-                raw = bank(4 + k % 2 if n < 4 else 5 if n == 7 else 2 * (n % 2) + 1, [P, 2, width], "raw%d" % k)
+                raw = bank((4, 5, 7, 4, 2, 4, 3, 2)[n] if n < 8 else (4, 2)[n % 2], [P, 2, width], "raw%d" % k)
                 nc.scalar.activation(abs_raw[:, :, rows[0] : rows[1], :], product(g, tp, q, 1, raw, rows), ABS)
-                turned = bank(6 + k % 2, [P, 2, CHUNK], "turned%d" % k)
+                turned = bank((0, 1, 2, 3, 6, 5, 1, 0)[n] if n < 8 else 6 + n % 2, [P, 2, CHUNK], "turned%d" % k)
                 blocks = [(u, s) for u in range(*rows) for s in range(2)]
                 for part in (neg_mag, abs_raw):
                     for u, s in blocks:
@@ -246,10 +247,11 @@ def tile_list_leakage_gap_audit_kernel(
         def fetch(dst, u, m0, m1):
             nc.vector.tensor_copy(dst, pages[u][:].indirect(entries(list3, m0, m1)))
 
-        def fetch_negated(dst, u):
+        def fetch_negated(rows):
             for m0 in range(0, M, M // 2):
-                window = pages[u][:].indirect(entries(list3, m0, m0 + M // 2))
-                nc.vector.tensor_scalar(dst[:, m0 : m0 + M // 2], window, -1.0, 0.0, MULT, ADD)
+                for u in range(2):
+                    window = pages[u][:].indirect(entries(list3, m0, m0 + M // 2))
+                    nc.vector.tensor_scalar(rows[u][:, m0 : m0 + M // 2], window, -1.0, 0.0, MULT, ADD)
 
         x_plain = {}
 
@@ -277,18 +279,19 @@ def tile_list_leakage_gap_audit_kernel(
                 gaps(0, tp, q, h_cols)
                 for u in range(2):
                     scatter(u, h_cols[:, u, :], wg_plain[:, cols], q * CHUNK, (q + 1) * CHUNK)
-                if tp == 0 and q == 0:
-                    quantise_w1_plain(0, 1)
+                if tp == 0 and q < 2:
+                    quantise_w1_plain(q, 1)
                 if tp == 0 and q == 3:
-                    quantise_w1_plain(1, 1)
                     quantise_w1_dealt()
             if tp == 1:
                 deal_wo_words()
                 deal_wo_scales(0, "h_last1")
-            x_pair = tile([P, 2, M], F32, "x_plain%d" % tp, ("tab3", "h00")[tp])
-            x_plain[tp] = [x_pair[:, u, :] for u in range(2)]
-            for u in range(2):
-                fetch_negated(x_plain[tp][u], u)
+            if tp == 0:
+                x_plain[tp] = [tile([P, M], F32, "x_plain0%d" % u, "w_bf1%d" % u)[:] for u in range(2)]
+            else:
+                x_second = tile([P, 2, M], F32, "x_plain1", "h00")
+                x_plain[tp] = [x_second[:, u, :] for u in range(2)]
+            fetch_negated(x_plain[tp])
 
         x_turned = tile([P, M // P, PACK, P], F32, "x_turned")
         lift_turned = tile([P, M // P, PACK, P], F32, "lift_turned")
@@ -318,7 +321,7 @@ def tile_list_leakage_gap_audit_kernel(
                 forward(
                     tp,
                     c,
-                    (2, 3) if c % 2 else (6, 7),
+                    (0, 1) if c % 2 else (6, 7),
                     x_turned[:, 2 * c : 2 * c + 2, :, rows],
                     lift_turned[:, 2 * c : 2 * c + 2, :, rows],
                     lambda acc: acc.rearrange("m s (j t) -> m s t j", t=PACK),
@@ -403,8 +406,7 @@ def tile_list_leakage_gap_audit_kernel(
         put_rows(0, range(2, 4), CHUNK)
         deal_wo_scales(1, "wg0")
         x_plain[2] = [tile([P, M], F32, "x_plain2%d" % u, ("tab0", "w_raw4")[u])[:] for u in range(2)]
-        for u in range(2):
-            fetch_negated(x_plain[2][u], u)
+        fetch_negated(x_plain[2])
         put_rows(1, range(4), CHUNK)
         forward_plain(1)
         backward(range(M // P))
@@ -416,13 +418,13 @@ def tile_list_leakage_gap_audit_kernel(
         y_banks = {}
 
         def y_groups(i):
-            index = M // P - 1 - i
+            index = (7, 3, 5, 4, 6, 2, 1, 0)[i]
             return [(index, 0, 2), (M // P - 1, 2, PACK)] if index == 0 else [(index, 0, PACK)]
 
         def output_pass_by_rows(a, c):
             for pair in range(2):
                 if a == 0:
-                    y_banks[c, "rows", pair] = bank(M // P - 1 - 2 * c - pair, [P, 2, CHUNK], "y_rows%d" % pair)
+                    y_banks[c, "rows", pair] = bank((6, 2)[pair], [P, 2, CHUNK], "y_rows%d" % pair)
                 for u in range(2):
                     t = 2 * pair + u
                     nc.tensor.matmul_mx(

@@ -75,22 +75,23 @@ def tile_list_leakage_gap_audit_kernel(
 
         nc.sync.dma_start(list1[:], offs)
         load_tab(0, 0, T // 4)
+        load_tab(0, T // 4, T // 2)
+        load_tab(0, T // 2, T)
+        nc.sync.dma_start(list2[:], offs2)
+        nc.sync.dma_start(list3[:], offs3)
+        load_w1(0, 0, 0, 0, 2)
+        load_w1(0, 0, 0, 2, 4)
         for quad in range(4):
             nc.sync.dma_start(
                 tab_sc[32 * quad : 32 * quad + 16, :].bitcast(I32),
                 tab_scales[:, 4 * quad : 4 * quad + 4, :].bitcast(I32),
             )
-        load_tab(0, T // 4, T // 2)
-        load_w1(0, 0, 0)
-        load_tab(0, T // 2, T)
         load_tab(1)
         load_w1(0, 1, 0)
         load_tab(2)
         load_tab(3)
-        nc.sync.dma_start(list2[:], offs2)
         nc.sync.dma_start(wg_plain[:, 0:CHUNK], wgs[:, 0:CHUNK])
         nc.sync.dma_start(wg_plain[:, CHUNK:S], wgs[:, CHUNK:S])
-        nc.sync.dma_start(list3[:], offs3)
         for b in range(2):
             load_w1(0, b, 1)
         for b in range(2):
@@ -141,9 +142,9 @@ def tile_list_leakage_gap_audit_kernel(
         for u in range(2):
             nc.vector.memset(pages[u][:].bitcast(I32), 0)
 
-        nc.vector.tensor_copy(picked_sc[:], tab_sc[:].indirect(list1[:]))
         gather_tab(0, 0, S)
         quantise_w1_plain(0, 0)
+        nc.vector.tensor_copy(picked_sc[:], tab_sc[:].indirect(list1[:]))
         gather_tab(1, 0, S)
         quantise_w1_plain(1, 0)
         gather_tab(2, 0, S // 2)

@@ -63,7 +63,7 @@ def tile_list_leakage_gap_audit_kernel(
 
         def load_w1(g, b, e, i0=0, i1=PACK):
             if (g, b, e) not in w_raw:
-                w_raw[g, b, e] = tile([P, PACK, CHUNK], F32, "w_raw%d%d%d" % (g, b, e), "w_raw%d" % (4 if (g, b, e) == (0, 1, 1) else 2 * b + e))
+                w_raw[g, b, e] = tile([P, PACK, CHUNK], F32, "w_raw%d%d%d" % (g, b, e), {(0, 0, 0): "picked1", (0, 1, 1): "w_raw4"}.get((g, b, e), "w_raw%d" % (2 * b + e)))
             c0 = g * K_PASS + e * CHUNK
             rows = w1[b * K_PASS : (b + 1) * K_PASS, c0 : c0 + CHUNK].rearrange("(p i) c -> p i c", i=PACK)
             nc.sync.dma_start(w_raw[g, b, e][:, i0:i1, :], rows[:, i0:i1, :])
@@ -74,18 +74,19 @@ def tile_list_leakage_gap_audit_kernel(
         wo_raw = tile([P, 2, 2 * N], U8, "wo_raw")
 
         nc.sync.dma_start(list1[:], offs)
-        load_tab(0, 0, T // 4)
-        load_tab(0, T // 4, T // 2)
-        load_tab(0, T // 2, T)
         nc.sync.dma_start(list2[:], offs2)
         nc.sync.dma_start(list3[:], offs3)
-        load_w1(0, 0, 0, 0, 2)
-        load_w1(0, 0, 0, 2, 4)
+        cuts = (0, T // 8, T // 4, T // 2, 3 * T // 4, T)
+        for t0, t1 in zip(cuts, cuts[1:]):
+            load_tab(0, t0, t1)
         for quad in range(4):
-            nc.sync.dma_start(
-                tab_sc[32 * quad : 32 * quad + 16, :].bitcast(I32),
-                tab_scales[:, 4 * quad : 4 * quad + 4, :].bitcast(I32),
-            )
+            step = T if quad < 2 else T // 2
+            for t0 in range(0, T, step):
+                nc.sync.dma_start(
+                    tab_sc[32 * quad : 32 * quad + 16, t0 : t0 + step].bitcast(I32),
+                    tab_scales[:, 4 * quad : 4 * quad + 4, t0 : t0 + step].bitcast(I32),
+                )
+        load_w1(0, 0, 0)
         load_tab(1)
         load_w1(0, 1, 0)
         load_tab(2)

@@ -42,6 +42,12 @@ def tile_list_leakage_gap_audit_kernel(
         def bank(index, shape, name):
             return ps.tile(shape, F32, name=name, tag="bank%d" % index)
 
+        taken = []
+
+        def next_bank():
+            taken.append((3, 4, 7, 6, 5, 2, 1, 0)[len(taken) % 8])
+            return taken[-1]
+
         def entries(lst, j0, j1):
             return lst[:, j0 // 16 : j1 // 16]
 
@@ -224,12 +230,12 @@ def tile_list_leakage_gap_audit_kernel(
             width = (rows[1] - rows[0]) * P
             if n == 0:
                 first_gaps(h_cols[:, 0, :])
-            mag = bank((0, 1, 2, 3, 4, 3, 2, 4)[n] if n < 8 else (3, 5)[n % 2], [P, 2, width], "mag%d" % n)
+            mag = bank((0, 1, 2, 3, 4, 3, 2, 4)[n] if n < 8 else next_bank(), [P, 2, width], "mag%d" % n)
             nc.scalar.activation(neg_mag[:, :, rows[0] : rows[1], :], product(g, tp, q, 0, mag, rows), COPY, scale=-1.0)
             for k in [n + 1]:
-                raw = bank((4, 5, 7, 4, 2, 4, 3, 2)[n] if n < 8 else (4, 2)[n % 2], [P, 2, width], "raw%d" % k)
+                raw = bank((4, 5, 7, 4, 2, 4, 3, 2)[n] if n < 8 else next_bank(), [P, 2, width], "raw%d" % k)
                 nc.scalar.activation(abs_raw[:, :, rows[0] : rows[1], :], product(g, tp, q, 1, raw, rows), ABS)
-                turned = bank((0, 1, 2, 3, 6, 5, 1, 0)[n] if n < 8 else 6 + n % 2, [P, 2, CHUNK], "turned%d" % k)
+                turned = bank((0, 1, 2, 3, 6, 5, 1, 0)[n] if n < 8 else next_bank(), [P, 2, CHUNK], "turned%d" % k)
                 blocks = [(u, s) for u in range(*rows) for s in range(2)]
                 for part in (neg_mag, abs_raw):
                     for u, s in blocks:
@@ -301,14 +307,14 @@ def tile_list_leakage_gap_audit_kernel(
         def turn(dst, src, start, stop):
             nc.tensor.matmul(dst, src, ident[:], start=start, stop=stop, is_transpose=True)
 
-        def forward(tp, c, banks, x_out, lift_out, order):
+        def forward(tp, c, x_out, lift_out, order):
             blocks = [(s, u) for s in range(2) for u in range(2)]
             thr_pair = [thr_turn[tp][:, u, :] for u in range(2)]
-            for index, parts, dst, func, scale in (
-                (banks[0], (x_plain[tp],), x_out, COPY, -1.0),
-                (banks[1], (x_plain[tp], thr_pair), lift_out, RELU, 1.0),
+            for parts, dst, func, scale in (
+                ((x_plain[tp],), x_out, COPY, -1.0),
+                ((x_plain[tp], thr_pair), lift_out, RELU, 1.0),
             ):
-                acc = bank(index, [P, 2, CHUNK], "forward%d_%d_%d" % (tp, c, index))
+                acc = bank(next_bank(), [P, 2, CHUNK], "forward%d_%d_%d" % (tp, c, len(parts)))
                 for part in parts:
                     for s, u in blocks:
                         m0 = c * CHUNK + s * P
@@ -317,13 +323,12 @@ def tile_list_leakage_gap_audit_kernel(
                         turn(acc[:, s, u * P : (u + 1) * P], part[u][:, m0 : m0 + P], first, last)
                 nc.scalar.activation(dst, order(acc[:]), func, scale=scale)
 
-        def forward_plain(tp):
+        def forward_plain(tp, columns):
             rows = slice(64 * tp, 64 * tp + 64)
-            for c in range(M // CHUNK):
+            for c in columns:
                 forward(
                     tp,
                     c,
-                    (0, 1) if c % 2 else (6, 7),
                     x_turned[:, 2 * c : 2 * c + 2, :, rows],
                     lift_turned[:, 2 * c : 2 * c + 2, :, rows],
                     lambda acc: acc.rearrange("m s (j t) -> m s t j", t=PACK),
@@ -334,15 +339,13 @@ def tile_list_leakage_gap_audit_kernel(
 
         h_dealt = {}
 
-        def put_rows(tp, quarters, step):
+        def put_rows(tp, q):
             if tp not in h_dealt:
                 h_dealt[tp] = tile([P, 2, S], F32, "h1%d" % tp)
-            h = h_dealt[tp]
-            for q in quarters:
-                gaps(1, tp, q, h[:, :, q * CHUNK : (q + 1) * CHUNK])
-            for j0 in range(quarters[0] * CHUNK, (quarters[-1] + 1) * CHUNK, step):
-                for u in range(2):
-                    scatter(u, h[:, u, j0 : j0 + step], wg[tp][:, u, j0 : j0 + step], j0, j0 + step)
+            cols = slice(q * CHUNK, (q + 1) * CHUNK)
+            gaps(1, tp, q, h_dealt[tp][:, :, cols])
+            for u in range(2):
+                scatter(u, h_dealt[tp][:, u, cols], wg[tp][:, u, cols], q * CHUNK, (q + 1) * CHUNK)
 
         chunks = M // CHUNK
         z_grouped = {}
@@ -366,7 +369,7 @@ def tile_list_leakage_gap_audit_kernel(
 
         def backward(tiles):
             for i in tiles:
-                acc = bank((i + 2) % 4, [P, PACK, P], "backward%d" % i)
+                acc = bank(next_bank(), [P, PACK, P], "backward%d" % i)
                 for part in (x_turned, lift_turned):
                     for t in range(PACK):
                         first = part is x_turned and t == 0
@@ -387,10 +390,12 @@ def tile_list_leakage_gap_audit_kernel(
                 in_=z_grouped[g, c][:, cols, :].rearrange("p m t -> p (m t)"),
             )
 
-        def dealt_maximum(c):
+        def forward_dealt(c):
             tiles = slice(2 * c, 2 * c + 2)
-            forward(2, c, (2, 3) if c % 2 else (0, 1), x_turned2[:, tiles, :], lift_turned2[:, tiles, :], lambda acc: acc)
-            acc = bank(6 + c % 2, [P, 2, 2, P], "backward1%d" % c)
+            forward(2, c, x_turned2[:, tiles, :], lift_turned2[:, tiles, :], lambda acc: acc)
+
+        def backward_dealt(c):
+            acc = bank(next_bank(), [P, 2, 2, P], "backward1%d" % c)
             blocks = [(s, u) for s in range(2) for u in range(2)]
             for part in (x_turned2, lift_turned2):
                 for s, u in blocks:
@@ -403,30 +408,45 @@ def tile_list_leakage_gap_audit_kernel(
                 acc[:].rearrange("p s u m -> p s m u"),
             )
 
-        put_rows(0, range(2), CHUNK)
-        forward_plain(0)
-        put_rows(0, range(2, 4), CHUNK)
+        put_rows(0, 0)
+        forward_plain(0, range(2))
+        put_rows(0, 1)
+        forward_plain(0, range(2, 4))
+        put_rows(0, 2)
+        put_rows(0, 3)
         deal_wo_scales(1, "wg0")
         x_plain[2] = [tile([P, M], F32, "x_plain2%d" % u, ("tab0", "w_raw4")[u])[:] for u in range(2)]
         fetch_negated(x_plain[2])
-        put_rows(1, range(4), CHUNK)
-        forward_plain(1)
-        backward(range(M // P))
+        put_rows(1, 0)
+        forward_plain(1, range(2))
+        put_rows(1, 1)
+        forward_plain(1, range(2, 4))
+        backward(range(4))
+        put_rows(1, 2)
+        backward(range(4, M // P))
         x_turned2 = tile([P, M // P, CHUNK], F32, "x_turned2", "tab3")
         lift_turned2 = tile([P, M // P, CHUNK], F32, "lift_turned2", "h01")
-        for c in range(chunks):
-            dealt_maximum(c)
+        forward_dealt(0)
+        put_rows(1, 3)
+        forward_dealt(1)
+        backward_dealt(0)
+        forward_dealt(2)
+        backward_dealt(1)
+        forward_dealt(3)
+        backward_dealt(2)
+        backward_dealt(3)
+        freed = taken[-8:]
+        y_bank = [freed[7], freed[6], freed[0], freed[1], freed[5], freed[4], freed[2], freed[3]]
 
         y_banks = {}
 
         def y_groups(i):
-            index = (7, 3, 5, 4, 6, 2, 1, 0)[i]
-            return [(index, 0, 2), (M // P - 1, 2, PACK)] if index == 0 else [(index, 0, PACK)]
+            return [(y_bank[i], 0, 2), (y_bank[0], 2, PACK)] if i == M // P - 1 else [(y_bank[i], 0, PACK)]
 
         def output_pass_by_rows(a, c):
             for pair in range(2):
                 if a == 0:
-                    y_banks[c, "rows", pair] = bank((6, 2)[pair], [P, 2, CHUNK], "y_rows%d" % pair)
+                    y_banks[c, "rows", pair] = bank(y_bank[2 * c + pair], [P, 2, CHUNK], "y_rows%d" % pair)
                 for u in range(2):
                     t = 2 * pair + u
                     nc.tensor.matmul_mx(

from contextlib import ExitStack

import concourse.mybir as mybir
from concourse.masks import make_identity

KH, T, S, T2, M, H, N = 1024, 2048, 1024, 2048, 1024, 1024, 512
FLOPS = 2 * (2 * KH * H * S + H * N * M)

F32 = mybir.dt.float32
BF16 = mybir.dt.bfloat16
I32 = mybir.dt.int32
U32 = mybir.dt.uint32
U16 = mybir.dt.uint16
U8 = mybir.dt.uint8
FP8X4 = mybir.dt.float8_e4m3fn_x4
FP4X4 = mybir.dt.float4_e2m1fn_x4
COPY = mybir.ActivationFunctionType.Copy
ABS = mybir.ActivationFunctionType.Abs
RELU = mybir.ActivationFunctionType.Relu
MULT = mybir.AluOpType.mult
ADD = mybir.AluOpType.add
MAX = mybir.AluOpType.max
SUB = mybir.AluOpType.subtract

P = 128
PACK = 4
K_PASS = P * PACK
CHUNK = 256


def tile_list_leakage_gap_audit_kernel(
    tc, tab_words, tab_scales, offs, offs2, offs3, w1, wgs, thr, wo_words, wo_scales, out_0, out_1, out_2
):
    nc = tc.nc
    with ExitStack() as ctx:
        sb = ctx.enter_context(tc.tile_pool(name="sb", bufs=1))
        ps = ctx.enter_context(tc.psum_pool(name="ps", bufs=1))

        def tile(shape, dtype, name, tag=None):
            return sb.tile(shape, dtype, name=name, tag=tag or name, align_bytes=64)

        def bank(index, shape, name):
            return ps.tile(shape, F32, name=name, tag="bank%d" % index)

        taken = []

        def next_bank():
            taken.append((3, 4, 7, 6, 5, 2, 1, 0)[len(taken) % 8])
            return taken[-1]

        def entries(lst, j0, j1):
            return lst[:, j0 // 16 : j1 // 16]

        list1 = tile([P, S // 16], U16, "list1")
        list2 = tile([P, S // 16], U16, "list2")
        list3 = tile([P, M // 16], U16, "list3")
        ident = tile([P, P], F32, "ident")
        tab_sc = tile([P, T], U8, "tab_sc")
        wo_sc_raw = tile([P, 2, N], U8, "wo_sc_raw")
        nc.gpsimd.memset(tab_sc[:].bitcast(I32), 0)
        nc.gpsimd.memset(wo_sc_raw[:].bitcast(I32), 0)
        make_identity(nc, ident[:])

        tab = [tile([P, T], I32, "tab%d" % a) for a in range(4)]
        w_raw = {}

        def load_tab(a, t0=0, t1=T):
            nc.sync.dma_start(tab[a][:, t0:t1], tab_words[a].rearrange("p t i -> p (t i)").bitcast(I32)[:, t0:t1])

        def load_w1(g, b, e, i0=0, i1=PACK):
            if (g, b, e) not in w_raw:
                w_raw[g, b, e] = tile([P, PACK, CHUNK], F32, "w_raw%d%d%d" % (g, b, e), {(0, 0, 0): "picked1", (0, 1, 1): "w_raw4"}.get((g, b, e), "w_raw%d" % (2 * b + e)))
            c0 = g * K_PASS + e * CHUNK
            rows = w1[b * K_PASS : (b + 1) * K_PASS, c0 : c0 + CHUNK].rearrange("(p i) c -> p i c", i=PACK)
            nc.sync.dma_start(w_raw[g, b, e][:, i0:i1, :], rows[:, i0:i1, :])

        wg_plain = tile([P, S], F32, "wg_plain")
        wg = [tile([P, 2, S], F32, "wg%d" % tp) for tp in range(2)]
        wgs_rows = wgs.rearrange("(q t) j -> q t j", t=PACK)
        wo_raw = tile([P, 2, 2 * N], U8, "wo_raw")

        nc.sync.dma_start(list1[:], offs)
        nc.sync.dma_start(list2[:], offs2)
        nc.sync.dma_start(list3[:], offs3)
        cuts = (0, T // 8, T // 4, T // 2, 3 * T // 4, T)
        for t0, t1 in zip(cuts, cuts[1:]):
            load_tab(0, t0, t1)
        for quad in range(4):
            step = T if quad < 2 else T // 2
            for t0 in range(0, T, step):
                nc.sync.dma_start(
                    tab_sc[32 * quad : 32 * quad + 16, t0 : t0 + step].bitcast(I32),
                    tab_scales[:, 4 * quad : 4 * quad + 4, t0 : t0 + step].bitcast(I32),
                )
        load_w1(0, 0, 0)
        load_tab(1)
        load_w1(0, 1, 0)
        load_tab(2)
        load_tab(3)
        nc.sync.dma_start(wg_plain[:, 0:CHUNK], wgs[:, 0:CHUNK])
        nc.sync.dma_start(wg_plain[:, CHUNK:S], wgs[:, CHUNK:S])
        for b in range(2):
            load_w1(0, b, 1)
        for b in range(2):
            for e in range(2):
                load_w1(1, b, e)

        w_codes = {}
        w_scales = {}

        def quantise_words(key, grouped, width, tag=None):
            codes = tile([P, width], U32, "w_codes%d%d%d" % key, tag)
            scales = tile([P, width], U8, "w_scales%d%d%d" % key)
            nc.vector.quantize_mx(out=codes[:].bitcast(FP8X4), scales=scales[:], in_=grouped)
            return codes, scales

        def quantise_w1_plain(b, tp):
            grouped = tile([P, CHUNK, PACK], BF16, "w_bf0%d%d" % (b, tp), "neg_mag%d" % b if tp else None)
            nc.scalar.copy(
                grouped[:].rearrange("p (m u) i -> p m i u", u=2),
                w_raw[0, b, tp][:].rearrange("p i (m u) -> p m i u", u=2),
            )
            codes, scales = quantise_words((0, b, tp), grouped[:].rearrange("p c i -> p (c i)"), CHUNK)
            w_codes[0, b, tp] = codes[:]
            w_scales[0, b, tp] = scales[:]

        def quantise_w1_dealt():
            grouped = [tile([P, 2, K_PASS // 2, PACK], BF16, "w_bf1%d" % b) for b in range(2)]
            for b in range(2):
                for e in range(2):
                    nc.scalar.copy(
                        grouped[b][:, :, e * P : (e + 1) * P, :].rearrange("p h (m u) i -> p h m i u", u=2),
                        w_raw[1, b, e][:].rearrange("p i (m h u) -> p h m i u", h=2, u=2),
                    )
            for b in range(2):
                flat = grouped[b][:].rearrange("p h c i -> p (h c i)")
                codes, scales = quantise_words((1, b, 0), flat, K_PASS, None if b else "w_raw3")
                for tp in range(2):
                    w_codes[1, b, tp] = codes[:, tp * CHUNK : (tp + 1) * CHUNK]
                    w_scales[1, b, tp] = scales[:, tp * CHUNK : (tp + 1) * CHUNK]

        picked_sc = tile([P, S], U8, "picked_sc")
        picked = [tile([P, S], U32, "picked%d" % a) for a in range(4)]

        def gather_tab(a, j0, j1):
            nc.vector.tensor_copy(picked[a][:, j0:j1], tab[a][:].bitcast(U32).indirect(entries(list1, j0, j1)))

        pages = [tile([P, T2], F32, "page%d" % u) for u in range(2)]
        for u in range(2):
            nc.vector.memset(pages[u][:].bitcast(I32), 0)

        gather_tab(0, 0, S)
        quantise_w1_plain(0, 0)
        nc.vector.tensor_copy(picked_sc[:], tab_sc[:].indirect(list1[:]))
        gather_tab(1, 0, S)
        quantise_w1_plain(1, 0)
        gather_tab(2, 0, S // 2)
        gather_tab(2, S // 2, S)
        gather_tab(3, 0, CHUNK)
        gather_tab(3, CHUNK, 2 * CHUNK)
        gather_tab(3, 2 * CHUNK, S)

        def first_gaps(h_row):
            sums = []
            for half in range(2):
                acc = bank(6 + half, [P, CHUNK], "first%d" % half)
                for b in range(2):
                    k = 2 * half + b
                    nc.tensor.matmul_mx(
                        out=acc[:],
                        lhsT=w_codes[0, b, 0][:, 0:P].bitcast(FP8X4),
                        lhsT_scale=w_scales[0, b, 0][:, 0:P],
                        rhs=picked[k][:, 0:CHUNK].bitcast(FP8X4),
                        rhs_scale=picked_sc[4 * k :, 0:CHUNK],
                        start=(b == 0),
                        stop=(b == 1),
                    )
                sums.append(acc)
            abs_first = tile([P, CHUNK], F32, "abs_first")
            nc.scalar.activation(abs_first[:], sums[1][:], ABS)
            nc.vector.tensor_tensor(h_row, sums[0][:], abs_first[:], SUB)

        thr_turn = [tile([P, 2, M], F32, "thr_turn%d" % tp, "tab%d" % tp) for tp in range(3)]
        thr_rows = thr[K_PASS:, :].rearrange("(p t) m -> p t m", t=PACK)
        thr_hi = [tile([P, 2, CHUNK], F32, "thr_hi%d" % c) for c in range(M // CHUNK)]

        def load_thr_plain(tp):
            rows = thr[tp * CHUNK : (tp + 1) * CHUNK, :].rearrange("(u q) m -> q u m", q=P)
            nc.sync.dma_start(thr_turn[tp][:], rows)

        load_thr_plain(0)
        for tp in range(2):
            for quad in (0, 2, 1, 3):
                nc.sync.dma_start(wg[tp][32 * quad : 32 * quad + 32, :, :], wgs_rows[:, 2 * tp : 2 * tp + 2, :])
        load_thr_plain(1)
        nc.sync.dma_start(thr_turn[2][:], thr_rows[:, 0:2, :])
        for c in range(M // CHUNK):
            nc.sync.dma_start(thr_hi[c][:], thr_rows[:, 2:4, c * CHUNK : (c + 1) * CHUNK])
        nc.sync.dma_start(wo_raw[:].bitcast(I32), wo_words.rearrange("a p c -> p a c").bitcast(I32))
        for quad in range(4):
            nc.sync.dma_start(
                wo_sc_raw[32 * quad : 32 * quad + 4, :, :].bitcast(I32),
                wo_scales[:, 4 * quad : 4 * quad + 4, :].rearrange("a q c -> q a c").bitcast(I32),
            )

        def product(g, tp, q, half, acc, rows=(0, 2)):
            w_cols = slice(rows[0] * P, rows[1] * P)
            for b in range(2):
                k = 2 * half + b
                for s in range(2):
                    cols = slice(q * CHUNK + s * P, q * CHUNK + (s + 1) * P)
                    nc.tensor.matmul_mx(
                        out=acc[:, s, :],
                        lhsT=picked[k][:, cols].bitcast(FP8X4),
                        lhsT_scale=picked_sc[4 * k :, cols],
                        rhs=w_codes[g, b, tp][:, w_cols].bitcast(FP8X4),
                        rhs_scale=w_scales[g, b, tp][:, w_cols],
                        start=(b == 0 and s == 0),
                        stop=(b == 1 and s == 1),
                    )
            if g == 0:
                return acc[:].rearrange("p s (u m) -> p s u m", m=P)
            return acc[:].rearrange("p s (m u) -> p s u m", u=2)

        def gaps(g, tp, q, h_cols):
            n = 8 * g + 4 * tp + q
            neg_mag = tile([P, 2, 2, P], F32, "neg_mag%d" % n, "neg_mag%d" % (n % 4))
            abs_raw = tile([P, 2, 2, P], F32, "abs_raw%d" % n, "abs_raw%d" % (n % 3))
            rows = (1, 2) if n == 0 else (0, 2)
            width = (rows[1] - rows[0]) * P
            if n == 0:
                first_gaps(h_cols[:, 0, :])
            mag = bank((0, 1, 2, 3, 4, 3, 2, 4)[n] if n < 8 else next_bank(), [P, 2, width], "mag%d" % n)
            nc.scalar.activation(neg_mag[:, :, rows[0] : rows[1], :], product(g, tp, q, 0, mag, rows), COPY, scale=-1.0)
            for k in [n + 1]:
                raw = bank((4, 5, 7, 4, 2, 4, 3, 2)[n] if n < 8 else next_bank(), [P, 2, width], "raw%d" % k)
                nc.scalar.activation(abs_raw[:, :, rows[0] : rows[1], :], product(g, tp, q, 1, raw, rows), ABS)
                turned = bank((0, 1, 2, 3, 6, 5, 1, 0)[n] if n < 8 else next_bank(), [P, 2, CHUNK], "turned%d" % k)
                blocks = [(u, s) for u in range(*rows) for s in range(2)]
                for part in (neg_mag, abs_raw):
                    for u, s in blocks:
                        nc.tensor.matmul(
                            turned[:, u, s * P : (s + 1) * P],
                            part[:, s, u, :],
                            ident[:],
                            start=(part is neg_mag and (u, s) == blocks[0]),
                            stop=(part is abs_raw and (u, s) == blocks[-1]),
                            is_transpose=True,
                        )
                nc.scalar.activation(h_cols[:, rows[0] : rows[1], :], turned[:, rows[0] : rows[1], :], COPY, scale=-1.0)

        def scatter(u, h_row, weights, j0, j1):
            nc.vector.tensor_tensor(pages[u][:].indirect(entries(list2, j0, j1)), h_row, weights, MULT)

        def fetch(dst, u, m0, m1):
            nc.vector.tensor_copy(dst, pages[u][:].indirect(entries(list3, m0, m1)))

        def fetch_negated(rows):
            for m0 in range(0, M, M // 2):
                for u in range(2):
                    window = pages[u][:].indirect(entries(list3, m0, m0 + M // 2))
                    nc.vector.tensor_scalar(rows[u][:, m0 : m0 + M // 2], window, -1.0, 0.0, MULT, ADD)

        x_plain = {}

        wo_dealt = {}

        def deal_wo_words():
            wo_dealt["codes"] = tile([P, 2, 2 * N], U8, "wo_codes", "w_bf000")
            nc.scalar.copy(
                wo_dealt["codes"][:].bitcast(U16).rearrange("p a (t c) -> p a t c", t=PACK),
                wo_raw[:].bitcast(U16).rearrange("p a (c t) -> p a t c", t=PACK),
            )

        def deal_wo_scales(a, tag):
            wo_dealt["scales", a] = tile([P, N], U8, "wo_sc%d" % a, tag)
            nc.gpsimd.tensor_copy(
                wo_dealt["scales", a][:].rearrange("p (t c) -> p t c", t=PACK),
                wo_sc_raw[:, a, :].rearrange("p (c t) -> p t c", t=PACK),
            )

        def plain_pair(tp):
            h = tile([P, 2, S], F32, "h0%d" % tp)
            for q in range(4):
                cols = slice(q * CHUNK, (q + 1) * CHUNK)
                h_cols = tile([P, 2, CHUNK], F32, "h_last%d" % tp)[:] if q == 3 else h[:, :, cols]
                gaps(0, tp, q, h_cols)
                for u in range(2):
                    scatter(u, h_cols[:, u, :], wg_plain[:, cols], q * CHUNK, (q + 1) * CHUNK)
                if tp == 0 and q < 2:
                    quantise_w1_plain(q, 1)
                if tp == 0 and q == 3:
                    quantise_w1_dealt()
            if tp == 1:
                deal_wo_words()
                deal_wo_scales(0, "h_last1")
            if tp == 0:
                x_plain[tp] = [tile([P, M], F32, "x_plain0%d" % u, "w_bf1%d" % u)[:] for u in range(2)]
            else:
                x_second = tile([P, 2, M], F32, "x_plain1", "h00")
                x_plain[tp] = [x_second[:, u, :] for u in range(2)]
            fetch_negated(x_plain[tp])

        x_turned = tile([P, M // P, PACK, P], F32, "x_turned")
        lift_turned = tile([P, M // P, PACK, P], F32, "lift_turned")

        def turn(dst, src, start, stop):
            nc.tensor.matmul(dst, src, ident[:], start=start, stop=stop, is_transpose=True)

        def forward(tp, c, x_out, lift_out, order):
            blocks = [(s, u) for s in range(2) for u in range(2)]
            thr_pair = [thr_turn[tp][:, u, :] for u in range(2)]
            for parts, dst, func, scale in (
                ((x_plain[tp],), x_out, COPY, -1.0),
                ((x_plain[tp], thr_pair), lift_out, RELU, 1.0),
            ):
                acc = bank(next_bank(), [P, 2, CHUNK], "forward%d_%d_%d" % (tp, c, len(parts)))
                for part in parts:
                    for s, u in blocks:
                        m0 = c * CHUNK + s * P
                        first = part is parts[0] and (s, u) == blocks[0]
                        last = part is parts[-1] and (s, u) == blocks[-1]
                        turn(acc[:, s, u * P : (u + 1) * P], part[u][:, m0 : m0 + P], first, last)
                nc.scalar.activation(dst, order(acc[:]), func, scale=scale)

        def forward_plain(tp, columns):
            rows = slice(64 * tp, 64 * tp + 64)
            for c in columns:
                forward(
                    tp,
                    c,
                    x_turned[:, 2 * c : 2 * c + 2, :, rows],
                    lift_turned[:, 2 * c : 2 * c + 2, :, rows],
                    lambda acc: acc.rearrange("m s (j t) -> m s t j", t=PACK),
                )

        plain_pair(0)
        plain_pair(1)

        h_dealt = {}

        def put_rows(tp, q):
            if tp not in h_dealt:
                h_dealt[tp] = tile([P, 2, S], F32, "h1%d" % tp)
            cols = slice(q * CHUNK, (q + 1) * CHUNK)
            gaps(1, tp, q, h_dealt[tp][:, :, cols])
            for u in range(2):
                scatter(u, h_dealt[tp][:, u, cols], wg[tp][:, u, cols], q * CHUNK, (q + 1) * CHUNK)

        chunks = M // CHUNK
        z_grouped = {}
        z_codes = {}
        z_scales = [tile([P, M], U8, "z_scales%d" % g) for g in range(2)]

        def in_chunk(m0, m1):
            c, s0 = divmod(m0, CHUNK)
            return c, slice(s0, s0 + m1 - m0)

        def threshold(m0, m1):
            c, cols = in_chunk(m0, m1)
            nc.vector.tensor_tensor(
                z_grouped[1, c][:, cols, 2:4].rearrange("p (c u) t -> p c t u", u=2),
                x_last[c][:, :, cols].rearrange("p t (c u) -> p c t u", u=2),
                thr_hi[c][:, :, cols].rearrange("p t (c u) -> p c t u", u=2),
                MAX,
            )

        z_tags = ("w_bf010", "h_last0", "wg_plain", "tab1")

        def backward(tiles):
            for i in tiles:
                acc = bank(next_bank(), [P, PACK, P], "backward%d" % i)
                for part in (x_turned, lift_turned):
                    for t in range(PACK):
                        first = part is x_turned and t == 0
                        turn(acc[:, t, :], part[:, i, t, :], first, part is lift_turned and t == PACK - 1)
                c, s = divmod(i, 2)
                if s == 0:
                    z_grouped[0, c] = tile([P, CHUNK, PACK], BF16, "z_grouped0%d" % c, z_tags[c])[:]
                nc.scalar.copy(z_grouped[0, c][:, s * P : (s + 1) * P, :], acc[:].rearrange("p t m -> p m t"))

        def quantise_z(g, m0, m1):
            c, s0 = divmod(m0, CHUNK)
            cols = slice(s0, s0 + m1 - m0)
            if (g, c) not in z_codes:
                z_codes[g, c] = tile([P, CHUNK], U32, "z_codes%d_%d" % (g, c), None if g else "thr_hi%d" % (c - 1) if c else "w_raw4")
            nc.vector.quantize_mx(
                out=z_codes[g, c][:, cols].bitcast(FP8X4),
                scales=z_scales[g][:, m0:m1],
                in_=z_grouped[g, c][:, cols, :].rearrange("p m t -> p (m t)"),
            )

        def forward_dealt(c):
            tiles = slice(2 * c, 2 * c + 2)
            forward(2, c, x_turned2[:, tiles, :], lift_turned2[:, tiles, :], lambda acc: acc)

        def backward_dealt(c):
            acc = bank(next_bank(), [P, 2, 2, P], "backward1%d" % c)
            blocks = [(s, u) for s in range(2) for u in range(2)]
            for part in (x_turned2, lift_turned2):
                for s, u in blocks:
                    first = part is x_turned2 and (s, u) == blocks[0]
                    last = part is lift_turned2 and (s, u) == blocks[-1]
                    turn(acc[:, s, u, :], part[:, 2 * c + s, u * P : (u + 1) * P], first, last)
            z_grouped[1, c] = tile([P, CHUNK, PACK], BF16, "z_grouped1%d" % c, "picked%d" % c)[:]
            nc.scalar.copy(
                z_grouped[1, c][:, :, 0:2].rearrange("p (s m) u -> p s m u", s=2),
                acc[:].rearrange("p s u m -> p s m u"),
            )

        put_rows(0, 0)
        forward_plain(0, range(2))
        put_rows(0, 1)
        forward_plain(0, range(2, 4))
        put_rows(0, 2)
        put_rows(0, 3)
        deal_wo_scales(1, "wg0")
        x_plain[2] = [tile([P, M], F32, "x_plain2%d" % u, ("tab0", "w_raw4")[u])[:] for u in range(2)]
        fetch_negated(x_plain[2])
        put_rows(1, 0)
        forward_plain(1, range(2))
        put_rows(1, 1)
        forward_plain(1, range(2, 4))
        backward(range(4))
        put_rows(1, 2)
        backward(range(4, M // P))
        x_turned2 = tile([P, M // P, CHUNK], F32, "x_turned2", "tab3")
        lift_turned2 = tile([P, M // P, CHUNK], F32, "lift_turned2", "h01")
        forward_dealt(0)
        put_rows(1, 3)
        forward_dealt(1)
        backward_dealt(0)
        forward_dealt(2)
        backward_dealt(1)
        forward_dealt(3)
        backward_dealt(2)
        backward_dealt(3)
        freed = taken[-8:]
        y_bank = [freed[7], freed[6], freed[0], freed[1], freed[5], freed[4], freed[2], freed[3]]

        y_banks = {}

        def y_groups(i):
            return [(y_bank[i], 0, 2), (y_bank[0], 2, PACK)] if i == M // P - 1 else [(y_bank[i], 0, PACK)]

        def output_pass_by_rows(a, c):
            for pair in range(2):
                if a == 0:
                    y_banks[c, "rows", pair] = bank(y_bank[2 * c + pair], [P, 2, CHUNK], "y_rows%d" % pair)
                for u in range(2):
                    t = 2 * pair + u
                    nc.tensor.matmul_mx(
                        out=y_banks[c, "rows", pair][:, u, :],
                        lhsT=wo_dealt["codes"][:, a, 2 * P * t : 2 * P * (t + 1)].bitcast(FP4X4),
                        lhsT_scale=wo_dealt["scales", a][:, P * t : P * (t + 1)],
                        rhs=z_codes[a, c][:].bitcast(FP8X4),
                        rhs_scale=z_scales[a][:, c * CHUNK : (c + 1) * CHUNK],
                        start=(a == 0 and u == 0),
                        stop=(a == 1 and u == 1),
                    )
                if a == 1:
                    rows = slice(2 * pair, 2 * pair + 2)
                    nc.scalar.copy(y[c][:, rows, :], y_banks[c, "rows", pair][:])
                    nc.sync.dma_start(out_rows[:, rows, c * CHUNK : (c + 1) * CHUNK], y[c][:, rows, :])

        def output_pass(a, m0, m1):
            for i in range(m0 // P, m1 // P):
                for index, t0, t1 in y_groups(i):
                    if a == 0:
                        y_banks[i, t0] = bank(index, [P, t1 - t0, P], "y%d_%d" % (i, t0))
                    for t in range(t0, t1):
                        nc.tensor.matmul_mx(
                            out=y_banks[i, t0][:, t - t0, :],
                            lhsT=wo_dealt["codes"][:, a, 2 * P * t : 2 * P * (t + 1)].bitcast(FP4X4),
                            lhsT_scale=wo_dealt["scales", a][:, P * t : P * (t + 1)],
                            rhs=z_codes[a, i // 2][:, i % 2 * P : (i % 2 + 1) * P].bitcast(FP8X4),
                            rhs_scale=z_scales[a][:, i * P : (i + 1) * P],
                            start=(a == 0 and t == t0),
                            stop=(a == 1 and t == t1 - 1),
                        )

        y = [tile([P, PACK, CHUNK], F32, "y%d" % c, "w_raw%d" % c) for c in range(chunks)]
        y_grouped = [tile([P, CHUNK, PACK], BF16, "y_grouped%d" % c, "neg_mag%d" % c) for c in range(chunks)]
        y_codes = tile([P, M], U32, "y_codes")
        y_scales = tile([P, M], U8, "y_scales")
        out_rows = out_0.rearrange("(p t) m -> p t m", t=PACK)
        out_words = out_1[0].rearrange("p m t -> p (m t)").bitcast(I32)

        def first_pass(m0, m1):
            quantise_z(0, m0, m1)
            output_pass(0, m0, min(m1, M - P))

        def second_pass(m0, m1):
            quantise_z(1, m0, m1)
            output_pass(1, m0, m1)
            c = m0 // CHUNK
            for i in range(m0 // P, m1 // P):
                for index, t0, t1 in y_groups(i):
                    step = P // 2 if t0 else P
                    for s0 in range(0, P, step):
                        dst = y[c][:, t0:t1, i % 2 * P + s0 : i % 2 * P + s0 + step]
                        nc.scalar.copy(dst, y_banks[i, t0][:, :, s0 : s0 + step])

        def store_y(m0, m1):
            c, cols = in_chunk(m0, m1)
            nc.sync.dma_start(out_rows[:, :, m0:m1], y[c][:, :, cols])

        def round_sums(c):
            for s in range(2):
                sums = y_banks[2 * c + s, 0][:].rearrange("p t m -> p m t")
                nc.scalar.copy(y_grouped[c][:, s * P : (s + 1) * P, :], sums)

        def round_y(m0, m1):
            c, s0 = divmod(m0, CHUNK)
            cols = slice(s0, s0 + m1 - m0)
            nc.vector.tensor_copy(
                y_grouped[c][:, cols, :].rearrange("p (m u) t -> p m t u", u=PACK),
                y[c][:, :, cols].rearrange("p t (m u) -> p m t u", u=PACK),
            )

        words_from = {3 * CHUNK: 0, M: 3 * CHUNK}

        def planes(m0, m1):
            c, s0 = divmod(m0, CHUNK)
            cols = slice(s0, s0 + m1 - m0)
            nc.vector.quantize_mx(
                out=y_codes[:, m0:m1].bitcast(FP8X4),
                scales=y_scales[:, m0:m1],
                in_=y_grouped[c][:, cols, :].rearrange("p m t -> p (m t)"),
            )
            if m1 in words_from:
                nc.sync.dma_start(out_words[:, words_from[m1] : m1], y_codes[:, words_from[m1] : m1].bitcast(I32))

        x_last = {}

        def fetch_last(u, m0, m1):
            c, cols = in_chunk(m0, m1)
            if c not in x_last:
                x_last[c] = tile([P, 2, CHUNK], F32, "x_last%d" % c, ("tab0", "tab2")[c % 2])
            fetch(x_last[c][:, u, cols], u, m0, m1)

        chunk = [(c * CHUNK, (c + 1) * CHUNK) for c in range(chunks)]
        half = [(i * P, (i + 1) * P) for i in range(M // P)]
        fetch_last(0, *chunk[0])
        fetch_last(1, *half[0])
        fetch_last(1, *half[1])
        first_pass(*chunk[0])
        threshold(*half[0])
        threshold(*half[1])
        second_pass(*half[0])
        fetch_last(0, *chunk[1])
        second_pass(*half[1])
        store_y(*chunk[0])
        round_sums(0)
        fetch_last(1, *chunk[1])
        first_pass(*chunk[1])
        fetch_last(0, *chunk[2])
        threshold(*chunk[1])
        fetch_last(1, *chunk[2])
        second_pass(*chunk[1])
        store_y(*chunk[1])
        round_sums(1)
        quantise_z(0, *chunk[2])
        output_pass_by_rows(0, 2)
        fetch_last(0, *chunk[3])
        threshold(*chunk[2])
        fetch_last(1, *chunk[3])
        quantise_z(1, *chunk[2])
        output_pass_by_rows(1, 2)
        first_pass(*chunk[3])
        threshold(*half[6])
        threshold(*half[7])
        second_pass(*half[6])
        store_y(*half[6])
        planes(*chunk[0])
        output_pass(0, *half[7])
        second_pass(*half[7])
        store_y(*half[7])
        planes(*chunk[1])
        round_y(*chunk[2])
        round_y(*half[6])
        planes(*chunk[2])
        planes(*half[6])
        halves = [(M - P, M - P // 2), (M - P // 2, M)]
        for cols in halves:
            round_y(*cols)
        for cols in halves:
            planes(*cols)
        for quad in range(4):
            queue = nc.sync if quad % 2 == 0 else nc.scalar
            queue.dma_start(
                out_2[0][4 * quad : 4 * quad + 4, :].bitcast(I32),
                y_scales[32 * quad : 32 * quad + 4, :].bitcast(I32),
            )
